import numpy as np
import ml_dtypes


def mxq(x, axis, fmt="e4m3"):
    dtype, down = {"e4m3": (ml_dtypes.float8_e4m3fn, 7), "e5m2": (ml_dtypes.float8_e5m2, 14)}[fmt]
    v = np.moveaxis(np.asarray(x, np.float32).astype(ml_dtypes.bfloat16).astype(np.float64), axis, -1)
    blocks = v.reshape(v.shape[:-1] + (-1, 32))
    amax = np.abs(blocks).max(-1, keepdims=True)
    byte = np.maximum(np.where(amax > 0, np.frexp(amax)[1] - 1 + 127, 0) - down, 1)
    scale = np.exp2(byte - 127.0)
    codes = (blocks / scale).astype(np.float32).astype(dtype).astype(np.float64)
    return np.moveaxis((codes * scale).reshape(v.shape), -1, axis)


WIDE = False


def mx_kscale(k):
    if not WIDE:
        return np.ones(k)
    levels = np.array([18, -18])
    if k % 512:
        return np.exp2(np.random.permutation(np.resize(levels, k // 32))).repeat(32)
    a = np.empty((k // 512, 16))
    for p in range(k // 512):
        a[p, :8] = np.random.permutation(np.resize(levels, 8))
        for g in range(8):
            far = levels[np.abs(levels - a[p, g]) >= 10]
            a[p, g + 8] = far[np.random.randint(len(far))]
    return np.exp2(a.ravel()).repeat(32)


def f64(x):
    return np.asarray(x).astype(np.float64)


def striped(idx):
    return np.tile(np.asarray(idx).reshape(-1, 16).T, (8, 1)).astype(np.uint16)


def unstriped(offs):
    return offs[:16].T.reshape(-1).astype(np.int64)


N, T, D, V = 512, 1024, 512, 512


def setup_inputs():
    n = np.random.standard_normal
    idx = np.random.permutation(T)[:N]
    s = mx_kscale(D)[:, None]
    z = mx_kscale(V)[:, None]
    w = n((D, V)) / np.sqrt(D)
    return {
        "xT": (n((D, T)) / s).astype(np.float32),
        "wd": (w * s).astype(np.float32),
        "wv": (w.T / z).astype(np.float32),
        "y": n((V, N)).astype(np.float32),
        "cw": (np.random.uniform(0.5, 1.5, (V, 1)) / np.sqrt(V) * z).astype(np.float32),
        "rw": np.tile(np.random.uniform(0.5, 1.5, N), (128, 1)).astype(np.float32),
        "offs": striped(idx),
    }


def reference(xT, wd, wv, y, cw, rw, offs):
    idx = unstriped(offs)
    a = mxq(f64(wd), 0, "e4m3").T @ mxq(f64(xT)[:, idx], 0, "e4m3")
    q = a - f64(y)
    g = f64(cw) * f64(rw)[:1] * q * np.exp(-0.5 * q * q)
    dx = mxq(f64(wv), 0, "e4m3").T @ mxq(g, 0, "e5m2")
    gx = np.zeros((D, T))
    gx[:, idx] = dx
    return gx

@@ -1,0 +1,196 @@
+from contextlib import ExitStack
+
+import concourse.mybir as mybir
+
+N, T, D, V = 512, 1024, 512, 512
+FLOPS = 2 * D * V * N + 2 * V * D * N
+
+F32 = mybir.dt.float32
+BF16 = mybir.dt.bfloat16
+U32 = mybir.dt.uint32
+U16 = mybir.dt.uint16
+U8 = mybir.dt.uint8
+E4M3 = mybir.dt.float8_e4m3fn_x4
+E5M2 = mybir.dt.float8_e5m2_x4
+ACT = mybir.ActivationFunctionType
+ALU = mybir.AluOpType
+
+P = 128
+PACK = 4
+HALF = 256
+RUN = 4
+
+
+def tile_attend_gml_wel_kernel(tc, xT, wd, wv, y, cw, rw, offs, out):
+    nc = tc.nc
+    with ExitStack() as ctx:
+        sb = ctx.enter_context(tc.tile_pool(name="sb", bufs=1))
+        ps = ctx.enter_context(tc.psum_pool(name="ps", bufs=8))
+
+        def tile(name, shape, dtype):
+            return sb.tile(shape, dtype, name=name, align_bytes=64)
+
+        def half(h):
+            return slice(h * HALF, (h + 1) * HALF)
+
+        def bank(name):
+            return ps.tile([P, 2 * HALF], F32, name=name, tag="bank")
+
+        offsets = sb.tile([P, N // 16], U16, name="offsets")
+        nc.sync.dma_start(offsets[:], offs)
+        x_planes = xT.rearrange("(p t) n -> p t n", t=PACK)
+        x_raw = [tile("x_raw%d" % t, [P, T], F32) for t in range(PACK)]
+        for t in range(PACK):
+            nc.sync.dma_start(x_raw[t][:], x_planes[:, t, :])
+        wd_planes = wd.rearrange("(p j) v -> p j v", j=PACK)
+        wv_planes = wv.rearrange("(p j) d -> p j d", j=PACK)
+        y_planes = y.rearrange("(p t) n -> p t n", t=PACK)
+        wd_raw = [tile("wd_raw%d" % h, [P, PACK, HALF], F32) for h in range(2)]
+        wv_raw = [tile("wv_raw%d" % h, [P, PACK, HALF], F32) for h in range(2)]
+        y_sb = [tile("y_sb%d" % h, [P, PACK, HALF], F32) for h in range(2)]
+        cw_sb = tile("cw_sb", [P, PACK], F32)
+        rw_sb = tile("rw_sb", [P, N], F32)
+        for h in range(2):
+            nc.sync.dma_start(wd_raw[h][:], wd_planes[:, :, half(h)])
+        nc.sync.dma_start(y_sb[0][:], y_planes[:, :, half(0)])
+        nc.sync.dma_start(cw_sb[:], cw.rearrange("(p t) o -> p (t o)", t=PACK))
+        nc.sync.dma_start(rw_sb[:], rw)
+        nc.sync.dma_start(wv_raw[0][:], wv_planes[:, :, half(0)])
+        nc.sync.dma_start(y_sb[1][:], y_planes[:, :, half(1)])
+        nc.sync.dma_start(wv_raw[1][:], wv_planes[:, :, half(1)])
+
+        warm_in = tile("warm_in", [P, 8], F32)
+        warm_out = tile("warm_out", [P, 8], F32)
+        nc.gpsimd.memset(warm_in[:], 0.0)
+        nc.scalar.activation(warm_out[:], warm_in[:], ACT.Exp)
+
+        windows = [tile("window%d" % b, [P, T], F32) for b in range(D // P)]
+        for b in range(D // P):
+            nc.vector.memset(windows[b][:], 0.0)
+        g_codes = tile("g_codes", [P, 3 * HALF], U32)
+        g_scales = tile("g_scales", [P, 3 * HALF], U8)
+        nc.vector.memset(g_codes[:, 0:HALF], 0)
+        nc.vector.memset(g_scales[:, 0:HALF].bitcast(U32), 0)
+
+        x_got = tile("x_got", [P, PACK, N], F32)
+        for t in range(PACK):
+            nc.vector.tensor_copy(x_got[:, t, :], x_raw[t][:].indirect(offsets[:]))
+
+        x_bf = [tile("x_bf%d" % h, [P, HALF * PACK], BF16) for h in range(2)]
+        x_codes = tile("x_codes", [P, N], U32)
+        x_scales = tile("x_scales", [P, N], U8)
+        wd_bf = tile("wd_bf", [P, PACK, P, PACK], BF16)
+        wd_codes = tile("wd_codes", [P, V], U32)
+        wd_scales = tile("wd_scales", [P, V], U8)
+        wv_bf = [tile("wv_bf%d" % h, [P, HALF * PACK], BF16) for h in range(2)]
+        wv_codes = tile("wv_codes", [P, D], U32)
+        wv_scales = tile("wv_scales", [P, D], U8)
+
+        def as_words(t2):
+            return t2.rearrange("p (c i t) -> p c t i", i=RUN, t=PACK)
+
+        def as_planes(t3):
+            return t3.rearrange("p t (c i) -> p c t i", i=RUN)
+
+        for h in range(2):
+            m = slice(h * (P // 2), (h + 1) * (P // 2))
+            nc.scalar.activation(
+                wd_bf[:, :, m, :].rearrange("p t m j -> p m j t"),
+                wd_raw[h][:].rearrange("p j (m t) -> p m j t", t=PACK),
+                ACT.Copy,
+            )
+        for h in range(2):
+            nc.vector.tensor_copy(as_words(x_bf[h][:]), as_planes(x_got[:, :, half(h)]))
+        nc.vector.quantize_mx(x_codes[:, half(0)].bitcast(E4M3), x_scales[:, half(0)], x_bf[0][:])
+        nc.vector.quantize_mx(
+            wd_codes[:].bitcast(E4M3), wd_scales[:], wd_bf[:].rearrange("p t m j -> p (t m j)")
+        )
+        nc.vector.quantize_mx(x_codes[:, half(1)].bitcast(E4M3), x_scales[:, half(1)], x_bf[1][:])
+
+        a_banks = [[bank("a%d_%d" % (h, u)) for u in range(2)] for h in range(2)]
+        for h in range(2):
+            for t in range(PACK):
+                cols = slice(t * P, (t + 1) * P)
+                nc.tensor.matmul_mx(
+                    a_banks[h][t // 2][:, half(t % 2)],
+                    lhsT=wd_codes[:, cols].bitcast(E4M3),
+                    lhsT_scale=wd_scales[:, cols],
+                    rhs=x_codes[:, half(h)].bitcast(E4M3),
+                    rhs_scale=x_scales[:, half(h)],
+                    start=True,
+                    stop=True,
+                )
+
+        q = [tile("q%d" % h, [P, PACK, HALF], F32) for h in range(2)]
+        sq = [tile("sq%d" % h, [P, PACK, HALF], F32) for h in range(2)]
+        e = [tile("e%d" % h, [P, PACK, HALF], F32) for h in range(2)]
+        wq = [tile("wq%d" % h, [P, PACK, HALF], F32) for h in range(2)]
+        g_bf = [tile("g_bf%d" % h, [P, HALF * PACK], BF16) for h in range(2)]
+
+        def pair(t3, u):
+            return t3[:, 2 * u : 2 * u + 2, :].rearrange("p t n -> p (t n)")
+
+        def residual(h):
+            for u in range(2):
+                nc.vector.tensor_tensor(pair(q[h], u), a_banks[h][u][:], pair(y_sb[h], u), ALU.subtract)
+                nc.scalar.activation(pair(sq[h], u), pair(q[h], u), ACT.Square)
+                nc.scalar.activation(pair(e[h], u), pair(sq[h], u), ACT.Exp, scale=-0.5)
+
+        def weigh(h):
+            for t in range(PACK):
+                nc.vector.scalar_tensor_tensor(
+                    wq[h][:, t, :], q[h][:, t, :], cw_sb[:, t : t + 1], rw_sb[:, half(h)], ALU.mult, ALU.mult
+                )
+
+        def gradient(h):
+            nc.vector.tensor_tensor(as_words(g_bf[h][:]), as_planes(wq[h][:]), as_planes(e[h][:]), ALU.mult)
+
+        def quantize_g(h):
+            nc.vector.quantize_mx(g_codes[:, half(h + 1)].bitcast(E5M2), g_scales[:, half(h + 1)], g_bf[h][:])
+
+        def round_wv(h):
+            nc.scalar.activation(as_words(wv_bf[h][:]), as_planes(wv_raw[h][:]), ACT.Copy)
+
+        def quantize_wv(h):
+            nc.vector.quantize_mx(wv_codes[:, half(h)].bitcast(E4M3), wv_scales[:, half(h)], wv_bf[h][:])
+
+        def product(b, first, lo, name):
+            cols = slice(b * P, (b + 1) * P)
+            mov = slice(first, first + 2 * HALF)
+            acc = bank(name)
+            nc.tensor.matmul_mx(
+                acc[:],
+                lhsT=wv_codes[:, cols].bitcast(E4M3),
+                lhsT_scale=wv_scales[:, cols],
+                rhs=g_codes[:, mov].bitcast(E5M2),
+                rhs_scale=g_scales[:, mov],
+                start=True,
+                stop=True,
+            )
+            staged = tile("dx_" + name, [P, 2 * HALF - lo], F32)
+            nc.scalar.activation(staged[:], acc[:, lo:], ACT.Copy)
+            return staged
+
+        def scatter(b, staged, entries):
+            cols = slice(entries.start // 16, entries.stop // 16)
+            nc.vector.tensor_copy(windows[b][:].indirect(offsets[:, cols]), staged[:])
+
+        residual(0)
+        weigh(0)
+        round_wv(0)
+        gradient(0)
+        residual(1)
+        quantize_g(0)
+        quantize_wv(0)
+        early = [product(b, 0, HALF, "early%d" % b) for b in range(2)]
+        weigh(1)
+        round_wv(1)
+        gradient(1)
+        scatter(0, early[0], half(0))
+        quantize_g(1)
+        quantize_wv(1)
+        late = [product(b, HALF, HALF if b < 2 else 0, "late%d" % b) for b in range(D // P)]
+        scatter(1, early[1], half(0))
+        for b in range(D // P):
+            scatter(b, late[b], half(1) if b < 2 else slice(0, N))
+            nc.sync.dma_start(out[b * P : (b + 1) * P, :], windows[b][:])

@@ -18,7 +18,7 @@ ALU = mybir.AluOpType
 P = 128
 PACK = 4
 HALF = 256
-RUN = 4
+RUN = 2
 
 
 def tile_attend_gml_wel_kernel(tc, xT, wd, wv, y, cw, rw, offs, out):
@@ -40,24 +40,23 @@ def tile_attend_gml_wel_kernel(tc, xT, wd, wv, y, cw, rw, offs, out):
         nc.sync.dma_start(offsets[:], offs)
         x_planes = xT.rearrange("(p t) n -> p t n", t=PACK)
         x_raw = [tile("x_raw%d" % t, [P, T], F32) for t in range(PACK)]
-        for t in range(PACK):
+        for t in (0, 2, 1, 3):
             nc.sync.dma_start(x_raw[t][:], x_planes[:, t, :])
         wd_planes = wd.rearrange("(p j) v -> p j v", j=PACK)
         wv_planes = wv.rearrange("(p j) d -> p j d", j=PACK)
         y_planes = y.rearrange("(p t) n -> p t n", t=PACK)
-        wd_raw = [tile("wd_raw%d" % h, [P, PACK, HALF], F32) for h in range(2)]
+        wd_raw = tile("wd_raw", [P, PACK, V], F32)
         wv_raw = [tile("wv_raw%d" % h, [P, PACK, HALF], F32) for h in range(2)]
-        y_sb = [tile("y_sb%d" % h, [P, PACK, HALF], F32) for h in range(2)]
+        y_sb = [tile("y_sb%d" % u, [P, 2, N], F32) for u in range(2)]
         cw_sb = tile("cw_sb", [P, PACK], F32)
         rw_sb = tile("rw_sb", [P, N], F32)
-        for h in range(2):
-            nc.sync.dma_start(wd_raw[h][:], wd_planes[:, :, half(h)])
-        nc.sync.dma_start(y_sb[0][:], y_planes[:, :, half(0)])
+        nc.sync.dma_start(wd_raw[:], wd_planes)
+        for u in range(2):
+            nc.sync.dma_start(y_sb[u][:], y_planes[:, 2 * u : 2 * u + 2, :])
         nc.sync.dma_start(cw_sb[:], cw.rearrange("(p t) o -> p (t o)", t=PACK))
         nc.sync.dma_start(rw_sb[:], rw)
-        nc.sync.dma_start(wv_raw[0][:], wv_planes[:, :, half(0)])
-        nc.sync.dma_start(y_sb[1][:], y_planes[:, :, half(1)])
-        nc.sync.dma_start(wv_raw[1][:], wv_planes[:, :, half(1)])
+        for h in range(2):
+            nc.sync.dma_start(wv_raw[h][:], wv_planes[:, :, half(h)])
 
         warm_in = tile("warm_in", [P, 8], F32)
         warm_out = tile("warm_out", [P, 8], F32)
@@ -66,20 +65,22 @@ def tile_attend_gml_wel_kernel(tc, xT, wd, wv, y, cw, rw, offs, out):
 
         windows = [tile("window%d" % b, [P, T], F32) for b in range(D // P)]
         for b in range(D // P):
-            nc.vector.memset(windows[b][:], 0.0)
+            (nc.vector if b < 2 else nc.gpsimd).memset(windows[b][:], 0.0)
         g_codes = tile("g_codes", [P, 3 * HALF], U32)
         g_scales = tile("g_scales", [P, 3 * HALF], U8)
-        nc.vector.memset(g_codes[:, 0:HALF], 0)
-        nc.vector.memset(g_scales[:, 0:HALF].bitcast(U32), 0)
+        nc.gpsimd.memset(g_codes[:, 0:HALF], 0)
+        nc.gpsimd.memset(g_scales[:, 0:HALF].bitcast(U32), 0)
 
-        x_got = tile("x_got", [P, PACK, N], F32)
-        for t in range(PACK):
-            nc.vector.tensor_copy(x_got[:, t, :], x_raw[t][:].indirect(offsets[:]))
+        x_bf = tile("x_bf", [P, N, PACK], BF16)
+        for t in range(2):
+            x_cast = tile("x_cast%d" % t, [P, T], BF16)
+            nc.vector.tensor_copy(x_cast[:], x_raw[t][:])
+            nc.scalar.activation(x_bf[:, :, t], x_cast[:].indirect(offsets[:]), ACT.Copy)
+            nc.vector.tensor_copy(x_bf[:, :, t + 2], x_raw[t + 2][:].indirect(offsets[:]))
 
-        x_bf = [tile("x_bf%d" % h, [P, HALF * PACK], BF16) for h in range(2)]
         x_codes = tile("x_codes", [P, N], U32)
         x_scales = tile("x_scales", [P, N], U8)
-        wd_bf = tile("wd_bf", [P, PACK, P, PACK], BF16)
+        wd_bf = [tile("wd_bf%d" % u, [P, 2, P, PACK], BF16) for u in range(2)]
         wd_codes = tile("wd_codes", [P, V], U32)
         wd_scales = tile("wd_scales", [P, V], U8)
         wv_bf = [tile("wv_bf%d" % h, [P, HALF * PACK], BF16) for h in range(2)]
@@ -92,20 +93,20 @@ def tile_attend_gml_wel_kernel(tc, xT, wd, wv, y, cw, rw, offs, out):
         def as_planes(t3):
             return t3.rearrange("p t (c i) -> p c t i", i=RUN)
 
-        for h in range(2):
-            m = slice(h * (P // 2), (h + 1) * (P // 2))
-            nc.scalar.activation(
-                wd_bf[:, :, m, :].rearrange("p t m j -> p m j t"),
-                wd_raw[h][:].rearrange("p j (m t) -> p m j t", t=PACK),
-                ACT.Copy,
+        wd_by_plane = wd_raw[:].rearrange("p j (m t) -> p m j t", t=PACK)
+
+        def quantize_wd(u):
+            nc.vector.quantize_mx(
+                wd_codes[:, half(u)].bitcast(E4M3),
+                wd_scales[:, half(u)],
+                wd_bf[u][:].rearrange("p t m j -> p (t m j)"),
             )
-        for h in range(2):
-            nc.vector.tensor_copy(as_words(x_bf[h][:]), as_planes(x_got[:, :, half(h)]))
-        nc.vector.quantize_mx(x_codes[:, half(0)].bitcast(E4M3), x_scales[:, half(0)], x_bf[0][:])
-        nc.vector.quantize_mx(
-            wd_codes[:].bitcast(E4M3), wd_scales[:], wd_bf[:].rearrange("p t m j -> p (t m j)")
-        )
-        nc.vector.quantize_mx(x_codes[:, half(1)].bitcast(E4M3), x_scales[:, half(1)], x_bf[1][:])
+
+        nc.scalar.activation(wd_bf[1][:].rearrange("p t m j -> p m j t"), wd_by_plane[:, :, :, 2:4], ACT.Copy)
+        nc.vector.tensor_copy(wd_bf[0][:].rearrange("p t m j -> p m j t"), wd_by_plane[:, :, :, 0:2])
+        nc.vector.quantize_mx(x_codes[:].bitcast(E4M3), x_scales[:], x_bf[:].rearrange("p n t -> p (n t)"))
+        for u in range(2):
+            quantize_wd(u)
 
         a_banks = [[bank("a%d_%d" % (h, u)) for u in range(2)] for h in range(2)]
         for h in range(2):
@@ -132,7 +133,12 @@ def tile_attend_gml_wel_kernel(tc, xT, wd, wv, y, cw, rw, offs, out):
 
         def residual(h):
             for u in range(2):
-                nc.vector.tensor_tensor(pair(q[h], u), a_banks[h][u][:], pair(y_sb[h], u), ALU.subtract)
+                nc.vector.tensor_tensor(
+                    q[h][:, 2 * u : 2 * u + 2, :],
+                    a_banks[h][u][:].rearrange("p (t n) -> p t n", t=2),
+                    y_sb[u][:, :, half(h)],
+                    ALU.subtract,
+                )
                 nc.scalar.activation(pair(sq[h], u), pair(q[h], u), ACT.Square)
                 nc.scalar.activation(pair(e[h], u), pair(sq[h], u), ACT.Exp, scale=-0.5)
 
@@ -167,13 +173,15 @@ def tile_attend_gml_wel_kernel(tc, xT, wd, wv, y, cw, rw, offs, out):
                 start=True,
                 stop=True,
             )
-            staged = tile("dx_" + name, [P, 2 * HALF - lo], F32)
-            nc.scalar.activation(staged[:], acc[:, lo:], ACT.Copy)
+            return acc[:, lo:]
+
+        def stage(acc, staged):
+            nc.scalar.activation(staged, acc, ACT.Copy)
             return staged
 
         def scatter(b, staged, entries):
             cols = slice(entries.start // 16, entries.stop // 16)
-            nc.vector.tensor_copy(windows[b][:].indirect(offsets[:, cols]), staged[:])
+            nc.vector.tensor_copy(windows[b][:].indirect(offsets[:, cols]), staged)
 
         residual(0)
         weigh(0)
@@ -183,14 +191,19 @@ def tile_attend_gml_wel_kernel(tc, xT, wd, wv, y, cw, rw, offs, out):
         quantize_g(0)
         quantize_wv(0)
         early = [product(b, 0, HALF, "early%d" % b) for b in range(2)]
+        early0 = stage(early[0], tile("dx_early0", [P, HALF], F32)[:])
         weigh(1)
         round_wv(1)
         gradient(1)
-        scatter(0, early[0], half(0))
+        early1 = stage(early[1], wq[1][:, 0, :])
+        scatter(0, early0, half(0))
         quantize_g(1)
         quantize_wv(1)
-        late = [product(b, HALF, HALF if b < 2 else 0, "late%d" % b) for b in range(D // P)]
-        scatter(1, early[1], half(0))
+        late = []
+        for b in range(D // P):
+            lo = HALF if b < 2 else 0
+            late.append(stage(product(b, HALF, lo, "late%d" % b), tile("dx_late%d" % b, [P, N - lo], F32)[:]))
+        scatter(1, early1, half(0))
         for b in range(D // P):
             scatter(b, late[b], half(1) if b < 2 else slice(0, N))
             nc.sync.dma_start(out[b * P : (b + 1) * P, :], windows[b][:])

@@ -17,105 +17,108 @@ ALU = mybir.AluOpType
 
 P = 128
 PACK = 4
+PAIR = 2
 HALF = 256
+GROUP = 16
+BANKS = 8
+EARLY_BLOCKS = 2
 RUN = 2
+GPSIMD_COLUMNS = 128
 
 
 def tile_attend_gml_wel_kernel(tc, xT, wd, wv, y, cw, rw, offs, out):
     nc = tc.nc
     with ExitStack() as ctx:
         sb = ctx.enter_context(tc.tile_pool(name="sb", bufs=1))
-        ps = ctx.enter_context(tc.psum_pool(name="ps", bufs=8))
+        ps = ctx.enter_context(tc.psum_pool(name="ps", bufs=BANKS))
 
         def tile(name, shape, dtype):
             return sb.tile(shape, dtype, name=name, align_bytes=64)
 
+        def bank(name):
+            return ps.tile([P, N], F32, name=name, tag="bank")
+
         def half(h):
             return slice(h * HALF, (h + 1) * HALF)
 
-        def bank(name):
-            return ps.tile([P, 2 * HALF], F32, name=name, tag="bank")
+        def planes(u):
+            return slice(PAIR * u, PAIR * (u + 1))
 
-        offsets = sb.tile([P, N // 16], U16, name="offsets")
+        def flat_pair(by_plane, u):
+            return by_plane[:, planes(u), :].rearrange("p t n -> p (t n)")
+
+        def as_words(packed):
+            return packed.rearrange("p (c i t) -> p c t i", i=RUN, t=PACK)
+
+        def as_planes(by_plane):
+            return by_plane.rearrange("p t (c i) -> p c t i", i=RUN)
+
+        offsets = sb.tile([P, N // GROUP], U16, name="offsets")
         nc.sync.dma_start(offsets[:], offs)
         x_planes = xT.rearrange("(p t) n -> p t n", t=PACK)
         x_raw = [tile("x_raw%d" % t, [P, T], F32) for t in range(PACK)]
-        for t in (0, 2, 1, 3):
+        for t in range(PAIR):
             nc.sync.dma_start(x_raw[t][:], x_planes[:, t, :])
+            nc.sync.dma_start(x_raw[t + PAIR][:], x_planes[:, t + PAIR, :])
         wd_planes = wd.rearrange("(p j) v -> p j v", j=PACK)
-        wv_planes = wv.rearrange("(p j) d -> p j d", j=PACK)
+        wv_planes = wv.rearrange("(p t) d -> p t d", t=PACK)
         y_planes = y.rearrange("(p t) n -> p t n", t=PACK)
         wd_raw = tile("wd_raw", [P, PACK, V], F32)
         wv_raw = [tile("wv_raw%d" % h, [P, PACK, HALF], F32) for h in range(2)]
-        y_sb = [tile("y_sb%d" % u, [P, 2, N], F32) for u in range(2)]
+        y_sb = [tile("y_sb%d" % u, [P, PAIR, N], F32) for u in range(2)]
         cw_sb = tile("cw_sb", [P, PACK], F32)
         rw_sb = tile("rw_sb", [P, N], F32)
         nc.sync.dma_start(wd_raw[:], wd_planes)
         for u in range(2):
-            nc.sync.dma_start(y_sb[u][:], y_planes[:, 2 * u : 2 * u + 2, :])
+            nc.sync.dma_start(y_sb[u][:], y_planes[:, planes(u), :])
         nc.sync.dma_start(cw_sb[:], cw.rearrange("(p t) o -> p (t o)", t=PACK))
         nc.sync.dma_start(rw_sb[:], rw)
         for h in range(2):
             nc.sync.dma_start(wv_raw[h][:], wv_planes[:, :, half(h)])
 
-        warm_in = tile("warm_in", [P, 8], F32)
-        warm_out = tile("warm_out", [P, 8], F32)
-        nc.gpsimd.memset(warm_in[:], 0.0)
-        nc.scalar.activation(warm_out[:], warm_in[:], ACT.Exp)
-
         windows = [tile("window%d" % b, [P, T], F32) for b in range(D // P)]
-        for b in range(D // P):
-            (nc.vector if b < 2 else nc.gpsimd).memset(windows[b][:], 0.0)
+        for b, engine in enumerate((nc.vector, nc.vector, nc.gpsimd, nc.gpsimd)):
+            engine.memset(windows[b][:], 0.0)
         g_codes = tile("g_codes", [P, 3 * HALF], U32)
         g_scales = tile("g_scales", [P, 3 * HALF], U8)
-        nc.gpsimd.memset(g_codes[:, 0:HALF], 0)
-        nc.gpsimd.memset(g_scales[:, 0:HALF].bitcast(U32), 0)
+        nc.gpsimd.memset(g_codes[:, half(0)], 0)
+        nc.gpsimd.memset(g_scales[:, half(0)].bitcast(U32), 0)
 
         x_bf = tile("x_bf", [P, N, PACK], BF16)
-        for t in range(2):
+        for t in range(PAIR):
             x_cast = tile("x_cast%d" % t, [P, T], BF16)
             nc.vector.tensor_copy(x_cast[:], x_raw[t][:])
             nc.scalar.activation(x_bf[:, :, t], x_cast[:].indirect(offsets[:]), ACT.Copy)
-            nc.vector.tensor_copy(x_bf[:, :, t + 2], x_raw[t + 2][:].indirect(offsets[:]))
+            nc.vector.tensor_copy(x_bf[:, :, t + PAIR], x_raw[t + PAIR][:].indirect(offsets[:]))
 
         x_codes = tile("x_codes", [P, N], U32)
         x_scales = tile("x_scales", [P, N], U8)
-        wd_bf = [tile("wd_bf%d" % u, [P, 2, P, PACK], BF16) for u in range(2)]
+        wd_bf = [tile("wd_bf%d" % u, [P, PAIR, P, PACK], BF16) for u in range(2)]
         wd_codes = tile("wd_codes", [P, V], U32)
         wd_scales = tile("wd_scales", [P, V], U8)
         wv_bf = [tile("wv_bf%d" % h, [P, HALF * PACK], BF16) for h in range(2)]
         wv_codes = tile("wv_codes", [P, D], U32)
         wv_scales = tile("wv_scales", [P, D], U8)
 
-        def as_words(t2):
-            return t2.rearrange("p (c i t) -> p c t i", i=RUN, t=PACK)
-
-        def as_planes(t3):
-            return t3.rearrange("p t (c i) -> p c t i", i=RUN)
-
         wd_by_plane = wd_raw[:].rearrange("p j (m t) -> p m j t", t=PACK)
-
-        def quantize_wd(u):
+        nc.scalar.activation(wd_bf[1][:].rearrange("p t m j -> p m j t"), wd_by_plane[:, :, :, planes(1)], ACT.Copy)
+        nc.vector.tensor_copy(wd_bf[0][:].rearrange("p t m j -> p m j t"), wd_by_plane[:, :, :, planes(0)])
+        nc.vector.quantize_mx(x_codes[:].bitcast(E4M3), x_scales[:], x_bf[:].rearrange("p n t -> p (n t)"))
+        for u in range(2):
             nc.vector.quantize_mx(
                 wd_codes[:, half(u)].bitcast(E4M3),
                 wd_scales[:, half(u)],
                 wd_bf[u][:].rearrange("p t m j -> p (t m j)"),
             )
 
-        nc.scalar.activation(wd_bf[1][:].rearrange("p t m j -> p m j t"), wd_by_plane[:, :, :, 2:4], ACT.Copy)
-        nc.vector.tensor_copy(wd_bf[0][:].rearrange("p t m j -> p m j t"), wd_by_plane[:, :, :, 0:2])
-        nc.vector.quantize_mx(x_codes[:].bitcast(E4M3), x_scales[:], x_bf[:].rearrange("p n t -> p (n t)"))
-        for u in range(2):
-            quantize_wd(u)
-
         a_banks = [[bank("a%d_%d" % (h, u)) for u in range(2)] for h in range(2)]
         for h in range(2):
             for t in range(PACK):
-                cols = slice(t * P, (t + 1) * P)
+                stationary = slice(t * P, (t + 1) * P)
                 nc.tensor.matmul_mx(
-                    a_banks[h][t // 2][:, half(t % 2)],
-                    lhsT=wd_codes[:, cols].bitcast(E4M3),
-                    lhsT_scale=wd_scales[:, cols],
+                    a_banks[h][t // PAIR][:, half(t % PAIR)],
+                    lhsT=wd_codes[:, stationary].bitcast(E4M3),
+                    lhsT_scale=wd_scales[:, stationary],
                     rhs=x_codes[:, half(h)].bitcast(E4M3),
                     rhs_scale=x_scales[:, half(h)],
                     start=True,
@@ -123,33 +126,36 @@ def tile_attend_gml_wel_kernel(tc, xT, wd, wv, y, cw, rw, offs, out):
                 )
 
         q = [tile("q%d" % h, [P, PACK, HALF], F32) for h in range(2)]
-        sq = [tile("sq%d" % h, [P, PACK, HALF], F32) for h in range(2)]
-        e = [tile("e%d" % h, [P, PACK, HALF], F32) for h in range(2)]
-        wq = [tile("wq%d" % h, [P, PACK, HALF], F32) for h in range(2)]
+        q_squared = [tile("sq%d" % h, [P, PACK, HALF], F32) for h in range(2)]
+        decay = [tile("e%d" % h, [P, PACK, HALF], F32) for h in range(2)]
+        q_weighted = [tile("wq%d" % h, [P, PACK, HALF], F32) for h in range(2)]
         g_bf = [tile("g_bf%d" % h, [P, HALF * PACK], BF16) for h in range(2)]
-
-        def pair(t3, u):
-            return t3[:, 2 * u : 2 * u + 2, :].rearrange("p t n -> p (t n)")
 
         def residual(h):
             for u in range(2):
                 nc.vector.tensor_tensor(
-                    q[h][:, 2 * u : 2 * u + 2, :],
-                    a_banks[h][u][:].rearrange("p (t n) -> p t n", t=2),
+                    q[h][:, planes(u), :],
+                    a_banks[h][u][:].rearrange("p (t n) -> p t n", t=PAIR),
                     y_sb[u][:, :, half(h)],
                     ALU.subtract,
                 )
-                nc.scalar.activation(pair(sq[h], u), pair(q[h], u), ACT.Square)
-                nc.scalar.activation(pair(e[h], u), pair(sq[h], u), ACT.Exp, scale=-0.5)
+                nc.scalar.activation(flat_pair(q_squared[h], u), flat_pair(q[h], u), ACT.Square)
+                nc.scalar.activation(flat_pair(decay[h], u), flat_pair(q_squared[h], u), ACT.Exp, scale=-0.5)
 
         def weigh(h):
             for t in range(PACK):
                 nc.vector.scalar_tensor_tensor(
-                    wq[h][:, t, :], q[h][:, t, :], cw_sb[:, t : t + 1], rw_sb[:, half(h)], ALU.mult, ALU.mult
+                    q_weighted[h][:, t, :], q[h][:, t, :], cw_sb[:, t : t + 1], rw_sb[:, half(h)], ALU.mult, ALU.mult
                 )
 
-        def gradient(h):
-            nc.vector.tensor_tensor(as_words(g_bf[h][:]), as_planes(wq[h][:]), as_planes(e[h][:]), ALU.mult)
+        def gradient(h, engine, first, last):
+            runs = slice(first // RUN, last // RUN)
+            engine.tensor_tensor(
+                as_words(g_bf[h][:])[:, runs],
+                as_planes(q_weighted[h][:])[:, runs],
+                as_planes(decay[h][:])[:, runs],
+                ALU.mult,
+            )
 
         def quantize_g(h):
             nc.vector.quantize_mx(g_codes[:, half(h + 1)].bitcast(E5M2), g_scales[:, half(h + 1)], g_bf[h][:])
@@ -160,50 +166,52 @@ def tile_attend_gml_wel_kernel(tc, xT, wd, wv, y, cw, rw, offs, out):
         def quantize_wv(h):
             nc.vector.quantize_mx(wv_codes[:, half(h)].bitcast(E4M3), wv_scales[:, half(h)], wv_bf[h][:])
 
-        def product(b, first, lo, name):
-            cols = slice(b * P, (b + 1) * P)
-            mov = slice(first, first + 2 * HALF)
+        def second_product(b, first, name):
+            stationary = slice(b * P, (b + 1) * P)
+            moving = slice(first, first + N)
             acc = bank(name)
             nc.tensor.matmul_mx(
                 acc[:],
-                lhsT=wv_codes[:, cols].bitcast(E4M3),
-                lhsT_scale=wv_scales[:, cols],
-                rhs=g_codes[:, mov].bitcast(E5M2),
-                rhs_scale=g_scales[:, mov],
+                lhsT=wv_codes[:, stationary].bitcast(E4M3),
+                lhsT_scale=wv_scales[:, stationary],
+                rhs=g_codes[:, moving].bitcast(E5M2),
+                rhs_scale=g_scales[:, moving],
                 start=True,
                 stop=True,
             )
-            return acc[:, lo:]
+            return acc
 
-        def stage(acc, staged):
-            nc.scalar.activation(staged, acc, ACT.Copy)
+        def stage(sums, staged):
+            nc.scalar.activation(staged, sums, ACT.Copy)
             return staged
 
         def scatter(b, staged, entries):
-            cols = slice(entries.start // 16, entries.stop // 16)
-            nc.vector.tensor_copy(windows[b][:].indirect(offsets[:, cols]), staged)
+            listed = offsets[:, entries.start // GROUP : entries.stop // GROUP]
+            nc.vector.tensor_copy(windows[b][:].indirect(listed), staged)
 
         residual(0)
         weigh(0)
         round_wv(0)
-        gradient(0)
+        gradient(0, nc.vector, 0, HALF)
         residual(1)
         quantize_g(0)
         quantize_wv(0)
-        early = [product(b, 0, HALF, "early%d" % b) for b in range(2)]
-        early0 = stage(early[0], tile("dx_early0", [P, HALF], F32)[:])
+        early = [second_product(b, 0, "early%d" % b)[:, half(1)] for b in range(EARLY_BLOCKS)]
+        early_first = stage(early[0], tile("dx_early0", [P, HALF], F32)[:])
         weigh(1)
         round_wv(1)
-        gradient(1)
-        early1 = stage(early[1], wq[1][:, 0, :])
-        scatter(0, early0, half(0))
+        gradient(1, nc.gpsimd, 0, GPSIMD_COLUMNS)
+        gradient(1, nc.vector, GPSIMD_COLUMNS, HALF)
+        early_second = stage(early[1], q_weighted[1][:, 0, :])
+        scatter(0, early_first, half(0))
         quantize_g(1)
         quantize_wv(1)
+        remaining = [half(1) if b < EARLY_BLOCKS else slice(0, N) for b in range(D // P)]
         late = []
-        for b in range(D // P):
-            lo = HALF if b < 2 else 0
-            late.append(stage(product(b, HALF, lo, "late%d" % b), tile("dx_late%d" % b, [P, N - lo], F32)[:]))
-        scatter(1, early1, half(0))
-        for b in range(D // P):
-            scatter(b, late[b], half(1) if b < 2 else slice(0, N))
+        for b, entries in enumerate(remaining):
+            sums = second_product(b, HALF, "late%d" % b)[:, entries]
+            late.append(stage(sums, tile("dx_late%d" % b, [P, entries.stop - entries.start], F32)[:]))
+        scatter(1, early_second, half(0))
+        for b, entries in enumerate(remaining):
+            scatter(b, late[b], entries)
             nc.sync.dma_start(out[b * P : (b + 1) * P, :], windows[b][:])

@@ -1,6 +1,7 @@
 from contextlib import ExitStack
 
 import concourse.mybir as mybir
+from concourse.masks import make_identity
 
 N, T, D, V = 512, 1024, 512, 512
 FLOPS = 2 * D * V * N + 2 * V * D * N
@@ -24,6 +25,9 @@ BANKS = 8
 EARLY_BLOCKS = 2
 RUN = 2
 GPSIMD_COLUMNS = 128
+CHUNKS = 4
+SCALAR_GROUPS = (64, 24)
+FIRST = 384
 
 
 def tile_attend_gml_wel_kernel(tc, xT, wd, wv, y, cw, rw, offs, out):
@@ -55,6 +59,10 @@ def tile_attend_gml_wel_kernel(tc, xT, wd, wv, y, cw, rw, offs, out):
 
         offsets = sb.tile([P, N // GROUP], U16, name="offsets")
         nc.sync.dma_start(offsets[:], offs)
+        cw_sb = tile("cw_sb", [P, PACK], F32)
+        rw_sb = tile("rw_sb", [P, PACK], F32)
+        nc.scalar.dma_start(rw_sb[:], rw[0:1, :].rearrange("o (m j) -> m (o j)", j=PACK))
+        nc.scalar.dma_start(cw_sb[:], cw.rearrange("(p t) o -> p (t o)", t=PACK))
         x_planes = xT.rearrange("(p t) n -> p t n", t=PACK)
         x_raw = [tile("x_raw%d" % t, [P, T], F32) for t in range(PACK)]
         for t in range(PAIR):
@@ -63,18 +71,28 @@ def tile_attend_gml_wel_kernel(tc, xT, wd, wv, y, cw, rw, offs, out):
         wd_planes = wd.rearrange("(p j) v -> p j v", j=PACK)
         wv_planes = wv.rearrange("(p t) d -> p t d", t=PACK)
         y_planes = y.rearrange("(p t) n -> p t n", t=PACK)
-        wd_raw = tile("wd_raw", [P, PACK, V], F32)
+        wd_raw = [sb.tile([P, PACK, HALF], F32, name="wd_raw%d" % h, tag=("wd_first", "wd_last")[h], align_bytes=64) for h in range(2)]
         wv_raw = [tile("wv_raw%d" % h, [P, PACK, HALF], F32) for h in range(2)]
-        y_sb = [tile("y_sb%d" % u, [P, PAIR, N], F32) for u in range(2)]
-        cw_sb = tile("cw_sb", [P, PACK], F32)
-        rw_sb = tile("rw_sb", [P, N], F32)
-        nc.sync.dma_start(wd_raw[:], wd_planes)
-        for u in range(2):
-            nc.sync.dma_start(y_sb[u][:], y_planes[:, planes(u), :])
-        nc.sync.dma_start(cw_sb[:], cw.rearrange("(p t) o -> p (t o)", t=PACK))
-        nc.sync.dma_start(rw_sb[:], rw)
+        y_sb = [tile("y_sb%d" % h, [P, PACK, HALF], F32) for h in range(2)]
         for h in range(2):
-            nc.sync.dma_start(wv_raw[h][:], wv_planes[:, :, half(h)])
+            nc.sync.dma_start(wd_raw[h][:], wd_planes[:, :, half(h)])
+        nc.sync.dma_start(wv_raw[0][:], wv_planes[:, :, half(0)])
+        nc.sync.dma_start(y_sb[0][:], y_planes[:, :, half(0)])
+        nc.sync.dma_start(y_sb[1][:], y_planes[:, :, half(1)])
+        nc.sync.dma_start(wv_raw[1][:], wv_planes[:, :, half(1)])
+
+        identity = tile("identity", [P, P], F32)
+        make_identity(nc, identity[:])
+        rw_bank = bank("rw_bank")
+        for j in range(PACK):
+            nc.tensor.transpose(rw_bank[:, j * P : (j + 1) * P], rw_sb[:, j : j + 1].to_broadcast([P, P]), identity[:])
+        rw_listed = rw_bank[:].rearrange("p (j m) -> p m j", j=PACK)
+
+        def rw_half(h):
+            return rw_listed[:, h * HALF // PACK : (h + 1) * HALF // PACK, :]
+
+        def in_fours(columns):
+            return columns.rearrange("p (m j) -> p m j", j=PACK)
 
         windows = [tile("window%d" % b, [P, T], F32) for b in range(D // P)]
         for b, engine in enumerate((nc.vector, nc.vector, nc.gpsimd, nc.gpsimd)):
@@ -84,87 +102,124 @@ def tile_attend_gml_wel_kernel(tc, xT, wd, wv, y, cw, rw, offs, out):
         nc.gpsimd.memset(g_codes[:, half(0)], 0)
         nc.gpsimd.memset(g_scales[:, half(0)].bitcast(U32), 0)
 
-        x_bf = tile("x_bf", [P, N, PACK], BF16)
+        x_cast = [tile("x_cast%d" % t, [P, T], BF16) for t in range(PAIR)]
+
+        def gather(x_bf, t, first, last):
+            listed = offsets[:, first // GROUP : last // GROUP]
+            nc.scalar.activation(x_bf[:, :, t], x_cast[t][:].indirect(listed), ACT.Copy)
+            nc.vector.tensor_copy(x_bf[:, :, t + PAIR], x_raw[t + PAIR][:].indirect(listed))
+
+        x_bf = tile("x_bf", [P, FIRST, PACK], BF16)
         for t in range(PAIR):
-            x_cast = tile("x_cast%d" % t, [P, T], BF16)
-            nc.vector.tensor_copy(x_cast[:], x_raw[t][:])
-            nc.scalar.activation(x_bf[:, :, t], x_cast[:].indirect(offsets[:]), ACT.Copy)
-            nc.vector.tensor_copy(x_bf[:, :, t + PAIR], x_raw[t + PAIR][:].indirect(offsets[:]))
+            nc.vector.tensor_copy(x_cast[t][:], x_raw[t][:])
+            gather(x_bf, t, 0, FIRST)
+
+        weights = tile("weights", [P, PACK, HALF], F32)
+        for t in range(PACK):
+            nc.scalar.activation(in_fours(weights[:, t, :]), rw_half(0), ACT.Copy, scale=cw_sb[:, t : t + 1])
 
         x_codes = tile("x_codes", [P, N], U32)
         x_scales = tile("x_scales", [P, N], U8)
-        wd_bf = [tile("wd_bf%d" % u, [P, PAIR, P, PACK], BF16) for u in range(2)]
+        wd_bf = sb.tile([P, PACK, P, PACK], BF16, name="wd_bf", tag="wd_bf", align_bytes=64)
         wd_codes = tile("wd_codes", [P, V], U32)
         wd_scales = tile("wd_scales", [P, V], U8)
-        wv_bf = [tile("wv_bf%d" % h, [P, HALF * PACK], BF16) for h in range(2)]
-        wv_codes = tile("wv_codes", [P, D], U32)
+        wv_bf = {0: tile("wv_bf0", [P, HALF * PACK], BF16)}
+        wv_codes = {1: tile("wv_codes1", [P, HALF], U32)}
         wv_scales = tile("wv_scales", [P, D], U8)
 
-        wd_by_plane = wd_raw[:].rearrange("p j (m t) -> p m j t", t=PACK)
-        nc.scalar.activation(wd_bf[1][:].rearrange("p t m j -> p m j t"), wd_by_plane[:, :, :, planes(1)], ACT.Copy)
-        nc.vector.tensor_copy(wd_bf[0][:].rearrange("p t m j -> p m j t"), wd_by_plane[:, :, :, planes(0)])
-        nc.vector.quantize_mx(x_codes[:].bitcast(E4M3), x_scales[:], x_bf[:].rearrange("p n t -> p (n t)"))
-        for u in range(2):
+        wd_dealt = wd_bf[:].rearrange("p t m j -> p m j t")
+        wd_by_plane = [wd_raw[h][:].rearrange("p j (m t) -> p m j t", t=PACK) for h in range(2)]
+        groups = HALF // PACK
+        for h, share in enumerate(SCALAR_GROUPS):
+            nc.scalar.activation(wd_dealt[:, h * groups : h * groups + share], wd_by_plane[h][:, :share], ACT.Copy)
+            if share < groups:
+                nc.vector.tensor_copy(wd_dealt[:, h * groups + share : (h + 1) * groups], wd_by_plane[h][:, share:])
+        for first, last in ((0, HALF), (HALF, FIRST)):
             nc.vector.quantize_mx(
-                wd_codes[:, half(u)].bitcast(E4M3),
-                wd_scales[:, half(u)],
-                wd_bf[u][:].rearrange("p t m j -> p (t m j)"),
+                x_codes[:, first:last].bitcast(E4M3),
+                x_scales[:, first:last],
+                x_bf[:, first:last, :].rearrange("p n t -> p (n t)"),
+            )
+        for t in range(PACK):
+            nc.vector.quantize_mx(
+                wd_codes[:, t * P : (t + 1) * P].bitcast(E4M3),
+                wd_scales[:, t * P : (t + 1) * P],
+                wd_bf[:, t].rearrange("p m j -> p (m j)"),
             )
 
-        a_banks = [[bank("a%d_%d" % (h, u)) for u in range(2)] for h in range(2)]
-        for h in range(2):
+        x_rest = sb.tile([P, N - FIRST, PACK], BF16, name="x_rest", tag="wd_last", align_bytes=64)
+        for t in range(PAIR):
+            gather(x_rest, t, FIRST, N)
+        nc.vector.quantize_mx(x_codes[:, FIRST:].bitcast(E4M3), x_scales[:, FIRST:], x_rest[:].rearrange("p n t -> p (n t)"))
+
+        a_banks = [bank("a%d" % c) for c in range(CHUNKS)]
+        for c in range(CHUNKS):
+            moving = slice(c * P, (c + 1) * P)
             for t in range(PACK):
                 stationary = slice(t * P, (t + 1) * P)
                 nc.tensor.matmul_mx(
-                    a_banks[h][t // PAIR][:, half(t % PAIR)],
+                    a_banks[c][:, stationary],
                     lhsT=wd_codes[:, stationary].bitcast(E4M3),
                     lhsT_scale=wd_scales[:, stationary],
-                    rhs=x_codes[:, half(h)].bitcast(E4M3),
-                    rhs_scale=x_scales[:, half(h)],
+                    rhs=x_codes[:, moving].bitcast(E4M3),
+                    rhs_scale=x_scales[:, moving],
                     start=True,
                     stop=True,
                 )
 
-        q = [tile("q%d" % h, [P, PACK, HALF], F32) for h in range(2)]
-        q_squared = [tile("sq%d" % h, [P, PACK, HALF], F32) for h in range(2)]
-        decay = [tile("e%d" % h, [P, PACK, HALF], F32) for h in range(2)]
-        q_weighted = [tile("wq%d" % h, [P, PACK, HALF], F32) for h in range(2)]
-        g_bf = [tile("g_bf%d" % h, [P, HALF * PACK], BF16) for h in range(2)]
+        q = [tile("q%d" % c, [P, PACK, P], F32) for c in range(CHUNKS)]
+        decay_all = tile("decay", [P, CHUNKS * N], F32)
+        decay = [decay_all[:, c * N : (c + 1) * N].rearrange("p (t n) -> p t n", t=PACK) for c in range(CHUNKS)]
+        q_weighted = [sb.tile([P, PACK, P], F32, name="wq%d" % c, tag="wq%d" % c, align_bytes=64) for c in range(CHUNKS)]
+        g_bf = {}
+        squared = {}
 
-        def residual(h):
-            for u in range(2):
-                nc.vector.tensor_tensor(
-                    q[h][:, planes(u), :],
-                    a_banks[h][u][:].rearrange("p (t n) -> p t n", t=PAIR),
-                    y_sb[u][:, :, half(h)],
-                    ALU.subtract,
-                )
-                nc.scalar.activation(flat_pair(q_squared[h], u), flat_pair(q[h], u), ACT.Square)
-                nc.scalar.activation(flat_pair(decay[h], u), flat_pair(q_squared[h], u), ACT.Exp, scale=-0.5)
+        def chunk(by_half, c):
+            return by_half[c // 2][:, :, (c % 2) * P : (c % 2 + 1) * P]
 
-        def weigh(h):
-            for t in range(PACK):
-                nc.vector.scalar_tensor_tensor(
-                    q_weighted[h][:, t, :], q[h][:, t, :], cw_sb[:, t : t + 1], rw_sb[:, half(h)], ALU.mult, ALU.mult
-                )
+        def residual(c):
+            nc.vector.tensor_tensor(
+                q[c][:], a_banks[c][:].rearrange("p (t n) -> p t n", t=PACK), chunk(y_sb, c), ALU.subtract
+            )
 
-        def gradient(h, engine, first, last):
+        def exponential(c):
+            squared[c] = sb.tile([P, PACK, P], F32, name="sq%d" % c, tag=["sqa","sqb","sqc","sqd"][c], align_bytes=64)
+            nc.scalar.activation(squared[c][:], q[c][:], ACT.Square)
+            nc.scalar.activation(decay[c][:], squared[c][:], ACT.Exp, scale=-0.5)
+
+        def weigh_gpsimd(c):
+            nc.gpsimd.tensor_tensor(q_weighted[c][:], q[c][:], chunk([weights], c), ALU.mult)
+
+        def weigh(c, t):
+            nc.vector.scalar_tensor_tensor(
+                in_fours(q_weighted[c][:, t, :]),
+                in_fours(q[c][:, t, :]),
+                cw_sb[:, t : t + 1],
+                rw_listed[:, c * P // PACK : (c + 1) * P // PACK, :],
+                ALU.mult,
+                ALU.mult,
+            )
+
+        def gradient(c, engine, first, last):
             runs = slice(first // RUN, last // RUN)
             engine.tensor_tensor(
-                as_words(g_bf[h][:])[:, runs],
-                as_planes(q_weighted[h][:])[:, runs],
-                as_planes(decay[h][:])[:, runs],
+                as_words(g_bf[c // 2][:, (c % 2) * N : (c % 2 + 1) * N])[:, runs],
+                as_planes(q_weighted[c][:])[:, runs],
+                as_planes(decay[c][:])[:, runs],
                 ALU.mult,
             )
 
         def quantize_g(h):
             nc.vector.quantize_mx(g_codes[:, half(h + 1)].bitcast(E5M2), g_scales[:, half(h + 1)], g_bf[h][:])
 
-        def round_wv(h):
-            nc.scalar.activation(as_words(wv_bf[h][:]), as_planes(wv_raw[h][:]), ACT.Copy)
+        def round_wv(h, engine):
+            if engine is nc.scalar:
+                nc.scalar.activation(as_words(wv_bf[h][:]), as_planes(wv_raw[h][:]), ACT.Copy)
+            else:
+                nc.vector.tensor_copy(as_words(wv_bf[h][:]), as_planes(wv_raw[h][:]))
 
         def quantize_wv(h):
-            nc.vector.quantize_mx(wv_codes[:, half(h)].bitcast(E4M3), wv_scales[:, half(h)], wv_bf[h][:])
+            nc.vector.quantize_mx(wv_codes[h][:].bitcast(E4M3), wv_scales[:, half(h)], wv_bf[h][:])
 
         def second_product(b, first, name):
             stationary = slice(b * P, (b + 1) * P)
@@ -172,7 +227,7 @@ def tile_attend_gml_wel_kernel(tc, xT, wd, wv, y, cw, rw, offs, out):
             acc = bank(name)
             nc.tensor.matmul_mx(
                 acc[:],
-                lhsT=wv_codes[:, stationary].bitcast(E4M3),
+                lhsT=wv_codes[b // 2][:, (b % 2) * P : (b % 2 + 1) * P].bitcast(E4M3),
                 lhsT_scale=wv_scales[:, stationary],
                 rhs=g_codes[:, moving].bitcast(E5M2),
                 rhs_scale=g_scales[:, moving],
@@ -189,21 +244,31 @@ def tile_attend_gml_wel_kernel(tc, xT, wd, wv, y, cw, rw, offs, out):
             listed = offsets[:, entries.start // GROUP : entries.stop // GROUP]
             nc.vector.tensor_copy(windows[b][:].indirect(listed), staged)
 
-        residual(0)
-        weigh(0)
-        round_wv(0)
-        gradient(0, nc.vector, 0, HALF)
-        residual(1)
-        quantize_g(0)
+        round_wv(0, nc.scalar)
+        for c in range(CHUNKS):
+            residual(c)
+        g_bf[0] = sb.tile([P, HALF * PACK], BF16, name="g_bf0", tag="g_bf0", align_bytes=64)
+        for c in range(2):
+            exponential(c)
+            weigh_gpsimd(c)
+        for c in range(2):
+            gradient(c, nc.vector, 0, P)
+        wv_codes[0] = sb.tile([P, HALF], U32, name="wv_codes0", tag="wq0", align_bytes=64)
         quantize_wv(0)
+        quantize_g(0)
         early = [second_product(b, 0, "early%d" % b)[:, half(1)] for b in range(EARLY_BLOCKS)]
         early_first = stage(early[0], tile("dx_early0", [P, HALF], F32)[:])
-        weigh(1)
-        round_wv(1)
-        gradient(1, nc.gpsimd, 0, GPSIMD_COLUMNS)
-        gradient(1, nc.vector, GPSIMD_COLUMNS, HALF)
-        early_second = stage(early[1], q_weighted[1][:, 0, :])
+        for c in range(2, 4):
+            for t in range(PACK):
+                weigh(c, t)
+            exponential(c)
+        g_bf[1] = sb.tile([P, HALF * PACK], BF16, name="g_bf1", tag="g_bf1", align_bytes=64)
+        gradient(2, nc.vector, 0, P)
+        gradient(3, nc.gpsimd, 0, P)
+        early_second = stage(early[1], decay_all[:, 3 * N - P : 3 * N + P])
         scatter(0, early_first, half(0))
+        wv_bf[1] = sb.tile([P, HALF * PACK], BF16, name="wv_bf1b", tag="wq3", align_bytes=64)
+        round_wv(1, nc.scalar)
         quantize_g(1)
         quantize_wv(1)
         remaining = [half(1) if b < EARLY_BLOCKS else slice(0, N) for b in range(D // P)]

@@ -26,8 +26,6 @@ EARLY_BLOCKS = 2
 RUN = 2
 GPSIMD_COLUMNS = 128
 CHUNKS = 4
-SCALAR_GROUPS = (64, 24)
-FIRST = 384
 
 
 def tile_attend_gml_wel_kernel(tc, xT, wd, wv, y, cw, rw, offs, out):
@@ -71,11 +69,10 @@ def tile_attend_gml_wel_kernel(tc, xT, wd, wv, y, cw, rw, offs, out):
         wd_planes = wd.rearrange("(p j) v -> p j v", j=PACK)
         wv_planes = wv.rearrange("(p t) d -> p t d", t=PACK)
         y_planes = y.rearrange("(p t) n -> p t n", t=PACK)
-        wd_raw = [sb.tile([P, PACK, HALF], F32, name="wd_raw%d" % h, tag=("wd_first", "wd_last")[h], align_bytes=64) for h in range(2)]
+        wd_raw = sb.tile([P, PACK, V], F32, name="wd_raw", tag="wd_last", align_bytes=64)
         wv_raw = [tile("wv_raw%d" % h, [P, PACK, HALF], F32) for h in range(2)]
         y_sb = [tile("y_sb%d" % h, [P, PACK, HALF], F32) for h in range(2)]
-        for h in range(2):
-            nc.sync.dma_start(wd_raw[h][:], wd_planes[:, :, half(h)])
+        nc.sync.dma_start(wd_raw[:], wd_planes)
         nc.sync.dma_start(wv_raw[0][:], wv_planes[:, :, half(0)])
         nc.sync.dma_start(y_sb[0][:], y_planes[:, :, half(0)])
         nc.sync.dma_start(y_sb[1][:], y_planes[:, :, half(1)])
@@ -104,53 +101,50 @@ def tile_attend_gml_wel_kernel(tc, xT, wd, wv, y, cw, rw, offs, out):
 
         x_cast = [tile("x_cast%d" % t, [P, T], BF16) for t in range(PAIR)]
 
-        def gather(x_bf, t, first, last):
-            listed = offsets[:, first // GROUP : last // GROUP]
-            nc.scalar.activation(x_bf[:, :, t], x_cast[t][:].indirect(listed), ACT.Copy)
-            nc.vector.tensor_copy(x_bf[:, :, t + PAIR], x_raw[t + PAIR][:].indirect(listed))
+        x_bf = tile("x_bf", [P, N, PACK], BF16)
 
-        x_bf = tile("x_bf", [P, FIRST, PACK], BF16)
-        for t in range(PAIR):
-            nc.vector.tensor_copy(x_cast[t][:], x_raw[t][:])
-            gather(x_bf, t, 0, FIRST)
+        def gather(t, first, last):
+            listed = offsets[:, first // GROUP : last // GROUP]
+            nc.scalar.activation(x_bf[:, first:last, t], x_cast[t][:].indirect(listed), ACT.Copy)
+            nc.vector.tensor_copy(x_bf[:, first:last, t + PAIR], x_raw[t + PAIR][:].indirect(listed))
+
+        nc.vector.tensor_copy(x_cast[0][:], x_raw[0][:])
+        gather(0, 0, N)
+        nc.vector.tensor_copy(x_cast[1][:], x_raw[1][:])
+        gather(1, 0, HALF)
+        gather(1, HALF, N)
 
         weights = tile("weights", [P, PACK, HALF], F32)
         for t in range(PACK):
             nc.scalar.activation(in_fours(weights[:, t, :]), rw_half(0), ACT.Copy, scale=cw_sb[:, t : t + 1])
 
-        x_codes = tile("x_codes", [P, N], U32)
+        x_codes = {0: tile("x_codes0", [P, HALF], U32)}
         x_scales = tile("x_scales", [P, N], U8)
-        wd_bf = sb.tile([P, PACK, P, PACK], BF16, name="wd_bf", tag="wd_bf", align_bytes=64)
+        wd_bf = [tile("wd_bf0", [P, PAIR, P, PACK], BF16), sb.tile([P, PAIR, P, PACK], BF16, name="wd_bf1", tag="wd_bf", align_bytes=64)]
         wd_codes = tile("wd_codes", [P, V], U32)
         wd_scales = tile("wd_scales", [P, V], U8)
         wv_bf = {0: tile("wv_bf0", [P, HALF * PACK], BF16)}
         wv_codes = {1: tile("wv_codes1", [P, HALF], U32)}
         wv_scales = tile("wv_scales", [P, D], U8)
 
-        wd_dealt = wd_bf[:].rearrange("p t m j -> p m j t")
-        wd_by_plane = [wd_raw[h][:].rearrange("p j (m t) -> p m j t", t=PACK) for h in range(2)]
-        groups = HALF // PACK
-        for h, share in enumerate(SCALAR_GROUPS):
-            nc.scalar.activation(wd_dealt[:, h * groups : h * groups + share], wd_by_plane[h][:, :share], ACT.Copy)
-            if share < groups:
-                nc.vector.tensor_copy(wd_dealt[:, h * groups + share : (h + 1) * groups], wd_by_plane[h][:, share:])
-        for first, last in ((0, HALF), (HALF, FIRST)):
+        wd_by_plane = wd_raw[:].rearrange("p j (m t) -> p m j t", t=PACK)
+        nc.scalar.activation(wd_bf[1][:].rearrange("p t m j -> p m j t"), wd_by_plane[:, :, :, planes(1)], ACT.Copy)
+        nc.vector.tensor_copy(wd_bf[0][:].rearrange("p t m j -> p m j t"), wd_by_plane[:, :, :, planes(0)])
+        def quantize_x(h):
             nc.vector.quantize_mx(
-                x_codes[:, first:last].bitcast(E4M3),
-                x_scales[:, first:last],
-                x_bf[:, first:last, :].rearrange("p n t -> p (n t)"),
-            )
-        for t in range(PACK):
-            nc.vector.quantize_mx(
-                wd_codes[:, t * P : (t + 1) * P].bitcast(E4M3),
-                wd_scales[:, t * P : (t + 1) * P],
-                wd_bf[:, t].rearrange("p m j -> p (m j)"),
+                x_codes[h][:].bitcast(E4M3), x_scales[:, half(h)], x_bf[:, half(h), :].rearrange("p n t -> p (n t)")
             )
 
-        x_rest = sb.tile([P, N - FIRST, PACK], BF16, name="x_rest", tag="wd_last", align_bytes=64)
-        for t in range(PAIR):
-            gather(x_rest, t, FIRST, N)
-        nc.vector.quantize_mx(x_codes[:, FIRST:].bitcast(E4M3), x_scales[:, FIRST:], x_rest[:].rearrange("p n t -> p (n t)"))
+        quantize_x(0)
+        for u in range(2):
+            nc.vector.quantize_mx(
+                wd_codes[:, half(u)].bitcast(E4M3),
+                wd_scales[:, half(u)],
+                wd_bf[u][:].rearrange("p t m j -> p (t m j)"),
+            )
+
+        x_codes[1] = sb.tile([P, HALF], U32, name="x_codes1", tag="wd_last", align_bytes=64)
+        quantize_x(1)
 
         a_banks = [bank("a%d" % c) for c in range(CHUNKS)]
         for c in range(CHUNKS):
@@ -161,7 +155,7 @@ def tile_attend_gml_wel_kernel(tc, xT, wd, wv, y, cw, rw, offs, out):
                     a_banks[c][:, stationary],
                     lhsT=wd_codes[:, stationary].bitcast(E4M3),
                     lhsT_scale=wd_scales[:, stationary],
-                    rhs=x_codes[:, moving].bitcast(E4M3),
+                    rhs=x_codes[c // 2][:, (c % 2) * P : (c % 2 + 1) * P].bitcast(E4M3),
                     rhs_scale=x_scales[:, moving],
                     start=True,
                     stop=True,
@@ -170,8 +164,10 @@ def tile_attend_gml_wel_kernel(tc, xT, wd, wv, y, cw, rw, offs, out):
         q = [tile("q%d" % c, [P, PACK, P], F32) for c in range(CHUNKS)]
         decay_all = tile("decay", [P, CHUNKS * N], F32)
         decay = [decay_all[:, c * N : (c + 1) * N].rearrange("p (t n) -> p t n", t=PACK) for c in range(CHUNKS)]
-        q_weighted = [sb.tile([P, PACK, P], F32, name="wq%d" % c, tag="wq%d" % c, align_bytes=64) for c in range(CHUNKS)]
-        g_bf = {}
+        late_words = tile("late_words", [P, HALF + N], F32)
+        q_weighted = {c: sb.tile([P, PACK, P], F32, name="wq%d" % c, tag="wq%d" % c, align_bytes=64)[:] for c in (0, 1, 3)}
+        q_weighted[2] = late_words[:, HALF:].rearrange("p (t n) -> p t n", t=PACK)
+        g_bf = {1: late_words[:, :N].bitcast(BF16)}
         squared = {}
 
         def chunk(by_half, c):
@@ -258,12 +254,13 @@ def tile_attend_gml_wel_kernel(tc, xT, wd, wv, y, cw, rw, offs, out):
         quantize_g(0)
         early = [second_product(b, 0, "early%d" % b)[:, half(1)] for b in range(EARLY_BLOCKS)]
         early_first = stage(early[0], tile("dx_early0", [P, HALF], F32)[:])
+        for t in range(PACK):
+            weigh(2, t)
         for c in range(2, 4):
-            for t in range(PACK):
-                weigh(c, t)
             exponential(c)
-        g_bf[1] = sb.tile([P, HALF * PACK], BF16, name="g_bf1", tag="g_bf1", align_bytes=64)
         gradient(2, nc.vector, 0, P)
+        for t in range(PACK):
+            weigh(3, t)
         gradient(3, nc.gpsimd, 0, P)
         early_second = stage(early[1], decay_all[:, 3 * N - P : 3 * N + P])
         scatter(0, early_first, half(0))

@@ -22,9 +22,7 @@ PAIR = 2
 HALF = 256
 GROUP = 16
 BANKS = 8
-EARLY_BLOCKS = 2
 RUN = 2
-GPSIMD_COLUMNS = 128
 CHUNKS = 4
 
 
@@ -34,8 +32,8 @@ def tile_attend_gml_wel_kernel(tc, xT, wd, wv, y, cw, rw, offs, out):
         sb = ctx.enter_context(tc.tile_pool(name="sb", bufs=1))
         ps = ctx.enter_context(tc.psum_pool(name="ps", bufs=BANKS))
 
-        def tile(name, shape, dtype):
-            return sb.tile(shape, dtype, name=name, align_bytes=64)
+        def tile(name, shape, dtype, tag=None):
+            return sb.tile(shape, dtype, name=name, tag=tag or name, align_bytes=64)
 
         def bank(name):
             return ps.tile([P, N], F32, name=name, tag="bank")
@@ -43,17 +41,20 @@ def tile_attend_gml_wel_kernel(tc, xT, wd, wv, y, cw, rw, offs, out):
         def half(h):
             return slice(h * HALF, (h + 1) * HALF)
 
+        def block(b):
+            return slice(b * P, (b + 1) * P)
+
         def planes(u):
             return slice(PAIR * u, PAIR * (u + 1))
-
-        def flat_pair(by_plane, u):
-            return by_plane[:, planes(u), :].rearrange("p t n -> p (t n)")
 
         def as_words(packed):
             return packed.rearrange("p (c i t) -> p c t i", i=RUN, t=PACK)
 
         def as_planes(by_plane):
             return by_plane.rearrange("p t (c i) -> p c t i", i=RUN)
+
+        def in_fours(columns):
+            return columns.rearrange("p (m j) -> p m j", j=PACK)
 
         offsets = sb.tile([P, N // GROUP], U16, name="offsets")
         nc.sync.dma_start(offsets[:], offs)
@@ -66,30 +67,23 @@ def tile_attend_gml_wel_kernel(tc, xT, wd, wv, y, cw, rw, offs, out):
         for t in range(PAIR):
             nc.sync.dma_start(x_raw[t][:], x_planes[:, t, :])
             nc.sync.dma_start(x_raw[t + PAIR][:], x_planes[:, t + PAIR, :])
-        wd_planes = wd.rearrange("(p j) v -> p j v", j=PACK)
         wv_planes = wv.rearrange("(p t) d -> p t d", t=PACK)
         y_planes = y.rearrange("(p t) n -> p t n", t=PACK)
-        wd_raw = sb.tile([P, PACK, V], F32, name="wd_raw", tag="wd_last", align_bytes=64)
+        wd_raw = tile("wd_raw", [P, PACK, V], F32)
         wv_raw = [tile("wv_raw%d" % h, [P, PACK, HALF], F32) for h in range(2)]
         y_sb = [tile("y_sb%d" % h, [P, PACK, HALF], F32) for h in range(2)]
-        nc.sync.dma_start(wd_raw[:], wd_planes)
+        nc.sync.dma_start(wd_raw[:], wd.rearrange("(p j) v -> p j v", j=PACK))
         nc.sync.dma_start(wv_raw[0][:], wv_planes[:, :, half(0)])
-        nc.sync.dma_start(y_sb[0][:], y_planes[:, :, half(0)])
-        nc.sync.dma_start(y_sb[1][:], y_planes[:, :, half(1)])
+        for h in range(2):
+            nc.sync.dma_start(y_sb[h][:], y_planes[:, :, half(h)])
         nc.sync.dma_start(wv_raw[1][:], wv_planes[:, :, half(1)])
 
         identity = tile("identity", [P, P], F32)
         make_identity(nc, identity[:])
         rw_bank = bank("rw_bank")
         for j in range(PACK):
-            nc.tensor.transpose(rw_bank[:, j * P : (j + 1) * P], rw_sb[:, j : j + 1].to_broadcast([P, P]), identity[:])
+            nc.tensor.transpose(rw_bank[:, block(j)], rw_sb[:, j : j + 1].to_broadcast([P, P]), identity[:])
         rw_listed = rw_bank[:].rearrange("p (j m) -> p m j", j=PACK)
-
-        def rw_half(h):
-            return rw_listed[:, h * HALF // PACK : (h + 1) * HALF // PACK, :]
-
-        def in_fours(columns):
-            return columns.rearrange("p (m j) -> p m j", j=PACK)
 
         windows = [tile("window%d" % b, [P, T], F32) for b in range(D // P)]
         for b, engine in enumerate((nc.vector, nc.vector, nc.gpsimd, nc.gpsimd)):
@@ -100,7 +94,6 @@ def tile_attend_gml_wel_kernel(tc, xT, wd, wv, y, cw, rw, offs, out):
         nc.gpsimd.memset(g_scales[:, half(0)].bitcast(U32), 0)
 
         x_cast = [tile("x_cast%d" % t, [P, T], BF16) for t in range(PAIR)]
-
         x_bf = tile("x_bf", [P, N, PACK], BF16)
 
         def gather(t, first, last):
@@ -116,115 +109,102 @@ def tile_attend_gml_wel_kernel(tc, xT, wd, wv, y, cw, rw, offs, out):
 
         weights = tile("weights", [P, PACK, HALF], F32)
         for t in range(PACK):
-            nc.scalar.activation(in_fours(weights[:, t, :]), rw_half(0), ACT.Copy, scale=cw_sb[:, t : t + 1])
+            nc.scalar.activation(
+                in_fours(weights[:, t, :]), rw_listed[:, : HALF // PACK, :], ACT.Copy, scale=cw_sb[:, t : t + 1]
+            )
 
-        x_codes = {0: tile("x_codes0", [P, HALF], U32)}
         x_scales = tile("x_scales", [P, N], U8)
-        wd_bf = [tile("wd_bf0", [P, PAIR, P, PACK], BF16), sb.tile([P, PAIR, P, PACK], BF16, name="wd_bf1", tag="wd_bf", align_bytes=64)]
+        wd_bf = [tile("wd_bf%d" % u, [P, PAIR, P, PACK], BF16) for u in range(2)]
         wd_codes = tile("wd_codes", [P, V], U32)
         wd_scales = tile("wd_scales", [P, V], U8)
-        wv_bf = {0: tile("wv_bf0", [P, HALF * PACK], BF16)}
-        wv_codes = {1: tile("wv_codes1", [P, HALF], U32)}
-        wv_scales = tile("wv_scales", [P, D], U8)
+
+        def quantize_x(h, tag):
+            codes = tile("x_codes%d" % h, [P, HALF], U32, tag)
+            nc.vector.quantize_mx(
+                codes[:].bitcast(E4M3), x_scales[:, half(h)], x_bf[:, half(h), :].rearrange("p n t -> p (n t)")
+            )
+            return codes
 
         wd_by_plane = wd_raw[:].rearrange("p j (m t) -> p m j t", t=PACK)
         nc.scalar.activation(wd_bf[1][:].rearrange("p t m j -> p m j t"), wd_by_plane[:, :, :, planes(1)], ACT.Copy)
         nc.vector.tensor_copy(wd_bf[0][:].rearrange("p t m j -> p m j t"), wd_by_plane[:, :, :, planes(0)])
-        def quantize_x(h):
+        x_codes = [quantize_x(0, "x_codes0")]
+        for t in range(PACK):
             nc.vector.quantize_mx(
-                x_codes[h][:].bitcast(E4M3), x_scales[:, half(h)], x_bf[:, half(h), :].rearrange("p n t -> p (n t)")
+                wd_codes[:, block(t)].bitcast(E4M3),
+                wd_scales[:, block(t)],
+                wd_bf[t // PAIR][:, t % PAIR].rearrange("p m j -> p (m j)"),
             )
+        x_codes.append(quantize_x(1, "wd_raw"))
 
-        quantize_x(0)
-        for u in range(2):
-            nc.vector.quantize_mx(
-                wd_codes[:, half(u)].bitcast(E4M3),
-                wd_scales[:, half(u)],
-                wd_bf[u][:].rearrange("p t m j -> p (t m j)"),
-            )
-
-        x_codes[1] = sb.tile([P, HALF], U32, name="x_codes1", tag="wd_last", align_bytes=64)
-        quantize_x(1)
-
-        a_banks = [bank("a%d" % c) for c in range(CHUNKS)]
-        for c in range(CHUNKS):
-            moving = slice(c * P, (c + 1) * P)
-            for t in range(PACK):
-                stationary = slice(t * P, (t + 1) * P)
+        parts = [(0, planes(0)), (0, planes(1))] + [(c, slice(0, PACK)) for c in range(1, CHUNKS)]
+        a_banks = [bank("a%d" % k) for k in range(len(parts))]
+        for k, (c, ts) in enumerate(parts):
+            for t in range(ts.start, ts.stop):
                 nc.tensor.matmul_mx(
-                    a_banks[c][:, stationary],
-                    lhsT=wd_codes[:, stationary].bitcast(E4M3),
-                    lhsT_scale=wd_scales[:, stationary],
-                    rhs=x_codes[c // 2][:, (c % 2) * P : (c % 2 + 1) * P].bitcast(E4M3),
-                    rhs_scale=x_scales[:, moving],
+                    a_banks[k][:, block(t)],
+                    lhsT=wd_codes[:, block(t)].bitcast(E4M3),
+                    lhsT_scale=wd_scales[:, block(t)],
+                    rhs=x_codes[c // 2][:, block(c % 2)].bitcast(E4M3),
+                    rhs_scale=x_scales[:, block(c)],
                     start=True,
                     stop=True,
                 )
 
-        q = [tile("q%d" % c, [P, PACK, P], F32) for c in range(CHUNKS)]
-        decay_all = tile("decay", [P, CHUNKS * N], F32)
-        decay = [decay_all[:, c * N : (c + 1) * N].rearrange("p (t n) -> p t n", t=PACK) for c in range(CHUNKS)]
-        late_words = tile("late_words", [P, HALF + N], F32)
-        q_weighted = {c: sb.tile([P, PACK, P], F32, name="wq%d" % c, tag="wq%d" % c, align_bytes=64)[:] for c in (0, 1, 3)}
-        q_weighted[2] = late_words[:, HALF:].rearrange("p (t n) -> p t n", t=PACK)
-        g_bf = {1: late_words[:, :N].bitcast(BF16)}
-        squared = {}
+        q_late = tile("q_late", [P, PACK, HALF], F32)
+        q = [tile("q%d" % c, [P, PACK, P], F32)[:] for c in range(2)] + [q_late[:, :, block(c)] for c in range(2)]
+        sq_late = tile("sq_late", [P, PACK, HALF], F32)
+        decay = [tile("e%d" % c, [P, PACK, P], F32) for c in range(2)]
+        decay_late = [tile("e%d" % c, [P, PACK, P], F32) for c in (2, 3)]
+        q_weighted = [tile("wq%d" % c, [P, PACK, P], F32) for c in range(2)]
+        wq_late = tile("wq_late", [P, PACK, HALF], F32)
+        g_first = tile("g_first", [P, HALF * PACK], BF16)
+        wv_scales = tile("wv_scales", [P, D], U8)
+        wv_codes = {}
 
-        def chunk(by_half, c):
-            return by_half[c // 2][:, :, (c % 2) * P : (c % 2 + 1) * P]
-
-        def residual(c):
+        def residual(k):
+            c, ts = parts[k]
             nc.vector.tensor_tensor(
-                q[c][:], a_banks[c][:].rearrange("p (t n) -> p t n", t=PACK), chunk(y_sb, c), ALU.subtract
+                q[c][:, ts],
+                a_banks[k][:].rearrange("p (t n) -> p t n", t=PACK)[:, ts],
+                y_sb[c // 2][:, ts, block(c % 2)],
+                ALU.subtract,
             )
 
-        def exponential(c):
-            squared[c] = sb.tile([P, PACK, P], F32, name="sq%d" % c, tag=["sqa","sqb","sqc","sqd"][c], align_bytes=64)
-            nc.scalar.activation(squared[c][:], q[c][:], ACT.Square)
-            nc.scalar.activation(decay[c][:], squared[c][:], ACT.Exp, scale=-0.5)
+        def weigh_late(first, last):
+            for t in range(PACK):
+                nc.vector.scalar_tensor_tensor(
+                    in_fours(wq_late[:, t, first:last]),
+                    in_fours(q_late[:, t, first:last]),
+                    cw_sb[:, t : t + 1],
+                    rw_listed[:, (HALF + first) // PACK : (HALF + last) // PACK, :],
+                    ALU.mult,
+                    ALU.mult,
+                )
 
-        def weigh_gpsimd(c):
-            nc.gpsimd.tensor_tensor(q_weighted[c][:], q[c][:], chunk([weights], c), ALU.mult)
+        def gradient(engine, words, weighted, exponential):
+            engine.tensor_tensor(as_words(words), as_planes(weighted), as_planes(exponential), ALU.mult)
 
-        def weigh(c, t):
-            nc.vector.scalar_tensor_tensor(
-                in_fours(q_weighted[c][:, t, :]),
-                in_fours(q[c][:, t, :]),
-                cw_sb[:, t : t + 1],
-                rw_listed[:, c * P // PACK : (c + 1) * P // PACK, :],
-                ALU.mult,
-                ALU.mult,
-            )
+        def quantize_g(words, first, last):
+            columns = slice(HALF + first, HALF + last)
+            nc.vector.quantize_mx(g_codes[:, columns].bitcast(E5M2), g_scales[:, columns], words)
 
-        def gradient(c, engine, first, last):
-            runs = slice(first // RUN, last // RUN)
-            engine.tensor_tensor(
-                as_words(g_bf[c // 2][:, (c % 2) * N : (c % 2 + 1) * N])[:, runs],
-                as_planes(q_weighted[c][:])[:, runs],
-                as_planes(decay[c][:])[:, runs],
-                ALU.mult,
-            )
+        def round_wv(h, tag):
+            rounded = tile("wv_bf%d" % h, [P, HALF * PACK], BF16, tag)
+            nc.scalar.activation(as_words(rounded[:]), as_planes(wv_raw[h][:]), ACT.Copy)
+            return rounded
 
-        def quantize_g(h):
-            nc.vector.quantize_mx(g_codes[:, half(h + 1)].bitcast(E5M2), g_scales[:, half(h + 1)], g_bf[h][:])
-
-        def round_wv(h, engine):
-            if engine is nc.scalar:
-                nc.scalar.activation(as_words(wv_bf[h][:]), as_planes(wv_raw[h][:]), ACT.Copy)
-            else:
-                nc.vector.tensor_copy(as_words(wv_bf[h][:]), as_planes(wv_raw[h][:]))
-
-        def quantize_wv(h):
-            nc.vector.quantize_mx(wv_codes[h][:].bitcast(E4M3), wv_scales[:, half(h)], wv_bf[h][:])
+        def quantize_wv(h, rounded, tag):
+            wv_codes[h] = tile("wv_codes%d" % h, [P, HALF], U32, tag)
+            nc.vector.quantize_mx(wv_codes[h][:].bitcast(E4M3), wv_scales[:, half(h)], rounded[:])
 
         def second_product(b, first, name):
-            stationary = slice(b * P, (b + 1) * P)
             moving = slice(first, first + N)
             acc = bank(name)
             nc.tensor.matmul_mx(
                 acc[:],
-                lhsT=wv_codes[b // 2][:, (b % 2) * P : (b % 2 + 1) * P].bitcast(E4M3),
-                lhsT_scale=wv_scales[:, stationary],
+                lhsT=wv_codes[b // 2][:, block(b % 2)].bitcast(E4M3),
+                lhsT_scale=wv_scales[:, block(b)],
                 rhs=g_codes[:, moving].bitcast(E5M2),
                 rhs_scale=g_scales[:, moving],
                 start=True,
@@ -240,40 +220,41 @@ def tile_attend_gml_wel_kernel(tc, xT, wd, wv, y, cw, rw, offs, out):
             listed = offsets[:, entries.start // GROUP : entries.stop // GROUP]
             nc.vector.tensor_copy(windows[b][:].indirect(listed), staged)
 
-        round_wv(0, nc.scalar)
-        for c in range(CHUNKS):
-            residual(c)
-        g_bf[0] = sb.tile([P, HALF * PACK], BF16, name="g_bf0", tag="g_bf0", align_bytes=64)
+        wv_first = round_wv(0, "wv_bf0")
+        for k in range(len(parts)):
+            residual(k)
+        squared = [tile("sq%d" % c, [P, PACK, P], F32) for c in range(2)]
+        for c, ts in parts[:-2]:
+            nc.scalar.activation(squared[c][:, ts], q[c][:, ts], ACT.Square)
+            nc.gpsimd.tensor_tensor(q_weighted[c][:, ts], q[c][:, ts], weights[:, ts, block(c)], ALU.mult)
+            if ts.stop == PACK:
+                nc.scalar.activation(decay[c][:], squared[c][:], ACT.Exp, scale=-0.5)
         for c in range(2):
-            exponential(c)
-            weigh_gpsimd(c)
+            gradient(nc.vector, g_first[:, c * N : (c + 1) * N], q_weighted[c][:], decay[c][:])
+        quantize_wv(0, wv_first, "wq0")
+        quantize_g(g_first[:], 0, HALF)
+        early = [second_product(b, 0, "early%d" % b) for b in range(2)]
+        early_first = stage(early[0][:, half(1)], tile("dx_early0", [P, HALF], F32)[:])
+        early_second = stage(early[1][:, block(2)], tile("dx_early1", [P, P], F32)[:])
+        g_second = tile("g_second", [P, HALF * PACK], BF16, "g_first")
         for c in range(2):
-            gradient(c, nc.vector, 0, P)
-        wv_codes[0] = sb.tile([P, HALF], U32, name="wv_codes0", tag="wq0", align_bytes=64)
-        quantize_wv(0)
-        quantize_g(0)
-        early = [second_product(b, 0, "early%d" % b)[:, half(1)] for b in range(EARLY_BLOCKS)]
-        early_first = stage(early[0], tile("dx_early0", [P, HALF], F32)[:])
-        for t in range(PACK):
-            weigh(2, t)
-        for c in range(2, 4):
-            exponential(c)
-        gradient(2, nc.vector, 0, P)
-        for t in range(PACK):
-            weigh(3, t)
-        gradient(3, nc.gpsimd, 0, P)
-        early_second = stage(early[1], decay_all[:, 3 * N - P : 3 * N + P])
+            nc.scalar.activation(sq_late[:, :, block(c)], q[2 + c], ACT.Square)
+        for c in range(2):
+            weigh_late(c * P, (c + 1) * P)
+            nc.scalar.activation(decay_late[c][:], sq_late[:, :, block(c)], ACT.Exp, scale=-0.5)
+            gradient(nc.gpsimd, g_second[:, c * N : (c + 1) * N], wq_late[:, :, block(c)], decay_late[c][:])
+        early_third = stage(early[1][:, block(3)], decay_late[1][:, 0])
         scatter(0, early_first, half(0))
-        wv_bf[1] = sb.tile([P, HALF * PACK], BF16, name="wv_bf1b", tag="wq3", align_bytes=64)
-        round_wv(1, nc.scalar)
-        quantize_g(1)
-        quantize_wv(1)
-        remaining = [half(1) if b < EARLY_BLOCKS else slice(0, N) for b in range(D // P)]
+        scatter(1, early_second, block(0))
+        wv_second = round_wv(1, "q_late")
+        quantize_g(g_second[:], HALF, N)
+        quantize_wv(1, wv_second, "wq_late")
+        remaining = [half(1), half(1), slice(0, N), slice(0, N)]
         late = []
         for b, entries in enumerate(remaining):
             sums = second_product(b, HALF, "late%d" % b)[:, entries]
             late.append(stage(sums, tile("dx_late%d" % b, [P, entries.stop - entries.start], F32)[:]))
-        scatter(1, early_second, half(0))
+        scatter(1, early_third, block(1))
         for b, entries in enumerate(remaining):
             scatter(b, late[b], entries)
-            nc.sync.dma_start(out[b * P : (b + 1) * P, :], windows[b][:])
+            nc.sync.dma_start(out[block(b), :], windows[b][:])

@@ -235,26 +235,24 @@ def tile_attend_gml_wel_kernel(tc, xT, wd, wv, y, cw, rw, offs, out):
         quantize_g(g_first[:], 0, HALF)
         early = [second_product(b, 0, "early%d" % b) for b in range(2)]
         early_first = stage(early[0][:, half(1)], tile("dx_early0", [P, HALF], F32)[:])
-        early_second = stage(early[1][:, block(2)], tile("dx_early1", [P, P], F32)[:])
-        g_second = tile("g_second", [P, HALF * PACK], BF16, "g_first")
+        g_second = tile("g_second", [P, HALF * PACK], BF16)
         for c in range(2):
             nc.scalar.activation(sq_late[:, :, block(c)], q[2 + c], ACT.Square)
         for c in range(2):
             weigh_late(c * P, (c + 1) * P)
             nc.scalar.activation(decay_late[c][:], sq_late[:, :, block(c)], ACT.Exp, scale=-0.5)
-            gradient(nc.gpsimd, g_second[:, c * N : (c + 1) * N], wq_late[:, :, block(c)], decay_late[c][:])
-        early_third = stage(early[1][:, block(3)], decay_late[1][:, 0])
+            gradient(nc.vector, g_second[:, c * N : (c + 1) * N], wq_late[:, :, block(c)], decay_late[c][:])
+        early_second = stage(early[1][:, half(1)], decay_late[1][:, :PAIR].rearrange("p t n -> p (t n)"))
         scatter(0, early_first, half(0))
-        scatter(1, early_second, block(0))
-        wv_second = round_wv(1, "q_late")
+        wv_second = round_wv(1, "wq_late")
         quantize_g(g_second[:], HALF, N)
-        quantize_wv(1, wv_second, "wq_late")
+        quantize_wv(1, wv_second, "wv_codes1")
         remaining = [half(1), half(1), slice(0, N), slice(0, N)]
         late = []
         for b, entries in enumerate(remaining):
             sums = second_product(b, HALF, "late%d" % b)[:, entries]
             late.append(stage(sums, tile("dx_late%d" % b, [P, entries.stop - entries.start], F32)[:]))
-        scatter(1, early_third, block(1))
+        scatter(1, early_second, half(0))
         for b, entries in enumerate(remaining):
             scatter(b, late[b], entries)
             nc.sync.dma_start(out[block(b), :], windows[b][:])

@@ -78,6 +78,10 @@ def tile_attend_gml_wel_kernel(tc, xT, wd, wv, y, cw, rw, offs, out):
             nc.sync.dma_start(y_sb[h][:], y_planes[:, :, half(h)])
         nc.sync.dma_start(wv_raw[1][:], wv_planes[:, :, half(1)])
 
+        warm = tile("warm", [P, PAIR], F32)
+        nc.gpsimd.memset(warm[:, :1], 0.0)
+        nc.scalar.activation(warm[:, 1:], warm[:, :1], ACT.Exp)
+
         identity = tile("identity", [P, P], F32)
         make_identity(nc, identity[:])
         rw_bank = bank("rw_bank")
@@ -226,11 +230,22 @@ def tile_attend_gml_wel_kernel(tc, xT, wd, wv, y, cw, rw, offs, out):
         squared = [tile("sq%d" % c, [P, PACK, P], F32) for c in range(2)]
         for c, ts in parts[:-2]:
             nc.scalar.activation(squared[c][:, ts], q[c][:, ts], ACT.Square)
-            nc.gpsimd.tensor_tensor(q_weighted[c][:, ts], q[c][:, ts], weights[:, ts, block(c)], ALU.mult)
             if ts.stop == PACK:
                 nc.scalar.activation(decay[c][:], squared[c][:], ACT.Exp, scale=-0.5)
-        for c in range(2):
-            gradient(nc.vector, g_first[:, c * N : (c + 1) * N], q_weighted[c][:], decay[c][:])
+        for c, u in ((0, 0), (0, 1), (1, 0)):
+            nc.gpsimd.tensor_tensor(q_weighted[c][:, planes(u)], q[c][:, planes(u)], weights[:, planes(u), block(c)], ALU.mult)
+        for t in range(PAIR, PACK):
+            nc.vector.scalar_tensor_tensor(
+                in_fours(q_weighted[1][:, t]),
+                in_fours(q[1][:, t]),
+                cw_sb[:, t : t + 1],
+                rw_listed[:, P // PACK : HALF // PACK, :],
+                ALU.mult,
+                ALU.mult,
+            )
+        weigh_late(0, HALF)
+        for c, engine in enumerate((nc.gpsimd, nc.vector)):
+            gradient(engine, g_first[:, c * N : (c + 1) * N], q_weighted[c][:], decay[c][:])
         quantize_wv(0, wv_first, "wq0")
         quantize_g(g_first[:], 0, HALF)
         early = [second_product(b, 0, "early%d" % b) for b in range(2)]
@@ -239,7 +254,6 @@ def tile_attend_gml_wel_kernel(tc, xT, wd, wv, y, cw, rw, offs, out):
         for c in range(2):
             nc.scalar.activation(sq_late[:, :, block(c)], q[2 + c], ACT.Square)
         for c in range(2):
-            weigh_late(c * P, (c + 1) * P)
             nc.scalar.activation(decay_late[c][:], sq_late[:, :, block(c)], ACT.Exp, scale=-0.5)
             gradient(nc.vector, g_second[:, c * N : (c + 1) * N], wq_late[:, :, block(c)], decay_late[c][:])
         early_second = stage(early[1][:, half(1)], decay_late[1][:, :PAIR].rearrange("p t n -> p (t n)"))

@@ -22,7 +22,7 @@ PAIR = 2
 HALF = 256
 GROUP = 16
 BANKS = 8
-RUN = 2
+RUN = 4
 CHUNKS = 4
 
 

@@ -78,10 +78,6 @@ def tile_attend_gml_wel_kernel(tc, xT, wd, wv, y, cw, rw, offs, out):
             nc.sync.dma_start(y_sb[h][:], y_planes[:, :, half(h)])
         nc.sync.dma_start(wv_raw[1][:], wv_planes[:, :, half(1)])
 
-        warm = tile("warm", [P, PAIR], F32)
-        nc.gpsimd.memset(warm[:, :1], 0.0)
-        nc.scalar.activation(warm[:, 1:], warm[:, :1], ACT.Exp)
-
         identity = tile("identity", [P, P], F32)
         make_identity(nc, identity[:])
         rw_bank = bank("rw_bank")

@@ -21,9 +21,10 @@ PACK = 4
 PAIR = 2
 HALF = 256
 GROUP = 16
+CHUNKS = N // P
 BANKS = 8
 RUN = 4
-CHUNKS = 4
+SCALAR_COLUMNS = 80
 
 
 def tile_attend_gml_wel_kernel(tc, xT, wd, wv, y, cw, rw, offs, out):
@@ -32,8 +33,8 @@ def tile_attend_gml_wel_kernel(tc, xT, wd, wv, y, cw, rw, offs, out):
         sb = ctx.enter_context(tc.tile_pool(name="sb", bufs=1))
         ps = ctx.enter_context(tc.psum_pool(name="ps", bufs=BANKS))
 
-        def tile(name, shape, dtype, tag=None):
-            return sb.tile(shape, dtype, name=name, tag=tag or name, align_bytes=64)
+        def tile(name, shape, dtype, takes_over=None):
+            return sb.tile(shape, dtype, name=name, tag=takes_over or name, align_bytes=64)
 
         def bank(name):
             return ps.tile([P, N], F32, name=name, tag="bank")
@@ -46,6 +47,9 @@ def tile_attend_gml_wel_kernel(tc, xT, wd, wv, y, cw, rw, offs, out):
 
         def planes(u):
             return slice(PAIR * u, PAIR * (u + 1))
+
+        def chunk_words(c):
+            return slice(c * P * PACK, (c + 1) * P * PACK)
 
         def as_words(packed):
             return packed.rearrange("p (c i t) -> p c t i", i=RUN, t=PACK)
@@ -83,7 +87,9 @@ def tile_attend_gml_wel_kernel(tc, xT, wd, wv, y, cw, rw, offs, out):
         rw_bank = bank("rw_bank")
         for j in range(PACK):
             nc.tensor.transpose(rw_bank[:, block(j)], rw_sb[:, j : j + 1].to_broadcast([P, P]), identity[:])
-        rw_listed = rw_bank[:].rearrange("p (j m) -> p m j", j=PACK)
+
+        def rw_entries(first, last):
+            return rw_bank[:].rearrange("p (j m) -> p m j", j=PACK)[:, first // PACK : last // PACK, :]
 
         windows = [tile("window%d" % b, [P, T], F32) for b in range(D // P)]
         for b, engine in enumerate((nc.vector, nc.vector, nc.gpsimd, nc.gpsimd)):
@@ -109,8 +115,9 @@ def tile_attend_gml_wel_kernel(tc, xT, wd, wv, y, cw, rw, offs, out):
 
         weights = tile("weights", [P, PACK, HALF], F32)
         for t in range(PACK):
+            columns = HALF if t < PAIR else P
             nc.scalar.activation(
-                in_fours(weights[:, t, :]), rw_listed[:, : HALF // PACK, :], ACT.Copy, scale=cw_sb[:, t : t + 1]
+                in_fours(weights[:, t, :columns]), rw_entries(0, columns), ACT.Copy, scale=cw_sb[:, t : t + 1]
             )
 
         x_scales = tile("x_scales", [P, N], U8)
@@ -118,26 +125,29 @@ def tile_attend_gml_wel_kernel(tc, xT, wd, wv, y, cw, rw, offs, out):
         wd_codes = tile("wd_codes", [P, V], U32)
         wd_scales = tile("wd_scales", [P, V], U8)
 
-        def quantize_x(h, tag):
-            codes = tile("x_codes%d" % h, [P, HALF], U32, tag)
+        def quantize_x(h, takes_over=None):
+            codes = tile("x_codes%d" % h, [P, HALF], U32, takes_over)
             nc.vector.quantize_mx(
                 codes[:].bitcast(E4M3), x_scales[:, half(h)], x_bf[:, half(h), :].rearrange("p n t -> p (n t)")
             )
             return codes
 
         wd_by_plane = wd_raw[:].rearrange("p j (m t) -> p m j t", t=PACK)
-        nc.scalar.activation(wd_bf[1][:].rearrange("p t m j -> p m j t"), wd_by_plane[:, :, :, planes(1)], ACT.Copy)
-        nc.vector.tensor_copy(wd_bf[0][:].rearrange("p t m j -> p m j t"), wd_by_plane[:, :, :, planes(0)])
-        x_codes = [quantize_x(0, "x_codes0")]
+        wd_dealt = [wd_bf[u][:].rearrange("p t m j -> p m j t") for u in range(2)]
+        nc.vector.tensor_copy(wd_dealt[0], wd_by_plane[:, :, :, planes(0)])
+        nc.scalar.activation(wd_dealt[1][:, :SCALAR_COLUMNS], wd_by_plane[:, :SCALAR_COLUMNS, :, planes(1)], ACT.Copy)
+        nc.vector.tensor_copy(wd_dealt[1][:, SCALAR_COLUMNS:], wd_by_plane[:, SCALAR_COLUMNS:, :, planes(1)])
+        x_codes = [quantize_x(0)]
         for t in range(PACK):
             nc.vector.quantize_mx(
                 wd_codes[:, block(t)].bitcast(E4M3),
                 wd_scales[:, block(t)],
                 wd_bf[t // PAIR][:, t % PAIR].rearrange("p m j -> p (m j)"),
             )
-        x_codes.append(quantize_x(1, "wd_raw"))
+        x_codes.append(quantize_x(1, takes_over="wd_raw"))
 
         parts = [(0, planes(0)), (0, planes(1))] + [(c, slice(0, PACK)) for c in range(1, CHUNKS)]
+        early_parts = [(c, ts) for c, ts in parts if c < 2]
         a_banks = [bank("a%d" % k) for k in range(len(parts))]
         for k, (c, ts) in enumerate(parts):
             for t in range(ts.start, ts.stop):
@@ -153,49 +163,37 @@ def tile_attend_gml_wel_kernel(tc, xT, wd, wv, y, cw, rw, offs, out):
 
         q_late = tile("q_late", [P, PACK, HALF], F32)
         q = [tile("q%d" % c, [P, PACK, P], F32)[:] for c in range(2)] + [q_late[:, :, block(c)] for c in range(2)]
-        sq_late = tile("sq_late", [P, PACK, HALF], F32)
-        decay = [tile("e%d" % c, [P, PACK, P], F32) for c in range(2)]
-        decay_late = [tile("e%d" % c, [P, PACK, P], F32) for c in (2, 3)]
-        q_weighted = [tile("wq%d" % c, [P, PACK, P], F32) for c in range(2)]
-        wq_late = tile("wq_late", [P, PACK, HALF], F32)
-        g_first = tile("g_first", [P, HALF * PACK], BF16)
+        squared_late = tile("sq_late", [P, PACK, HALF], F32)
+        decay = [tile("e%d" % c, [P, PACK, P], F32) for c in range(CHUNKS)]
+        weighted_early = [tile("wq%d" % c, [P, PACK, P], F32) for c in range(2)]
+        weighted_late = tile("wq_late", [P, PACK, HALF], F32)
+        g_early = tile("g_first", [P, HALF * PACK], BF16)
         wv_scales = tile("wv_scales", [P, D], U8)
         wv_codes = {}
 
-        def residual(k):
-            c, ts = parts[k]
-            nc.vector.tensor_tensor(
-                q[c][:, ts],
-                a_banks[k][:].rearrange("p (t n) -> p t n", t=PACK)[:, ts],
-                y_sb[c // 2][:, ts, block(c % 2)],
-                ALU.subtract,
+        def weigh(weighted, residual, t, first, last):
+            nc.vector.scalar_tensor_tensor(
+                in_fours(weighted[:, t]),
+                in_fours(residual[:, t]),
+                cw_sb[:, t : t + 1],
+                rw_entries(first, last),
+                ALU.mult,
+                ALU.mult,
             )
-
-        def weigh_late(first, last):
-            for t in range(PACK):
-                nc.vector.scalar_tensor_tensor(
-                    in_fours(wq_late[:, t, first:last]),
-                    in_fours(q_late[:, t, first:last]),
-                    cw_sb[:, t : t + 1],
-                    rw_listed[:, (HALF + first) // PACK : (HALF + last) // PACK, :],
-                    ALU.mult,
-                    ALU.mult,
-                )
 
         def gradient(engine, words, weighted, exponential):
             engine.tensor_tensor(as_words(words), as_planes(weighted), as_planes(exponential), ALU.mult)
 
-        def quantize_g(words, first, last):
-            columns = slice(HALF + first, HALF + last)
-            nc.vector.quantize_mx(g_codes[:, columns].bitcast(E5M2), g_scales[:, columns], words)
+        def quantize_g(h, words):
+            nc.vector.quantize_mx(g_codes[:, half(h + 1)].bitcast(E5M2), g_scales[:, half(h + 1)], words[:])
 
-        def round_wv(h, tag):
-            rounded = tile("wv_bf%d" % h, [P, HALF * PACK], BF16, tag)
+        def round_wv(h, takes_over=None):
+            rounded = tile("wv_bf%d" % h, [P, HALF * PACK], BF16, takes_over)
             nc.scalar.activation(as_words(rounded[:]), as_planes(wv_raw[h][:]), ACT.Copy)
             return rounded
 
-        def quantize_wv(h, rounded, tag):
-            wv_codes[h] = tile("wv_codes%d" % h, [P, HALF], U32, tag)
+        def quantize_wv(h, rounded, takes_over=None):
+            wv_codes[h] = tile("wv_codes%d" % h, [P, HALF], U32, takes_over)
             nc.vector.quantize_mx(wv_codes[h][:].bitcast(E4M3), wv_scales[:, half(h)], rounded[:])
 
         def second_product(b, first, name):
@@ -220,43 +218,46 @@ def tile_attend_gml_wel_kernel(tc, xT, wd, wv, y, cw, rw, offs, out):
             listed = offsets[:, entries.start // GROUP : entries.stop // GROUP]
             nc.vector.tensor_copy(windows[b][:].indirect(listed), staged)
 
-        wv_first = round_wv(0, "wv_bf0")
-        for k in range(len(parts)):
-            residual(k)
-        squared = [tile("sq%d" % c, [P, PACK, P], F32) for c in range(2)]
-        for c, ts in parts[:-2]:
-            nc.scalar.activation(squared[c][:, ts], q[c][:, ts], ACT.Square)
-            if ts.stop == PACK:
-                nc.scalar.activation(decay[c][:], squared[c][:], ACT.Exp, scale=-0.5)
-        for c, u in ((0, 0), (0, 1), (1, 0)):
-            nc.gpsimd.tensor_tensor(q_weighted[c][:, planes(u)], q[c][:, planes(u)], weights[:, planes(u), block(c)], ALU.mult)
-        for t in range(PAIR, PACK):
-            nc.vector.scalar_tensor_tensor(
-                in_fours(q_weighted[1][:, t]),
-                in_fours(q[1][:, t]),
-                cw_sb[:, t : t + 1],
-                rw_listed[:, P // PACK : HALF // PACK, :],
-                ALU.mult,
-                ALU.mult,
+        wv_first = round_wv(0)
+        for k, (c, ts) in enumerate(parts):
+            nc.vector.tensor_tensor(
+                q[c][:, ts],
+                a_banks[k][:].rearrange("p (t n) -> p t n", t=PACK)[:, ts],
+                y_sb[c // 2][:, ts, block(c % 2)],
+                ALU.subtract,
             )
-        weigh_late(0, HALF)
+
+        squared_early = [tile("sq%d" % c, [P, PACK, P], F32) for c in range(2)]
+        for c, ts in early_parts:
+            nc.scalar.activation(squared_early[c][:, ts], q[c][:, ts], ACT.Square)
+            if ts.stop == PACK:
+                nc.scalar.activation(decay[c][:], squared_early[c][:], ACT.Exp, scale=-0.5)
+        for c, u in ((0, 0), (0, 1), (1, 0)):
+            nc.gpsimd.tensor_tensor(
+                weighted_early[c][:, planes(u)], q[c][:, planes(u)], weights[:, planes(u), block(c)], ALU.mult
+            )
+        for t in range(PAIR, PACK):
+            weigh(weighted_early[1], q[1], t, P, HALF)
+        for t in range(PACK):
+            weigh(weighted_late, q_late, t, HALF, N)
         for c, engine in enumerate((nc.gpsimd, nc.vector)):
-            gradient(engine, g_first[:, c * N : (c + 1) * N], q_weighted[c][:], decay[c][:])
-        quantize_wv(0, wv_first, "wq0")
-        quantize_g(g_first[:], 0, HALF)
-        early = [second_product(b, 0, "early%d" % b) for b in range(2)]
-        early_first = stage(early[0][:, half(1)], tile("dx_early0", [P, HALF], F32)[:])
-        g_second = tile("g_second", [P, HALF * PACK], BF16)
+            gradient(engine, g_early[:, chunk_words(c)], weighted_early[c][:], decay[c][:])
+        quantize_wv(0, wv_first, takes_over="wq1")
+        quantize_g(0, g_early)
+        early_sums = [second_product(b, 0, "early%d" % b)[:, half(1)] for b in range(2)]
+        early_first = stage(early_sums[0], tile("dx_early0", [P, HALF], F32)[:])
+
+        g_late = tile("g_second", [P, HALF * PACK], BF16)
         for c in range(2):
-            nc.scalar.activation(sq_late[:, :, block(c)], q[2 + c], ACT.Square)
+            nc.scalar.activation(squared_late[:, :, block(c)], q[2 + c], ACT.Square)
         for c in range(2):
-            nc.scalar.activation(decay_late[c][:], sq_late[:, :, block(c)], ACT.Exp, scale=-0.5)
-            gradient(nc.vector, g_second[:, c * N : (c + 1) * N], wq_late[:, :, block(c)], decay_late[c][:])
-        early_second = stage(early[1][:, half(1)], decay_late[1][:, :PAIR].rearrange("p t n -> p (t n)"))
+            nc.scalar.activation(decay[2 + c][:], squared_late[:, :, block(c)], ACT.Exp, scale=-0.5)
+            gradient(nc.vector, g_late[:, chunk_words(c)], weighted_late[:, :, block(c)], decay[2 + c][:])
+        early_second = stage(early_sums[1], decay[3][:, planes(0)].rearrange("p t n -> p (t n)"))
         scatter(0, early_first, half(0))
-        wv_second = round_wv(1, "wq_late")
-        quantize_g(g_second[:], HALF, N)
-        quantize_wv(1, wv_second, "wv_codes1")
+        wv_second = round_wv(1, takes_over="wq_late")
+        quantize_g(1, g_late)
+        quantize_wv(1, wv_second)
         remaining = [half(1), half(1), slice(0, N), slice(0, N)]
         late = []
         for b, entries in enumerate(remaining):

@@ -22,22 +22,20 @@ PAIR = 2
 HALF = 256
 GROUP = 16
 CHUNKS = N // P
-BANKS = 8
 RUN = 4
-SCALAR_COLUMNS = 80
 
 
 def tile_attend_gml_wel_kernel(tc, xT, wd, wv, y, cw, rw, offs, out):
     nc = tc.nc
     with ExitStack() as ctx:
         sb = ctx.enter_context(tc.tile_pool(name="sb", bufs=1))
-        ps = ctx.enter_context(tc.psum_pool(name="ps", bufs=BANKS))
+        ps = ctx.enter_context(tc.psum_pool(name="ps", bufs=1))
 
         def tile(name, shape, dtype, takes_over=None):
             return sb.tile(shape, dtype, name=name, tag=takes_over or name, align_bytes=64)
 
-        def bank(name):
-            return ps.tile([P, N], F32, name=name, tag="bank")
+        def bank(name, takes_over=None):
+            return ps.tile([P, N], F32, name=name, tag=takes_over or name)
 
         def half(h):
             return slice(h * HALF, (h + 1) * HALF)
@@ -88,8 +86,8 @@ def tile_attend_gml_wel_kernel(tc, xT, wd, wv, y, cw, rw, offs, out):
         for j in range(PACK):
             nc.tensor.transpose(rw_bank[:, block(j)], rw_sb[:, j : j + 1].to_broadcast([P, P]), identity[:])
 
-        def rw_entries(first, last):
-            return rw_bank[:].rearrange("p (j m) -> p m j", j=PACK)[:, first // PACK : last // PACK, :]
+        def rw_entries(entries):
+            return rw_bank[:].rearrange("p (j m) -> p m j", j=PACK)[:, entries.start // PACK : entries.stop // PACK, :]
 
         windows = [tile("window%d" % b, [P, T], F32) for b in range(D // P)]
         for b, engine in enumerate((nc.vector, nc.vector, nc.gpsimd, nc.gpsimd)):
@@ -113,12 +111,13 @@ def tile_attend_gml_wel_kernel(tc, xT, wd, wv, y, cw, rw, offs, out):
         gather(1, 0, HALF)
         gather(1, HALF, N)
 
-        weights = tile("weights", [P, PACK, HALF], F32)
-        for t in range(PACK):
-            columns = HALF if t < PAIR else P
-            nc.scalar.activation(
-                in_fours(weights[:, t, :columns]), rw_entries(0, columns), ACT.Copy, scale=cw_sb[:, t : t + 1]
-            )
+        weighted = [tile("wq%d" % h, [P, PACK, HALF], F32) for h in range(2)]
+        weights = [weighted[0][:, planes(1)], tile("weights", [P, PAIR, HALF], F32)[:]]
+        for h in range(2):
+            for t in range(PAIR):
+                nc.scalar.activation(
+                    in_fours(weights[h][:, t]), rw_entries(half(h)), ACT.Copy, scale=cw_sb[:, t : t + 1]
+                )
 
         x_scales = tile("x_scales", [P, N], U8)
         wd_bf = [tile("wd_bf%d" % u, [P, PAIR, P, PACK], BF16) for u in range(2)]
@@ -135,8 +134,7 @@ def tile_attend_gml_wel_kernel(tc, xT, wd, wv, y, cw, rw, offs, out):
         wd_by_plane = wd_raw[:].rearrange("p j (m t) -> p m j t", t=PACK)
         wd_dealt = [wd_bf[u][:].rearrange("p t m j -> p m j t") for u in range(2)]
         nc.vector.tensor_copy(wd_dealt[0], wd_by_plane[:, :, :, planes(0)])
-        nc.scalar.activation(wd_dealt[1][:, :SCALAR_COLUMNS], wd_by_plane[:, :SCALAR_COLUMNS, :, planes(1)], ACT.Copy)
-        nc.vector.tensor_copy(wd_dealt[1][:, SCALAR_COLUMNS:], wd_by_plane[:, SCALAR_COLUMNS:, :, planes(1)])
+        nc.vector.tensor_copy(wd_dealt[1], wd_by_plane[:, :, :, planes(1)])
         x_codes = [quantize_x(0)]
         for t in range(PACK):
             nc.vector.quantize_mx(
@@ -144,48 +142,40 @@ def tile_attend_gml_wel_kernel(tc, xT, wd, wv, y, cw, rw, offs, out):
                 wd_scales[:, block(t)],
                 wd_bf[t // PAIR][:, t % PAIR].rearrange("p m j -> p (m j)"),
             )
-        x_codes.append(quantize_x(1, takes_over="wd_raw"))
+        x_codes.append(quantize_x(1, takes_over="wd_bf0"))
 
-        parts = [(0, planes(0)), (0, planes(1))] + [(c, slice(0, PACK)) for c in range(1, CHUNKS)]
-        early_parts = [(c, ts) for c, ts in parts if c < 2]
-        a_banks = [bank("a%d" % k) for k in range(len(parts))]
-        for k, (c, ts) in enumerate(parts):
-            for t in range(ts.start, ts.stop):
-                nc.tensor.matmul_mx(
-                    a_banks[k][:, block(t)],
-                    lhsT=wd_codes[:, block(t)].bitcast(E4M3),
-                    lhsT_scale=wd_scales[:, block(t)],
-                    rhs=x_codes[c // 2][:, block(c % 2)].bitcast(E4M3),
-                    rhs_scale=x_scales[:, block(c)],
-                    start=True,
-                    stop=True,
-                )
+        a_banks = {}
+        for h in range(2):
+            for u in range(2):
+                a_banks[h, u] = bank("a%d%d" % (h, u))
+                for t in range(PAIR * u, PAIR * (u + 1)):
+                    nc.tensor.matmul_mx(
+                        a_banks[h, u][:, half(t % PAIR)],
+                        lhsT=wd_codes[:, block(t)].bitcast(E4M3),
+                        lhsT_scale=wd_scales[:, block(t)],
+                        rhs=x_codes[h][:].bitcast(E4M3),
+                        rhs_scale=x_scales[:, half(h)],
+                        start=True,
+                        stop=True,
+                    )
 
-        q_late = tile("q_late", [P, PACK, HALF], F32)
-        q = [tile("q%d" % c, [P, PACK, P], F32)[:] for c in range(2)] + [q_late[:, :, block(c)] for c in range(2)]
-        squared_late = tile("sq_late", [P, PACK, HALF], F32)
-        decay = [tile("e%d" % c, [P, PACK, P], F32) for c in range(CHUNKS)]
-        weighted_early = [tile("wq%d" % c, [P, PACK, P], F32) for c in range(2)]
-        weighted_late = tile("wq_late", [P, PACK, HALF], F32)
-        g_early = tile("g_first", [P, HALF * PACK], BF16)
+        q = [tile("q%d" % h, [P, PACK, HALF], F32) for h in range(2)]
+        squared = {(h, u): tile("sq%d%d" % (h, u), [P, PAIR, HALF], F32) for h in range(2) for u in range(2)}
+        decay = [tile("e%d" % h, [P, PACK, HALF], F32) for h in range(2)]
+        g_words = [tile("g%d" % h, [P, HALF * PACK], BF16) for h in range(2)]
         wv_scales = tile("wv_scales", [P, D], U8)
         wv_codes = {}
 
-        def weigh(weighted, residual, t, first, last):
-            nc.vector.scalar_tensor_tensor(
-                in_fours(weighted[:, t]),
-                in_fours(residual[:, t]),
-                cw_sb[:, t : t + 1],
-                rw_entries(first, last),
-                ALU.mult,
+        def gradient(h, c):
+            nc.vector.tensor_tensor(
+                as_words(g_words[h][:, chunk_words(c)]),
+                as_planes(weighted[h][:, :, block(c)]),
+                as_planes(decay[h][:, :, block(c)]),
                 ALU.mult,
             )
 
-        def gradient(engine, words, weighted, exponential):
-            engine.tensor_tensor(as_words(words), as_planes(weighted), as_planes(exponential), ALU.mult)
-
-        def quantize_g(h, words):
-            nc.vector.quantize_mx(g_codes[:, half(h + 1)].bitcast(E5M2), g_scales[:, half(h + 1)], words[:])
+        def quantize_g(h):
+            nc.vector.quantize_mx(g_codes[:, half(h + 1)].bitcast(E5M2), g_scales[:, half(h + 1)], g_words[h][:])
 
         def round_wv(h, takes_over=None):
             rounded = tile("wv_bf%d" % h, [P, HALF * PACK], BF16, takes_over)
@@ -196,9 +186,9 @@ def tile_attend_gml_wel_kernel(tc, xT, wd, wv, y, cw, rw, offs, out):
             wv_codes[h] = tile("wv_codes%d" % h, [P, HALF], U32, takes_over)
             nc.vector.quantize_mx(wv_codes[h][:].bitcast(E4M3), wv_scales[:, half(h)], rounded[:])
 
-        def second_product(b, first, name):
+        def second_product(b, first, name, takes_over=None):
             moving = slice(first, first + N)
-            acc = bank(name)
+            acc = bank(name, takes_over)
             nc.tensor.matmul_mx(
                 acc[:],
                 lhsT=wv_codes[b // 2][:, block(b % 2)].bitcast(E4M3),
@@ -219,51 +209,44 @@ def tile_attend_gml_wel_kernel(tc, xT, wd, wv, y, cw, rw, offs, out):
             nc.vector.tensor_copy(windows[b][:].indirect(listed), staged)
 
         wv_first = round_wv(0)
-        for k, (c, ts) in enumerate(parts):
-            nc.vector.tensor_tensor(
-                q[c][:, ts],
-                a_banks[k][:].rearrange("p (t n) -> p t n", t=PACK)[:, ts],
-                y_sb[c // 2][:, ts, block(c % 2)],
-                ALU.subtract,
-            )
-
-        squared_early = [tile("sq%d" % c, [P, PACK, P], F32) for c in range(2)]
-        for c, ts in early_parts:
-            nc.scalar.activation(squared_early[c][:, ts], q[c][:, ts], ACT.Square)
-            if ts.stop == PACK:
-                nc.scalar.activation(decay[c][:], squared_early[c][:], ACT.Exp, scale=-0.5)
-        for c, u in ((0, 0), (0, 1), (1, 0)):
-            nc.gpsimd.tensor_tensor(
-                weighted_early[c][:, planes(u)], q[c][:, planes(u)], weights[:, planes(u), block(c)], ALU.mult
-            )
-        for t in range(PAIR, PACK):
-            weigh(weighted_early[1], q[1], t, P, HALF)
-        for t in range(PACK):
-            weigh(weighted_late, q_late, t, HALF, N)
-        for c, engine in enumerate((nc.gpsimd, nc.vector)):
-            gradient(engine, g_early[:, chunk_words(c)], weighted_early[c][:], decay[c][:])
-        quantize_wv(0, wv_first, takes_over="wq1")
-        quantize_g(0, g_early)
+        for h in range(2):
+            for u in range(2):
+                nc.vector.tensor_tensor(
+                    q[h][:, planes(u)],
+                    a_banks[h, u][:].rearrange("p (t n) -> p t n", t=PAIR),
+                    y_sb[h][:, planes(u)],
+                    ALU.subtract,
+                )
+            nc.gpsimd.tensor_tensor(weighted[h][:, planes(0)], q[h][:, planes(0)], weights[h], ALU.mult)
+        for h in range(2):
+            for u in range(2):
+                nc.scalar.activation(squared[h, u][:], q[h][:, planes(u)], ACT.Square)
+            for u in range(2):
+                nc.scalar.activation(decay[h][:, planes(u)], squared[h, u][:], ACT.Exp, scale=-0.5)
+        for h in range(2):
+            for t in range(PAIR, PACK):
+                nc.vector.scalar_tensor_tensor(
+                    in_fours(weighted[h][:, t]),
+                    in_fours(q[h][:, t]),
+                    cw_sb[:, t : t + 1],
+                    rw_entries(half(h)),
+                    ALU.mult,
+                    ALU.mult,
+                )
+        for c in range(2):
+            gradient(0, c)
+        quantize_wv(0, wv_first, takes_over="weights")
+        quantize_g(0)
         early_sums = [second_product(b, 0, "early%d" % b)[:, half(1)] for b in range(2)]
-        early_first = stage(early_sums[0], tile("dx_early0", [P, HALF], F32)[:])
-
-        g_late = tile("g_second", [P, HALF * PACK], BF16)
         for c in range(2):
-            nc.scalar.activation(squared_late[:, :, block(c)], q[2 + c], ACT.Square)
-        for c in range(2):
-            nc.scalar.activation(decay[2 + c][:], squared_late[:, :, block(c)], ACT.Exp, scale=-0.5)
-            gradient(nc.vector, g_late[:, chunk_words(c)], weighted_late[:, :, block(c)], decay[2 + c][:])
-        early_second = stage(early_sums[1], decay[3][:, planes(0)].rearrange("p t n -> p (t n)"))
-        scatter(0, early_first, half(0))
-        wv_second = round_wv(1, takes_over="wq_late")
-        quantize_g(1, g_late)
+            gradient(1, c)
+        wv_second = round_wv(1, takes_over="sq10")
         quantize_wv(1, wv_second)
+        quantize_g(1)
+        for b in range(2):
+            scatter(b, stage(early_sums[b], tile("dx_early%d" % b, [P, HALF], F32)[:]), half(0))
         remaining = [half(1), half(1), slice(0, N), slice(0, N)]
-        late = []
         for b, entries in enumerate(remaining):
-            sums = second_product(b, HALF, "late%d" % b)[:, entries]
-            late.append(stage(sums, tile("dx_late%d" % b, [P, entries.stop - entries.start], F32)[:]))
-        scatter(1, early_second, half(0))
-        for b, entries in enumerate(remaining):
-            scatter(b, late[b], entries)
+            sums = second_product(b, HALF, "late%d" % b, "a%d%d" % (b // 2, b % 2))[:, entries]
+            scatter(b, stage(sums, tile("dx_late%d" % b, [P, entries.stop - entries.start], F32)[:]), entries)
             nc.sync.dma_start(out[block(b), :], windows[b][:])

@@ -23,6 +23,7 @@ HALF = 256
 GROUP = 16
 CHUNKS = N // P
 RUN = 4
+SCALAR_COLUMNS = 80
 
 
 def tile_attend_gml_wel_kernel(tc, xT, wd, wv, y, cw, rw, offs, out):
@@ -73,12 +74,11 @@ def tile_attend_gml_wel_kernel(tc, xT, wd, wv, y, cw, rw, offs, out):
         y_planes = y.rearrange("(p t) n -> p t n", t=PACK)
         wd_raw = tile("wd_raw", [P, PACK, V], F32)
         wv_raw = [tile("wv_raw%d" % h, [P, PACK, HALF], F32) for h in range(2)]
-        y_sb = [tile("y_sb%d" % h, [P, PACK, HALF], F32) for h in range(2)]
+        y_sb = tile("y_sb", [P, PACK, N], F32)
         nc.sync.dma_start(wd_raw[:], wd.rearrange("(p j) v -> p j v", j=PACK))
-        nc.sync.dma_start(wv_raw[0][:], wv_planes[:, :, half(0)])
+        nc.sync.dma_start(y_sb[:], y_planes)
         for h in range(2):
-            nc.sync.dma_start(y_sb[h][:], y_planes[:, :, half(h)])
-        nc.sync.dma_start(wv_raw[1][:], wv_planes[:, :, half(1)])
+            nc.sync.dma_start(wv_raw[h][:], wv_planes[:, :, half(h)])
 
         identity = tile("identity", [P, P], F32)
         make_identity(nc, identity[:])
@@ -112,12 +112,15 @@ def tile_attend_gml_wel_kernel(tc, xT, wd, wv, y, cw, rw, offs, out):
         gather(1, HALF, N)
 
         weighted = [tile("wq%d" % h, [P, PACK, HALF], F32) for h in range(2)]
-        weights = [weighted[0][:, planes(1)], tile("weights", [P, PAIR, HALF], F32)[:]]
-        for h in range(2):
+        weights = [weighted[0][:, planes(1)]]
+
+        def spread_weights(h):
             for t in range(PAIR):
                 nc.scalar.activation(
                     in_fours(weights[h][:, t]), rw_entries(half(h)), ACT.Copy, scale=cw_sb[:, t : t + 1]
                 )
+
+        spread_weights(0)
 
         x_scales = tile("x_scales", [P, N], U8)
         wd_bf = [tile("wd_bf%d" % u, [P, PAIR, P, PACK], BF16) for u in range(2)]
@@ -134,7 +137,10 @@ def tile_attend_gml_wel_kernel(tc, xT, wd, wv, y, cw, rw, offs, out):
         wd_by_plane = wd_raw[:].rearrange("p j (m t) -> p m j t", t=PACK)
         wd_dealt = [wd_bf[u][:].rearrange("p t m j -> p m j t") for u in range(2)]
         nc.vector.tensor_copy(wd_dealt[0], wd_by_plane[:, :, :, planes(0)])
-        nc.vector.tensor_copy(wd_dealt[1], wd_by_plane[:, :, :, planes(1)])
+        nc.scalar.activation(wd_dealt[1][:, :SCALAR_COLUMNS], wd_by_plane[:, :SCALAR_COLUMNS, :, planes(1)], ACT.Copy)
+        nc.vector.tensor_copy(wd_dealt[1][:, SCALAR_COLUMNS:], wd_by_plane[:, SCALAR_COLUMNS:, :, planes(1)])
+        weights.append(tile("weights", [P, PAIR, HALF], F32, takes_over="wd_raw")[:])
+        spread_weights(1)
         x_codes = [quantize_x(0)]
         for t in range(PACK):
             nc.vector.quantize_mx(
@@ -164,7 +170,7 @@ def tile_attend_gml_wel_kernel(tc, xT, wd, wv, y, cw, rw, offs, out):
         decay = [tile("e%d" % h, [P, PACK, HALF], F32) for h in range(2)]
         g_words = [tile("g%d" % h, [P, HALF * PACK], BF16) for h in range(2)]
         wv_scales = tile("wv_scales", [P, D], U8)
-        wv_codes = {}
+        wv_codes = tile("wv_codes", [P, D], U32)
 
         def gradient(h, c):
             nc.vector.tensor_tensor(
@@ -177,21 +183,25 @@ def tile_attend_gml_wel_kernel(tc, xT, wd, wv, y, cw, rw, offs, out):
         def quantize_g(h):
             nc.vector.quantize_mx(g_codes[:, half(h + 1)].bitcast(E5M2), g_scales[:, half(h + 1)], g_words[h][:])
 
-        def round_wv(h, takes_over=None):
-            rounded = tile("wv_bf%d" % h, [P, HALF * PACK], BF16, takes_over)
-            nc.scalar.activation(as_words(rounded[:]), as_planes(wv_raw[h][:]), ACT.Copy)
+        def round_wv(first, last, takes_over, engine):
+            rounded = tile("wv_bf%d" % first, [P, (last - first) * P * PACK], BF16, takes_over)
+            columns = as_planes(wv_raw[first // 2][:, :, first % 2 * P : ((last - 1) % 2 + 1) * P])
+            if engine is nc.vector:
+                nc.vector.tensor_copy(as_words(rounded[:]), columns)
+            else:
+                nc.scalar.activation(as_words(rounded[:]), columns, ACT.Copy)
             return rounded
 
-        def quantize_wv(h, rounded, takes_over=None):
-            wv_codes[h] = tile("wv_codes%d" % h, [P, HALF], U32, takes_over)
-            nc.vector.quantize_mx(wv_codes[h][:].bitcast(E4M3), wv_scales[:, half(h)], rounded[:])
+        def quantize_wv(first, last, words):
+            columns = slice(first * P, last * P)
+            nc.vector.quantize_mx(wv_codes[:, columns].bitcast(E4M3), wv_scales[:, columns], words)
 
         def second_product(b, first, name, takes_over=None):
             moving = slice(first, first + N)
             acc = bank(name, takes_over)
             nc.tensor.matmul_mx(
                 acc[:],
-                lhsT=wv_codes[b // 2][:, block(b % 2)].bitcast(E4M3),
+                lhsT=wv_codes[:, block(b)].bitcast(E4M3),
                 lhsT_scale=wv_scales[:, block(b)],
                 rhs=g_codes[:, moving].bitcast(E5M2),
                 rhs_scale=g_scales[:, moving],
@@ -208,13 +218,12 @@ def tile_attend_gml_wel_kernel(tc, xT, wd, wv, y, cw, rw, offs, out):
             listed = offsets[:, entries.start // GROUP : entries.stop // GROUP]
             nc.vector.tensor_copy(windows[b][:].indirect(listed), staged)
 
-        wv_first = round_wv(0)
         for h in range(2):
             for u in range(2):
                 nc.vector.tensor_tensor(
                     q[h][:, planes(u)],
                     a_banks[h, u][:].rearrange("p (t n) -> p t n", t=PAIR),
-                    y_sb[h][:, planes(u)],
+                    y_sb[:, planes(u), half(h)],
                     ALU.subtract,
                 )
             nc.gpsimd.tensor_tensor(weighted[h][:, planes(0)], q[h][:, planes(0)], weights[h], ALU.mult)
@@ -233,20 +242,22 @@ def tile_attend_gml_wel_kernel(tc, xT, wd, wv, y, cw, rw, offs, out):
                     ALU.mult,
                     ALU.mult,
                 )
+        wv_first = round_wv(0, 1, "wd_raw", nc.vector)
         for c in range(2):
             gradient(0, c)
-        quantize_wv(0, wv_first, takes_over="weights")
+        quantize_wv(0, 1, wv_first[:])
         quantize_g(0)
-        early_sums = [second_product(b, 0, "early%d" % b)[:, half(1)] for b in range(2)]
+        early_sums = second_product(0, 0, "early")[:, half(1)]
+        wv_second = round_wv(1, 2, "sq10", nc.scalar)
         for c in range(2):
             gradient(1, c)
-        wv_second = round_wv(1, takes_over="sq10")
-        quantize_wv(1, wv_second)
+        quantize_wv(1, 2, wv_second[:])
         quantize_g(1)
-        for b in range(2):
-            scatter(b, stage(early_sums[b], tile("dx_early%d" % b, [P, HALF], F32)[:]), half(0))
-        remaining = [half(1), half(1), slice(0, N), slice(0, N)]
-        for b, entries in enumerate(remaining):
+        scatter(0, stage(early_sums, decay[1][:, 0]), half(0))
+        wv_rest = round_wv(2, 4, "g1", nc.scalar)
+        for b, entries in ((1, slice(0, N)), (0, half(1)), (2, slice(0, N)), (3, slice(0, N))):
+            if b == 2:
+                quantize_wv(2, 4, wv_rest[:])
             sums = second_product(b, HALF, "late%d" % b, "a%d%d" % (b // 2, b % 2))[:, entries]
             scatter(b, stage(sums, tile("dx_late%d" % b, [P, entries.stop - entries.start], F32)[:]), entries)
             nc.sync.dma_start(out[block(b), :], windows[b][:])

@@ -74,9 +74,10 @@ def tile_attend_gml_wel_kernel(tc, xT, wd, wv, y, cw, rw, offs, out):
         y_planes = y.rearrange("(p t) n -> p t n", t=PACK)
         wd_raw = tile("wd_raw", [P, PACK, V], F32)
         wv_raw = [tile("wv_raw%d" % h, [P, PACK, HALF], F32) for h in range(2)]
-        y_sb = tile("y_sb", [P, PACK, N], F32)
+        y_sb = [tile("y_sb%d" % h, [P, PACK, HALF], F32) for h in range(2)]
         nc.sync.dma_start(wd_raw[:], wd.rearrange("(p j) v -> p j v", j=PACK))
-        nc.sync.dma_start(y_sb[:], y_planes)
+        for h in range(2):
+            nc.sync.dma_start(y_sb[h][:], y_planes[:, :, half(h)])
         for h in range(2):
             nc.sync.dma_start(wv_raw[h][:], wv_planes[:, :, half(h)])
 
@@ -90,7 +91,7 @@ def tile_attend_gml_wel_kernel(tc, xT, wd, wv, y, cw, rw, offs, out):
             return rw_bank[:].rearrange("p (j m) -> p m j", j=PACK)[:, entries.start // PACK : entries.stop // PACK, :]
 
         windows = [tile("window%d" % b, [P, T], F32) for b in range(D // P)]
-        for b, engine in enumerate((nc.vector, nc.vector, nc.gpsimd, nc.gpsimd)):
+        for b, engine in enumerate((nc.vector, nc.vector, nc.vector, nc.gpsimd)):
             engine.memset(windows[b][:], 0.0)
         g_codes = tile("g_codes", [P, 3 * HALF], U32)
         g_scales = tile("g_scales", [P, 3 * HALF], U8)
@@ -223,7 +224,7 @@ def tile_attend_gml_wel_kernel(tc, xT, wd, wv, y, cw, rw, offs, out):
                 nc.vector.tensor_tensor(
                     q[h][:, planes(u)],
                     a_banks[h, u][:].rearrange("p (t n) -> p t n", t=PAIR),
-                    y_sb[:, planes(u), half(h)],
+                    y_sb[h][:, planes(u)],
                     ALU.subtract,
                 )
             nc.gpsimd.tensor_tensor(weighted[h][:, planes(0)], q[h][:, planes(0)], weights[h], ALU.mult)
@@ -254,7 +255,7 @@ def tile_attend_gml_wel_kernel(tc, xT, wd, wv, y, cw, rw, offs, out):
         quantize_wv(1, 2, wv_second[:])
         quantize_g(1)
         scatter(0, stage(early_sums, decay[1][:, 0]), half(0))
-        wv_rest = round_wv(2, 4, "g1", nc.scalar)
+        wv_rest = round_wv(2, 4, "sq11", nc.scalar)
         for b, entries in ((1, slice(0, N)), (0, half(1)), (2, slice(0, N)), (3, slice(0, N))):
             if b == 2:
                 quantize_wv(2, 4, wv_rest[:])

@@ -73,13 +73,11 @@ def tile_attend_gml_wel_kernel(tc, xT, wd, wv, y, cw, rw, offs, out):
         wv_planes = wv.rearrange("(p t) d -> p t d", t=PACK)
         y_planes = y.rearrange("(p t) n -> p t n", t=PACK)
         wd_raw = tile("wd_raw", [P, PACK, V], F32)
-        wv_raw = [tile("wv_raw%d" % h, [P, PACK, HALF], F32) for h in range(2)]
-        y_sb = [tile("y_sb%d" % h, [P, PACK, HALF], F32) for h in range(2)]
+        wv_raw = tile("wv_raw", [P, PACK, D], F32)
+        y_sb = tile("y_sb", [P, PACK, N], F32)
         nc.sync.dma_start(wd_raw[:], wd.rearrange("(p j) v -> p j v", j=PACK))
-        for h in range(2):
-            nc.sync.dma_start(y_sb[h][:], y_planes[:, :, half(h)])
-        for h in range(2):
-            nc.sync.dma_start(wv_raw[h][:], wv_planes[:, :, half(h)])
+        nc.sync.dma_start(y_sb[:], y_planes)
+        nc.sync.dma_start(wv_raw[:], wv_planes)
 
         identity = tile("identity", [P, P], F32)
         make_identity(nc, identity[:])
@@ -186,7 +184,7 @@ def tile_attend_gml_wel_kernel(tc, xT, wd, wv, y, cw, rw, offs, out):
 
         def round_wv(first, last, takes_over, engine):
             rounded = tile("wv_bf%d" % first, [P, (last - first) * P * PACK], BF16, takes_over)
-            columns = as_planes(wv_raw[first // 2][:, :, first % 2 * P : ((last - 1) % 2 + 1) * P])
+            columns = as_planes(wv_raw[:, :, first * P : last * P])
             if engine is nc.vector:
                 nc.vector.tensor_copy(as_words(rounded[:]), columns)
             else:
@@ -224,7 +222,7 @@ def tile_attend_gml_wel_kernel(tc, xT, wd, wv, y, cw, rw, offs, out):
                 nc.vector.tensor_tensor(
                     q[h][:, planes(u)],
                     a_banks[h, u][:].rearrange("p (t n) -> p t n", t=PAIR),
-                    y_sb[h][:, planes(u)],
+                    y_sb[:, planes(u), half(h)],
                     ALU.subtract,
                 )
             nc.gpsimd.tensor_tensor(weighted[h][:, planes(0)], q[h][:, planes(0)], weights[h], ALU.mult)

@@ -21,9 +21,8 @@ PACK = 4
 PAIR = 2
 HALF = 256
 GROUP = 16
-CHUNKS = N // P
 RUN = 4
-SCALAR_COLUMNS = 80
+SCALAR_COLUMNS = (24, 40)
 
 
 def tile_attend_gml_wel_kernel(tc, xT, wd, wv, y, cw, rw, offs, out):
@@ -60,24 +59,24 @@ def tile_attend_gml_wel_kernel(tc, xT, wd, wv, y, cw, rw, offs, out):
             return columns.rearrange("p (m j) -> p m j", j=PACK)
 
         offsets = sb.tile([P, N // GROUP], U16, name="offsets")
-        nc.sync.dma_start(offsets[:], offs)
         cw_sb = tile("cw_sb", [P, PACK], F32)
         rw_sb = tile("rw_sb", [P, PACK], F32)
         nc.scalar.dma_start(rw_sb[:], rw[0:1, :].rearrange("o (m j) -> m (o j)", j=PACK))
         nc.scalar.dma_start(cw_sb[:], cw.rearrange("(p t) o -> p (t o)", t=PACK))
         x_planes = xT.rearrange("(p t) n -> p t n", t=PACK)
         x_raw = [tile("x_raw%d" % t, [P, T], F32) for t in range(PACK)]
-        for t in range(PAIR):
+        nc.sync.dma_start(offsets[:], offs)
+        for t in (0, 2, 1, 3):
             nc.sync.dma_start(x_raw[t][:], x_planes[:, t, :])
-            nc.sync.dma_start(x_raw[t + PAIR][:], x_planes[:, t + PAIR, :])
         wv_planes = wv.rearrange("(p t) d -> p t d", t=PACK)
         y_planes = y.rearrange("(p t) n -> p t n", t=PACK)
         wd_raw = tile("wd_raw", [P, PACK, V], F32)
-        wv_raw = tile("wv_raw", [P, PACK, D], F32)
-        y_sb = tile("y_sb", [P, PACK, N], F32)
+        wv_raw = [tile("wv_raw0", [P, PACK, P], F32), tile("wv_raw1", [P, PACK, D - P], F32)]
+        y_sb = [tile("y_sb%d" % u, [P, PAIR, N], F32) for u in range(2)]
         nc.sync.dma_start(wd_raw[:], wd.rearrange("(p j) v -> p j v", j=PACK))
-        nc.sync.dma_start(y_sb[:], y_planes)
-        nc.sync.dma_start(wv_raw[:], wv_planes)
+        for u, columns in enumerate((slice(0, P), slice(P, D))):
+            nc.sync.dma_start(y_sb[u][:], y_planes[:, planes(u), :])
+            nc.sync.dma_start(wv_raw[u][:], wv_planes[:, :, columns])
 
         identity = tile("identity", [P, P], F32)
         make_identity(nc, identity[:])
@@ -88,13 +87,13 @@ def tile_attend_gml_wel_kernel(tc, xT, wd, wv, y, cw, rw, offs, out):
         def rw_entries(entries):
             return rw_bank[:].rearrange("p (j m) -> p m j", j=PACK)[:, entries.start // PACK : entries.stop // PACK, :]
 
-        windows = [tile("window%d" % b, [P, T], F32) for b in range(D // P)]
-        for b, engine in enumerate((nc.vector, nc.vector, nc.vector, nc.gpsimd)):
-            engine.memset(windows[b][:], 0.0)
         g_codes = tile("g_codes", [P, 3 * HALF], U32)
         g_scales = tile("g_scales", [P, 3 * HALF], U8)
         nc.gpsimd.memset(g_codes[:, half(0)], 0)
         nc.gpsimd.memset(g_scales[:, half(0)].bitcast(U32), 0)
+        windows = [tile("window%d" % b, [P, T], F32) for b in range(D // P)]
+        for b, engine in enumerate((nc.vector, nc.vector, nc.vector, nc.gpsimd)):
+            engine.memset(windows[b][:], 0.0)
 
         x_cast = [tile("x_cast%d" % t, [P, T], BF16) for t in range(PAIR)]
         x_bf = tile("x_bf", [P, N, PACK], BF16)
@@ -111,15 +110,13 @@ def tile_attend_gml_wel_kernel(tc, xT, wd, wv, y, cw, rw, offs, out):
         gather(1, HALF, N)
 
         weighted = [tile("wq%d" % h, [P, PACK, HALF], F32) for h in range(2)]
-        weights = [weighted[0][:, planes(1)]]
-
-        def spread_weights(h):
+        weights = [weighted[0][:, planes(1)], tile("weights", [P, PAIR, HALF], F32)[:]]
+        for h in range(2):
             for t in range(PAIR):
+                plane = PAIR * h + t
                 nc.scalar.activation(
-                    in_fours(weights[h][:, t]), rw_entries(half(h)), ACT.Copy, scale=cw_sb[:, t : t + 1]
+                    in_fours(weights[h][:, t]), rw_entries(half(h)), ACT.Copy, scale=cw_sb[:, plane : plane + 1]
                 )
-
-        spread_weights(0)
 
         x_scales = tile("x_scales", [P, N], U8)
         wd_bf = [tile("wd_bf%d" % u, [P, PAIR, P, PACK], BF16) for u in range(2)]
@@ -135,11 +132,9 @@ def tile_attend_gml_wel_kernel(tc, xT, wd, wv, y, cw, rw, offs, out):
 
         wd_by_plane = wd_raw[:].rearrange("p j (m t) -> p m j t", t=PACK)
         wd_dealt = [wd_bf[u][:].rearrange("p t m j -> p m j t") for u in range(2)]
-        nc.vector.tensor_copy(wd_dealt[0], wd_by_plane[:, :, :, planes(0)])
-        nc.scalar.activation(wd_dealt[1][:, :SCALAR_COLUMNS], wd_by_plane[:, :SCALAR_COLUMNS, :, planes(1)], ACT.Copy)
-        nc.vector.tensor_copy(wd_dealt[1][:, SCALAR_COLUMNS:], wd_by_plane[:, SCALAR_COLUMNS:, :, planes(1)])
-        weights.append(tile("weights", [P, PAIR, HALF], F32, takes_over="wd_raw")[:])
-        spread_weights(1)
+        for u, split in enumerate(SCALAR_COLUMNS):
+            nc.scalar.activation(wd_dealt[u][:, :split], wd_by_plane[:, :split, :, planes(u)], ACT.Copy)
+            nc.vector.tensor_copy(wd_dealt[u][:, split:], wd_by_plane[:, split:, :, planes(u)])
         x_codes = [quantize_x(0)]
         for t in range(PACK):
             nc.vector.quantize_mx(
@@ -150,12 +145,13 @@ def tile_attend_gml_wel_kernel(tc, xT, wd, wv, y, cw, rw, offs, out):
         x_codes.append(quantize_x(1, takes_over="wd_bf0"))
 
         a_banks = {}
+        first_bank = bank("a_first")
         for h in range(2):
-            for u in range(2):
+            for u in (h, 1 - h):
                 a_banks[h, u] = bank("a%d%d" % (h, u))
                 for t in range(PAIR * u, PAIR * (u + 1)):
                     nc.tensor.matmul_mx(
-                        a_banks[h, u][:, half(t % PAIR)],
+                        (first_bank if (h, t) == (0, 0) else a_banks[h, u])[:, half(t % PAIR)],
                         lhsT=wd_codes[:, block(t)].bitcast(E4M3),
                         lhsT_scale=wd_scales[:, block(t)],
                         rhs=x_codes[h][:].bitcast(E4M3),
@@ -164,10 +160,9 @@ def tile_attend_gml_wel_kernel(tc, xT, wd, wv, y, cw, rw, offs, out):
                         stop=True,
                     )
 
-        q = [tile("q%d" % h, [P, PACK, HALF], F32) for h in range(2)]
-        squared = {(h, u): tile("sq%d%d" % (h, u), [P, PAIR, HALF], F32) for h in range(2) for u in range(2)}
-        decay = [tile("e%d" % h, [P, PACK, HALF], F32) for h in range(2)]
-        g_words = [tile("g%d" % h, [P, HALF * PACK], BF16) for h in range(2)]
+        q = {(h, u): tile("q%d%d" % (h, u), [P, PAIR, HALF], F32)[:] for h, u in ((0, 0), (0, 1), (1, 1))}
+        q[1, 0] = y_sb[1][:, :, half(0)]
+        decay = [tile("e%d" % h, [P, 2, PACK, P], F32) for h in range(2)]
         wv_scales = tile("wv_scales", [P, D], U8)
         wv_codes = tile("wv_codes", [P, D], U32)
 
@@ -175,20 +170,15 @@ def tile_attend_gml_wel_kernel(tc, xT, wd, wv, y, cw, rw, offs, out):
             nc.vector.tensor_tensor(
                 as_words(g_words[h][:, chunk_words(c)]),
                 as_planes(weighted[h][:, :, block(c)]),
-                as_planes(decay[h][:, :, block(c)]),
+                as_planes(decay[h][:, c]),
                 ALU.mult,
             )
 
         def quantize_g(h):
             nc.vector.quantize_mx(g_codes[:, half(h + 1)].bitcast(E5M2), g_scales[:, half(h + 1)], g_words[h][:])
 
-        def round_wv(first, last, takes_over, engine):
-            rounded = tile("wv_bf%d" % first, [P, (last - first) * P * PACK], BF16, takes_over)
-            columns = as_planes(wv_raw[:, :, first * P : last * P])
-            if engine is nc.vector:
-                nc.vector.tensor_copy(as_words(rounded[:]), columns)
-            else:
-                nc.scalar.activation(as_words(rounded[:]), columns, ACT.Copy)
+        def round_wv(columns, rounded):
+            nc.scalar.activation(as_words(rounded), as_planes(columns), ACT.Copy)
             return rounded
 
         def quantize_wv(first, last, words):
@@ -217,46 +207,71 @@ def tile_attend_gml_wel_kernel(tc, xT, wd, wv, y, cw, rw, offs, out):
             listed = offsets[:, entries.start // GROUP : entries.stop // GROUP]
             nc.vector.tensor_copy(windows[b][:].indirect(listed), staged)
 
+        wv_first = round_wv(wv_raw[0][:], weighted[0][:, 0].bitcast(BF16))
+        squared = {(h, u): tile("sq%d%d" % (h, u), [P, PAIR, HALF], F32) for h, u in ((0, 1), (1, 0), (1, 1))}
+        squared[0, 0] = tile("sq00", [P, PAIR, HALF], F32, takes_over="wv_raw0")
         for h in range(2):
-            for u in range(2):
+            for u in (h, 1 - h):
+                if (h, u) == (0, 0):
+                    for t, sums in enumerate((first_bank, a_banks[h, u])):
+                        nc.vector.tensor_tensor(q[h, u][:, t], sums[:, half(t)], y_sb[u][:, t, half(h)], ALU.subtract)
+                    quantize_wv(0, 1, wv_first)
+                    continue
                 nc.vector.tensor_tensor(
-                    q[h][:, planes(u)],
+                    q[h, u],
                     a_banks[h, u][:].rearrange("p (t n) -> p t n", t=PAIR),
-                    y_sb[:, planes(u), half(h)],
+                    y_sb[u][:, :, half(h)],
                     ALU.subtract,
                 )
-            nc.gpsimd.tensor_tensor(weighted[h][:, planes(0)], q[h][:, planes(0)], weights[h], ALU.mult)
+            nc.gpsimd.tensor_tensor(weighted[h][:, planes(h)], q[h, h], weights[h], ALU.mult)
         for h in range(2):
-            for u in range(2):
-                nc.scalar.activation(squared[h, u][:], q[h][:, planes(u)], ACT.Square)
-            for u in range(2):
-                nc.scalar.activation(decay[h][:, planes(u)], squared[h, u][:], ACT.Exp, scale=-0.5)
+            if h == 0:
+                for t in range(PAIR):
+                    nc.scalar.activation(squared[0, 0][:, t], q[0, 0][:, t], ACT.Square)
+                for t in range(PAIR):
+                    nc.scalar.activation(
+                        decay[0][:, :, t], squared[0, 0][:, t].rearrange("p (c i) -> p c i", c=2), ACT.Exp, scale=-0.5
+                    )
+            pairs = (1, 0) if h else (1,)
+            for u in pairs:
+                nc.scalar.activation(squared[h, u][:], q[h, u], ACT.Square)
+            for u in pairs:
+                nc.scalar.activation(
+                    decay[h][:, :, planes(u)],
+                    squared[h, u][:].rearrange("p t (c i) -> p c t i", c=2),
+                    ACT.Exp,
+                    scale=-0.5,
+                )
         for h in range(2):
-            for t in range(PAIR, PACK):
+            for t in range(PAIR * (1 - h), PAIR * (2 - h)):
                 nc.vector.scalar_tensor_tensor(
                     in_fours(weighted[h][:, t]),
-                    in_fours(q[h][:, t]),
+                    in_fours(q[h, 1 - h][:, t % PAIR]),
                     cw_sb[:, t : t + 1],
                     rw_entries(half(h)),
                     ALU.mult,
                     ALU.mult,
                 )
-        wv_first = round_wv(0, 1, "wd_raw", nc.vector)
+        g_words = [tile("g0", [P, HALF * PACK], BF16), tile("g1", [P, HALF * PACK], BF16)]
         for c in range(2):
             gradient(0, c)
-        quantize_wv(0, 1, wv_first[:])
-        quantize_g(0)
+        for c in range(2):
+            columns = slice(HALF + c * P, HALF + (c + 1) * P)
+            nc.vector.quantize_mx(g_codes[:, columns].bitcast(E5M2), g_scales[:, columns], g_words[0][:, chunk_words(c)])
         early_sums = second_product(0, 0, "early")[:, half(1)]
-        wv_second = round_wv(1, 2, "sq10", nc.scalar)
+        wv_second = round_wv(wv_raw[1][:, :, :P], tile("wv_bf1", [P, P * PACK], BF16, "sq10")[:])
         for c in range(2):
             gradient(1, c)
-        quantize_wv(1, 2, wv_second[:])
+        quantize_wv(1, 2, wv_second)
         quantize_g(1)
-        scatter(0, stage(early_sums, decay[1][:, 0]), half(0))
-        wv_rest = round_wv(2, 4, "sq11", nc.scalar)
+        early = decay[1][:].rearrange("p c t i -> p (c t i)")[:, N + GROUP - HALF : N + GROUP]
+        for columns in (slice(0, HALF - GROUP), slice(HALF - GROUP, HALF)):
+            stage(early_sums[:, columns], early[:, columns])
+        scatter(0, early, half(0))
+        wv_rest = round_wv(wv_raw[1][:, :, P:], tile("wv_bf2", [P, HALF * PACK], BF16, "sq10")[:])
         for b, entries in ((1, slice(0, N)), (0, half(1)), (2, slice(0, N)), (3, slice(0, N))):
             if b == 2:
-                quantize_wv(2, 4, wv_rest[:])
+                quantize_wv(2, 4, wv_rest)
             sums = second_product(b, HALF, "late%d" % b, "a%d%d" % (b // 2, b % 2))[:, entries]
             scatter(b, stage(sums, tile("dx_late%d" % b, [P, entries.stop - entries.start], F32)[:]), entries)
             nc.sync.dma_start(out[block(b), :], windows[b][:])

@@ -71,12 +71,12 @@ def tile_attend_gml_wel_kernel(tc, xT, wd, wv, y, cw, rw, offs, out):
         wv_planes = wv.rearrange("(p t) d -> p t d", t=PACK)
         y_planes = y.rearrange("(p t) n -> p t n", t=PACK)
         wd_raw = tile("wd_raw", [P, PACK, V], F32)
-        wv_raw = [tile("wv_raw0", [P, PACK, P], F32), tile("wv_raw1", [P, PACK, D - P], F32)]
+        wv_raw = tile("wv_raw", [P, PACK, D], F32)
         y_sb = [tile("y_sb%d" % u, [P, PAIR, N], F32) for u in range(2)]
         nc.sync.dma_start(wd_raw[:], wd.rearrange("(p j) v -> p j v", j=PACK))
-        for u, columns in enumerate((slice(0, P), slice(P, D))):
+        for u in range(2):
             nc.sync.dma_start(y_sb[u][:], y_planes[:, planes(u), :])
-            nc.sync.dma_start(wv_raw[u][:], wv_planes[:, :, columns])
+        nc.sync.dma_start(wv_raw[:], wv_planes)
 
         identity = tile("identity", [P, P], F32)
         make_identity(nc, identity[:])
@@ -109,8 +109,7 @@ def tile_attend_gml_wel_kernel(tc, xT, wd, wv, y, cw, rw, offs, out):
         gather(1, 0, HALF)
         gather(1, HALF, N)
 
-        weighted = [tile("wq%d" % h, [P, PACK, HALF], F32) for h in range(2)]
-        weights = [weighted[0][:, planes(1)], tile("weights", [P, PAIR, HALF], F32)[:]]
+        weights = [tile("weights%d" % h, [P, PAIR, HALF], F32)[:] for h in range(2)]
         for h in range(2):
             for t in range(PAIR):
                 plane = PAIR * h + t
@@ -143,6 +142,7 @@ def tile_attend_gml_wel_kernel(tc, xT, wd, wv, y, cw, rw, offs, out):
                 wd_bf[t // PAIR][:, t % PAIR].rearrange("p m j -> p (m j)"),
             )
         x_codes.append(quantize_x(1, takes_over="wd_bf0"))
+        weighted = [tile("wq%d" % h, [P, PACK, HALF], F32) for h in range(2)]
 
         a_banks = {}
         first_bank = bank("a_first")
@@ -160,7 +160,8 @@ def tile_attend_gml_wel_kernel(tc, xT, wd, wv, y, cw, rw, offs, out):
                         stop=True,
                     )
 
-        q = {(h, u): tile("q%d%d" % (h, u), [P, PAIR, HALF], F32)[:] for h, u in ((0, 0), (0, 1), (1, 1))}
+        q = {(h, u): tile("q%d%d" % (h, u), [P, PAIR, HALF], F32)[:] for h, u in ((0, 1), (1, 1))}
+        q[0, 0] = tile("q00", [P, PAIR, HALF], F32, takes_over="wd_bf1")[:]
         q[1, 0] = y_sb[1][:, :, half(0)]
         decay = [tile("e%d" % h, [P, 2, PACK, P], F32) for h in range(2)]
         wv_scales = tile("wv_scales", [P, D], U8)
@@ -207,15 +208,12 @@ def tile_attend_gml_wel_kernel(tc, xT, wd, wv, y, cw, rw, offs, out):
             listed = offsets[:, entries.start // GROUP : entries.stop // GROUP]
             nc.vector.tensor_copy(windows[b][:].indirect(listed), staged)
 
-        wv_first = round_wv(wv_raw[0][:], weighted[0][:, 0].bitcast(BF16))
-        squared = {(h, u): tile("sq%d%d" % (h, u), [P, PAIR, HALF], F32) for h, u in ((0, 1), (1, 0), (1, 1))}
-        squared[0, 0] = tile("sq00", [P, PAIR, HALF], F32, takes_over="wv_raw0")
+        squared = {(h, u): tile("sq%d%d" % (h, u), [P, PAIR, HALF], F32) for h in range(2) for u in range(2)}
         for h in range(2):
             for u in (h, 1 - h):
                 if (h, u) == (0, 0):
                     for t, sums in enumerate((first_bank, a_banks[h, u])):
                         nc.vector.tensor_tensor(q[h, u][:, t], sums[:, half(t)], y_sb[u][:, t, half(h)], ALU.subtract)
-                    quantize_wv(0, 1, wv_first)
                     continue
                 nc.vector.tensor_tensor(
                     q[h, u],
@@ -252,14 +250,16 @@ def tile_attend_gml_wel_kernel(tc, xT, wd, wv, y, cw, rw, offs, out):
                     ALU.mult,
                     ALU.mult,
                 )
-        g_words = [tile("g0", [P, HALF * PACK], BF16), tile("g1", [P, HALF * PACK], BF16)]
+        wv_first = tile("wv_bf0", [P, P * PACK], BF16)
+        nc.vector.tensor_copy(as_words(wv_first[:]), as_planes(wv_raw[:, :, :P]))
+        g_words = [tile("g0", [P, HALF * PACK], BF16)]
         for c in range(2):
             gradient(0, c)
-        for c in range(2):
-            columns = slice(HALF + c * P, HALF + (c + 1) * P)
-            nc.vector.quantize_mx(g_codes[:, columns].bitcast(E5M2), g_scales[:, columns], g_words[0][:, chunk_words(c)])
+        quantize_wv(0, 1, wv_first[:])
+        quantize_g(0)
+        g_words.append(tile("g1", [P, HALF * PACK], BF16, takes_over="wv_bf0"))
         early_sums = second_product(0, 0, "early")[:, half(1)]
-        wv_second = round_wv(wv_raw[1][:, :, :P], tile("wv_bf1", [P, P * PACK], BF16, "sq10")[:])
+        wv_second = round_wv(wv_raw[:, :, block(1)], tile("wv_bf1", [P, P * PACK], BF16, "sq10")[:])
         for c in range(2):
             gradient(1, c)
         quantize_wv(1, 2, wv_second)
@@ -268,7 +268,7 @@ def tile_attend_gml_wel_kernel(tc, xT, wd, wv, y, cw, rw, offs, out):
         for columns in (slice(0, HALF - GROUP), slice(HALF - GROUP, HALF)):
             stage(early_sums[:, columns], early[:, columns])
         scatter(0, early, half(0))
-        wv_rest = round_wv(wv_raw[1][:, :, P:], tile("wv_bf2", [P, HALF * PACK], BF16, "sq10")[:])
+        wv_rest = round_wv(wv_raw[:, :, half(1)], tile("wv_bf2", [P, HALF * PACK], BF16, "sq10")[:])
         for b, entries in ((1, slice(0, N)), (0, half(1)), (2, slice(0, N)), (3, slice(0, N))):
             if b == 2:
                 quantize_wv(2, 4, wv_rest)

@@ -22,7 +22,7 @@ PAIR = 2
 HALF = 256
 GROUP = 16
 RUN = 4
-SCALAR_COLUMNS = (24, 40)
+SCALAR_COLUMNS = 80
 
 
 def tile_attend_gml_wel_kernel(tc, xT, wd, wv, y, cw, rw, offs, out):
@@ -109,13 +109,16 @@ def tile_attend_gml_wel_kernel(tc, xT, wd, wv, y, cw, rw, offs, out):
         gather(1, 0, HALF)
         gather(1, HALF, N)
 
-        weights = [tile("weights%d" % h, [P, PAIR, HALF], F32)[:] for h in range(2)]
-        for h in range(2):
+        weights = [tile("weights0", [P, PAIR, HALF], F32)[:]]
+
+        def spread_weights(h):
             for t in range(PAIR):
                 plane = PAIR * h + t
                 nc.scalar.activation(
                     in_fours(weights[h][:, t]), rw_entries(half(h)), ACT.Copy, scale=cw_sb[:, plane : plane + 1]
                 )
+
+        spread_weights(0)
 
         x_scales = tile("x_scales", [P, N], U8)
         wd_bf = [tile("wd_bf%d" % u, [P, PAIR, P, PACK], BF16) for u in range(2)]
@@ -131,9 +134,11 @@ def tile_attend_gml_wel_kernel(tc, xT, wd, wv, y, cw, rw, offs, out):
 
         wd_by_plane = wd_raw[:].rearrange("p j (m t) -> p m j t", t=PACK)
         wd_dealt = [wd_bf[u][:].rearrange("p t m j -> p m j t") for u in range(2)]
-        for u, split in enumerate(SCALAR_COLUMNS):
-            nc.scalar.activation(wd_dealt[u][:, :split], wd_by_plane[:, :split, :, planes(u)], ACT.Copy)
-            nc.vector.tensor_copy(wd_dealt[u][:, split:], wd_by_plane[:, split:, :, planes(u)])
+        nc.vector.tensor_copy(wd_dealt[0], wd_by_plane[:, :, :, planes(0)])
+        nc.scalar.activation(wd_dealt[1][:, :SCALAR_COLUMNS], wd_by_plane[:, :SCALAR_COLUMNS, :, planes(1)], ACT.Copy)
+        nc.vector.tensor_copy(wd_dealt[1][:, SCALAR_COLUMNS:], wd_by_plane[:, SCALAR_COLUMNS:, :, planes(1)])
+        weights.append(tile("weights1", [P, PAIR, HALF], F32, takes_over="wd_raw")[:])
+        spread_weights(1)
         x_codes = [quantize_x(0)]
         for t in range(PACK):
             nc.vector.quantize_mx(

@@ -22,7 +22,7 @@ PAIR = 2
 HALF = 256
 GROUP = 16
 RUN = 4
-SCALAR_COLUMNS = 80
+SCALAR_COLUMNS = 64
 
 
 def tile_attend_gml_wel_kernel(tc, xT, wd, wv, y, cw, rw, offs, out):
@@ -91,9 +91,8 @@ def tile_attend_gml_wel_kernel(tc, xT, wd, wv, y, cw, rw, offs, out):
         g_scales = tile("g_scales", [P, 3 * HALF], U8)
         nc.gpsimd.memset(g_codes[:, half(0)], 0)
         nc.gpsimd.memset(g_scales[:, half(0)].bitcast(U32), 0)
-        windows = [tile("window%d" % b, [P, T], F32) for b in range(D // P)]
-        for b, engine in enumerate((nc.vector, nc.vector, nc.vector, nc.gpsimd)):
-            engine.memset(windows[b][:], 0.0)
+        windows = [tile("window0", [P, T], F32)]
+        nc.vector.memset(windows[0][:], 0.0)
 
         x_cast = [tile("x_cast%d" % t, [P, T], BF16) for t in range(PAIR)]
         x_bf = tile("x_bf", [P, N, PACK], BF16)
@@ -109,7 +108,7 @@ def tile_attend_gml_wel_kernel(tc, xT, wd, wv, y, cw, rw, offs, out):
         gather(1, 0, HALF)
         gather(1, HALF, N)
 
-        weights = [tile("weights0", [P, PAIR, HALF], F32)[:]]
+        weights = [wd_raw[:, planes(h), : SCALAR_COLUMNS * PACK] for h in range(2)]
 
         def spread_weights(h):
             for t in range(PAIR):
@@ -117,8 +116,6 @@ def tile_attend_gml_wel_kernel(tc, xT, wd, wv, y, cw, rw, offs, out):
                 nc.scalar.activation(
                     in_fours(weights[h][:, t]), rw_entries(half(h)), ACT.Copy, scale=cw_sb[:, plane : plane + 1]
                 )
-
-        spread_weights(0)
 
         x_scales = tile("x_scales", [P, N], U8)
         wd_bf = [tile("wd_bf%d" % u, [P, PAIR, P, PACK], BF16) for u in range(2)]
@@ -137,8 +134,8 @@ def tile_attend_gml_wel_kernel(tc, xT, wd, wv, y, cw, rw, offs, out):
         nc.vector.tensor_copy(wd_dealt[0], wd_by_plane[:, :, :, planes(0)])
         nc.scalar.activation(wd_dealt[1][:, :SCALAR_COLUMNS], wd_by_plane[:, :SCALAR_COLUMNS, :, planes(1)], ACT.Copy)
         nc.vector.tensor_copy(wd_dealt[1][:, SCALAR_COLUMNS:], wd_by_plane[:, SCALAR_COLUMNS:, :, planes(1)])
-        weights.append(tile("weights1", [P, PAIR, HALF], F32, takes_over="wd_raw")[:])
-        spread_weights(1)
+        for h in range(2):
+            spread_weights(h)
         x_codes = [quantize_x(0)]
         for t in range(PACK):
             nc.vector.quantize_mx(
@@ -277,6 +274,9 @@ def tile_attend_gml_wel_kernel(tc, xT, wd, wv, y, cw, rw, offs, out):
         for b, entries in ((1, slice(0, N)), (0, half(1)), (2, slice(0, N)), (3, slice(0, N))):
             if b == 2:
                 quantize_wv(2, 4, wv_rest)
+            if b > 0:
+                windows.append(tile("window%d" % b, [P, T], F32, ("wv_bf0", "sq10", "dx_late1")[b - 1]))
+                nc.gpsimd.memset(windows[b][:], 0.0)
             sums = second_product(b, HALF, "late%d" % b, "a%d%d" % (b // 2, b % 2))[:, entries]
             scatter(b, stage(sums, tile("dx_late%d" % b, [P, entries.stop - entries.start], F32)[:]), entries)
             nc.sync.dma_start(out[block(b), :], windows[b][:])

@@ -23,6 +23,7 @@ HALF = 256
 GROUP = 16
 RUN = 4
 SCALAR_COLUMNS = 64
+SCALAR_ENTRIES = 96
 
 
 def tile_attend_gml_wel_kernel(tc, xT, wd, wv, y, cw, rw, offs, out):
@@ -95,18 +96,21 @@ def tile_attend_gml_wel_kernel(tc, xT, wd, wv, y, cw, rw, offs, out):
         nc.vector.memset(windows[0][:], 0.0)
 
         x_cast = [tile("x_cast%d" % t, [P, T], BF16) for t in range(PAIR)]
-        x_bf = tile("x_bf", [P, N, PACK], BF16)
+        gathered = [tile("gathered%d" % h, [P, PACK, HALF], BF16) for h in range(2)]
+        x_bf = [tile("x_bf%d" % h, [P, HALF * PACK], BF16) for h in range(2)]
+        for t in range(PAIR):
+            nc.vector.tensor_copy(x_cast[t][:], x_raw[t][:])
+            for h in range(2):
+                listed = offsets[:, h * HALF // GROUP : (h + 1) * HALF // GROUP]
+                nc.scalar.activation(gathered[h][:, t], x_cast[t][:].indirect(listed), ACT.Copy)
+                nc.vector.tensor_copy(gathered[h][:, t + PAIR], x_raw[t + PAIR][:].indirect(listed))
 
-        def gather(t, first, last):
-            listed = offsets[:, first // GROUP : last // GROUP]
-            nc.scalar.activation(x_bf[:, first:last, t], x_cast[t][:].indirect(listed), ACT.Copy)
-            nc.vector.tensor_copy(x_bf[:, first:last, t + PAIR], x_raw[t + PAIR][:].indirect(listed))
+        def weave(h, first, last):
+            return as_words(x_bf[h][:, first * PACK : last * PACK]), as_planes(gathered[h][:, :, first:last])
 
-        nc.vector.tensor_copy(x_cast[0][:], x_raw[0][:])
-        gather(0, 0, N)
-        nc.vector.tensor_copy(x_cast[1][:], x_raw[1][:])
-        gather(1, 0, HALF)
-        gather(1, HALF, N)
+        nc.scalar.activation(*weave(0, 0, SCALAR_ENTRIES), ACT.Copy)
+        nc.vector.tensor_copy(*weave(0, SCALAR_ENTRIES, HALF))
+        nc.scalar.activation(*weave(1, 0, HALF), ACT.Copy)
 
         weights = [wd_raw[:, planes(h), : SCALAR_COLUMNS * PACK] for h in range(2)]
 
@@ -125,7 +129,7 @@ def tile_attend_gml_wel_kernel(tc, xT, wd, wv, y, cw, rw, offs, out):
         def quantize_x(h, takes_over=None):
             codes = tile("x_codes%d" % h, [P, HALF], U32, takes_over)
             nc.vector.quantize_mx(
-                codes[:].bitcast(E4M3), x_scales[:, half(h)], x_bf[:, half(h), :].rearrange("p n t -> p (n t)")
+                codes[:].bitcast(E4M3), x_scales[:, half(h)], x_bf[h][:]
             )
             return codes
 

@@ -24,6 +24,7 @@ GROUP = 16
 RUN = 4
 SCALAR_COLUMNS = 64
 SCALAR_ENTRIES = 96
+SCALAR_POSITIONS = 320
 
 
 def tile_attend_gml_wel_kernel(tc, xT, wd, wv, y, cw, rw, offs, out):
@@ -62,12 +63,13 @@ def tile_attend_gml_wel_kernel(tc, xT, wd, wv, y, cw, rw, offs, out):
         offsets = sb.tile([P, N // GROUP], U16, name="offsets")
         cw_sb = tile("cw_sb", [P, PACK], F32)
         rw_sb = tile("rw_sb", [P, PACK], F32)
-        nc.scalar.dma_start(rw_sb[:], rw[0:1, :].rearrange("o (m j) -> m (o j)", j=PACK))
-        nc.scalar.dma_start(cw_sb[:], cw.rearrange("(p t) o -> p (t o)", t=PACK))
         x_planes = xT.rearrange("(p t) n -> p t n", t=PACK)
         x_raw = [tile("x_raw%d" % t, [P, T], F32) for t in range(PACK)]
+        nc.sync.dma_start(x_raw[0][:], x_planes[:, 0, :])
         nc.sync.dma_start(offsets[:], offs)
-        for t in (0, 2, 1, 3):
+        nc.sync.dma_start(rw_sb[:], rw[0:1, :].rearrange("o (m j) -> m (o j)", j=PACK))
+        nc.sync.dma_start(cw_sb[:], cw.rearrange("(p t) o -> p (t o)", t=PACK))
+        for t in (2, 1, 3):
             nc.sync.dma_start(x_raw[t][:], x_planes[:, t, :])
         wv_planes = wv.rearrange("(p t) d -> p t d", t=PACK)
         y_planes = y.rearrange("(p t) n -> p t n", t=PACK)
@@ -99,7 +101,8 @@ def tile_attend_gml_wel_kernel(tc, xT, wd, wv, y, cw, rw, offs, out):
         gathered = [tile("gathered%d" % h, [P, PACK, HALF], BF16) for h in range(2)]
         x_bf = [tile("x_bf%d" % h, [P, HALF * PACK], BF16) for h in range(2)]
         for t in range(PAIR):
-            nc.vector.tensor_copy(x_cast[t][:], x_raw[t][:])
+            nc.scalar.activation(x_cast[t][:, :SCALAR_POSITIONS], x_raw[t][:, :SCALAR_POSITIONS], ACT.Copy)
+            nc.vector.tensor_copy(x_cast[t][:, SCALAR_POSITIONS:], x_raw[t][:, SCALAR_POSITIONS:])
             for h in range(2):
                 listed = offsets[:, h * HALF // GROUP : (h + 1) * HALF // GROUP]
                 nc.scalar.activation(gathered[h][:, t], x_cast[t][:].indirect(listed), ACT.Copy)

@@ -67,8 +67,6 @@ def tile_attend_gml_wel_kernel(tc, xT, wd, wv, y, cw, rw, offs, out):
         x_raw = [tile("x_raw%d" % t, [P, T], F32) for t in range(PACK)]
         nc.sync.dma_start(x_raw[0][:], x_planes[:, 0, :])
         nc.sync.dma_start(offsets[:], offs)
-        nc.sync.dma_start(rw_sb[:], rw[0:1, :].rearrange("o (m j) -> m (o j)", j=PACK))
-        nc.sync.dma_start(cw_sb[:], cw.rearrange("(p t) o -> p (t o)", t=PACK))
         for t in (2, 1, 3):
             nc.sync.dma_start(x_raw[t][:], x_planes[:, t, :])
         wv_planes = wv.rearrange("(p t) d -> p t d", t=PACK)
@@ -77,6 +75,8 @@ def tile_attend_gml_wel_kernel(tc, xT, wd, wv, y, cw, rw, offs, out):
         wv_raw = tile("wv_raw", [P, PACK, D], F32)
         y_sb = [tile("y_sb%d" % u, [P, PAIR, N], F32) for u in range(2)]
         nc.sync.dma_start(wd_raw[:], wd.rearrange("(p j) v -> p j v", j=PACK))
+        nc.sync.dma_start(rw_sb[:], rw[0:1, :].rearrange("o (m j) -> m (o j)", j=PACK))
+        nc.sync.dma_start(cw_sb[:], cw.rearrange("(p t) o -> p (t o)", t=PACK))
         for u in range(2):
             nc.sync.dma_start(y_sb[u][:], y_planes[:, planes(u), :])
         nc.sync.dma_start(wv_raw[:], wv_planes)

@@ -272,17 +272,21 @@ def tile_attend_gml_wel_kernel(tc, xT, wd, wv, y, cw, rw, offs, out):
         for c in range(2):
             gradient(1, c)
         quantize_wv(1, 2, wv_second)
+        second_sums = second_product(1, 0, "early_second")[:, half(1)]
         quantize_g(1)
         early = decay[1][:].rearrange("p c t i -> p (c t i)")[:, N + GROUP - HALF : N + GROUP]
         for columns in (slice(0, HALF - GROUP), slice(HALF - GROUP, HALF)):
             stage(early_sums[:, columns], early[:, columns])
         scatter(0, early, half(0))
+        windows.append(tile("window1", [P, T], F32, "wv_bf0"))
+        nc.gpsimd.memset(windows[1][:], 0.0)
+        scatter(1, stage(second_sums, tile("dx_early1", [P, HALF], F32)[:]), half(0))
         wv_rest = round_wv(wv_raw[:, :, half(1)], tile("wv_bf2", [P, HALF * PACK], BF16, "sq10")[:])
-        for b, entries in ((1, slice(0, N)), (0, half(1)), (2, slice(0, N)), (3, slice(0, N))):
+        for b, entries in ((0, half(1)), (1, half(1)), (2, slice(0, N)), (3, slice(0, N))):
             if b == 2:
                 quantize_wv(2, 4, wv_rest)
-            if b > 0:
-                windows.append(tile("window%d" % b, [P, T], F32, ("wv_bf0", "sq10", "dx_late1")[b - 1]))
+            if b > 1:
+                windows.append(tile("window%d" % b, [P, T], F32, ("sq10", "dx_late1")[b - 2]))
                 nc.gpsimd.memset(windows[b][:], 0.0)
             sums = second_product(b, HALF, "late%d" % b, "a%d%d" % (b // 2, b % 2))[:, entries]
             scatter(b, stage(sums, tile("dx_late%d" % b, [P, entries.stop - entries.start], F32)[:]), entries)

@@ -25,6 +25,7 @@ RUN = 4
 SCALAR_COLUMNS = 64
 SCALAR_ENTRIES = 96
 SCALAR_POSITIONS = 320
+SCALAR_WV = 64
 
 
 def tile_attend_gml_wel_kernel(tc, xT, wd, wv, y, cw, rw, offs, out):
@@ -94,8 +95,9 @@ def tile_attend_gml_wel_kernel(tc, xT, wd, wv, y, cw, rw, offs, out):
         g_scales = tile("g_scales", [P, 3 * HALF], U8)
         nc.gpsimd.memset(g_codes[:, half(0)], 0)
         nc.gpsimd.memset(g_scales[:, half(0)].bitcast(U32), 0)
-        windows = [tile("window0", [P, T], F32)]
-        nc.vector.memset(windows[0][:], 0.0)
+        windows = [tile("window%d" % b, [P, T], F32) for b in range(2)]
+        for window in windows:
+            nc.vector.memset(window[:], 0.0)
 
         x_cast = [tile("x_cast%d" % t, [P, T], BF16) for t in range(PAIR)]
         gathered = [tile("gathered%d" % h, [P, PACK, HALF], BF16) for h in range(2)]
@@ -217,7 +219,8 @@ def tile_attend_gml_wel_kernel(tc, xT, wd, wv, y, cw, rw, offs, out):
             listed = offsets[:, entries.start // GROUP : entries.stop // GROUP]
             nc.vector.tensor_copy(windows[b][:].indirect(listed), staged)
 
-        squared = {(h, u): tile("sq%d%d" % (h, u), [P, PAIR, HALF], F32) for h in range(2) for u in range(2)}
+        squared = {(0, u): tile("sq0%d" % u, [P, PAIR, HALF], F32) for u in range(2)}
+        late_squared = tile("sq10", [P, PACK, HALF], F32)
         for h in range(2):
             for u in (h, 1 - h):
                 if (h, u) == (0, 0):
@@ -239,16 +242,20 @@ def tile_attend_gml_wel_kernel(tc, xT, wd, wv, y, cw, rw, offs, out):
                     nc.scalar.activation(
                         decay[0][:, :, t], squared[0, 0][:, t].rearrange("p (c i) -> p c i", c=2), ACT.Exp, scale=-0.5
                     )
-            pairs = (1, 0) if h else (1,)
-            for u in pairs:
-                nc.scalar.activation(squared[h, u][:], q[h, u], ACT.Square)
-            for u in pairs:
+                nc.scalar.activation(squared[0, 1][:], q[0, 1], ACT.Square)
                 nc.scalar.activation(
-                    decay[h][:, :, planes(u)],
-                    squared[h, u][:].rearrange("p t (c i) -> p c t i", c=2),
+                    decay[0][:, :, planes(1)],
+                    squared[0, 1][:].rearrange("p t (c i) -> p c t i", c=2),
                     ACT.Exp,
                     scale=-0.5,
                 )
+                wv_first = tile("wv_bf0", [P, P * PACK], BF16)
+                round_wv(wv_raw[:, :, :SCALAR_WV], wv_first[:, : SCALAR_WV * PACK])
+                continue
+            for u in (1, 0):
+                nc.scalar.activation(late_squared[:, planes(u)], q[h, u], ACT.Square)
+            for c in range(2):
+                nc.scalar.activation(decay[h][:, c], late_squared[:, :, block(c)], ACT.Exp, scale=-0.5)
         for h in range(2):
             for t in range(PAIR * (1 - h), PAIR * (2 - h)):
                 nc.vector.scalar_tensor_tensor(
@@ -259,8 +266,7 @@ def tile_attend_gml_wel_kernel(tc, xT, wd, wv, y, cw, rw, offs, out):
                     ALU.mult,
                     ALU.mult,
                 )
-        wv_first = tile("wv_bf0", [P, P * PACK], BF16)
-        nc.vector.tensor_copy(as_words(wv_first[:]), as_planes(wv_raw[:, :, :P]))
+        nc.vector.tensor_copy(as_words(wv_first[:, SCALAR_WV * PACK :]), as_planes(wv_raw[:, :, SCALAR_WV:P]))
         g_words = [tile("g0", [P, HALF * PACK], BF16)]
         for c in range(2):
             gradient(0, c)
@@ -278,8 +284,6 @@ def tile_attend_gml_wel_kernel(tc, xT, wd, wv, y, cw, rw, offs, out):
         for columns in (slice(0, HALF - GROUP), slice(HALF - GROUP, HALF)):
             stage(early_sums[:, columns], early[:, columns])
         scatter(0, early, half(0))
-        windows.append(tile("window1", [P, T], F32, "wv_bf0"))
-        nc.gpsimd.memset(windows[1][:], 0.0)
         scatter(1, stage(second_sums, tile("dx_early1", [P, HALF], F32)[:]), half(0))
         wv_rest = round_wv(wv_raw[:, :, half(1)], tile("wv_bf2", [P, HALF * PACK], BF16, "sq10")[:])
         for b, entries in ((0, half(1)), (1, half(1)), (2, slice(0, N)), (3, slice(0, N))):

@@ -22,10 +22,6 @@ PAIR = 2
 HALF = 256
 GROUP = 16
 RUN = 4
-SCALAR_COLUMNS = 64
-SCALAR_ENTRIES = 96
-SCALAR_POSITIONS = 320
-SCALAR_WV = 64
 
 
 def tile_attend_gml_wel_kernel(tc, xT, wd, wv, y, cw, rw, offs, out):
@@ -49,9 +45,6 @@ def tile_attend_gml_wel_kernel(tc, xT, wd, wv, y, cw, rw, offs, out):
         def planes(u):
             return slice(PAIR * u, PAIR * (u + 1))
 
-        def chunk_words(c):
-            return slice(c * P * PACK, (c + 1) * P * PACK)
-
         def as_words(packed):
             return packed.rearrange("p (c i t) -> p c t i", i=RUN, t=PACK)
 
@@ -61,26 +54,27 @@ def tile_attend_gml_wel_kernel(tc, xT, wd, wv, y, cw, rw, offs, out):
         def in_fours(columns):
             return columns.rearrange("p (m j) -> p m j", j=PACK)
 
+        def listed(entries):
+            return offsets[:, entries.start // GROUP : entries.stop // GROUP]
+
         offsets = sb.tile([P, N // GROUP], U16, name="offsets")
         cw_sb = tile("cw_sb", [P, PACK], F32)
         rw_sb = tile("rw_sb", [P, PACK], F32)
         x_planes = xT.rearrange("(p t) n -> p t n", t=PACK)
         x_raw = [tile("x_raw%d" % t, [P, T], F32) for t in range(PACK)]
-        nc.sync.dma_start(x_raw[0][:], x_planes[:, 0, :])
-        nc.sync.dma_start(offsets[:], offs)
-        for t in (2, 1, 3):
-            nc.sync.dma_start(x_raw[t][:], x_planes[:, t, :])
-        wv_planes = wv.rearrange("(p t) d -> p t d", t=PACK)
-        y_planes = y.rearrange("(p t) n -> p t n", t=PACK)
         wd_raw = tile("wd_raw", [P, PACK, V], F32)
         wv_raw = tile("wv_raw", [P, PACK, D], F32)
-        y_sb = [tile("y_sb%d" % u, [P, PAIR, N], F32) for u in range(2)]
+        y_planes = y.rearrange("(p t) n -> p t n", t=PACK)
+        y_sb = [tile("y_sb%d" % h, [P, PACK, HALF], F32) for h in range(2)]
         nc.sync.dma_start(wd_raw[:], wd.rearrange("(p j) v -> p j v", j=PACK))
+        nc.sync.dma_start(offsets[:], offs)
+        for t in range(PACK):
+            nc.sync.dma_start(x_raw[t][:], x_planes[:, t, :])
         nc.sync.dma_start(rw_sb[:], rw[0:1, :].rearrange("o (m j) -> m (o j)", j=PACK))
         nc.sync.dma_start(cw_sb[:], cw.rearrange("(p t) o -> p (t o)", t=PACK))
-        for u in range(2):
-            nc.sync.dma_start(y_sb[u][:], y_planes[:, planes(u), :])
-        nc.sync.dma_start(wv_raw[:], wv_planes)
+        nc.sync.dma_start(y_sb[0][:], y_planes[:, :, half(0)])
+        nc.sync.dma_start(y_sb[1][:], y_planes[:, :, half(1)])
+        nc.sync.dma_start(wv_raw[:], wv.rearrange("(p t) d -> p t d", t=PACK))
 
         identity = tile("identity", [P, P], F32)
         make_identity(nc, identity[:])
@@ -91,207 +85,170 @@ def tile_attend_gml_wel_kernel(tc, xT, wd, wv, y, cw, rw, offs, out):
         def rw_entries(entries):
             return rw_bank[:].rearrange("p (j m) -> p m j", j=PACK)[:, entries.start // PACK : entries.stop // PACK, :]
 
-        g_codes = tile("g_codes", [P, 3 * HALF], U32)
-        g_scales = tile("g_scales", [P, 3 * HALF], U8)
-        nc.gpsimd.memset(g_codes[:, half(0)], 0)
-        nc.gpsimd.memset(g_scales[:, half(0)].bitcast(U32), 0)
-        windows = [tile("window%d" % b, [P, T], F32) for b in range(2)]
+        windows = [tile("window%d" % b, [P, T], F32) for b in range(PACK)]
         for window in windows:
-            nc.vector.memset(window[:], 0.0)
+            nc.gpsimd.memset(window[:], 0.0)
 
-        x_cast = [tile("x_cast%d" % t, [P, T], BF16) for t in range(PAIR)]
-        gathered = [tile("gathered%d" % h, [P, PACK, HALF], BF16) for h in range(2)]
-        x_bf = [tile("x_bf%d" % h, [P, HALF * PACK], BF16) for h in range(2)]
-        for t in range(PAIR):
-            nc.scalar.activation(x_cast[t][:, :SCALAR_POSITIONS], x_raw[t][:, :SCALAR_POSITIONS], ACT.Copy)
-            nc.vector.tensor_copy(x_cast[t][:, SCALAR_POSITIONS:], x_raw[t][:, SCALAR_POSITIONS:])
-            for h in range(2):
-                listed = offsets[:, h * HALF // GROUP : (h + 1) * HALF // GROUP]
-                nc.scalar.activation(gathered[h][:, t], x_cast[t][:].indirect(listed), ACT.Copy)
-                nc.vector.tensor_copy(gathered[h][:, t + PAIR], x_raw[t + PAIR][:].indirect(listed))
-
-        def weave(h, first, last):
-            return as_words(x_bf[h][:, first * PACK : last * PACK]), as_planes(gathered[h][:, :, first:last])
-
-        nc.scalar.activation(*weave(0, 0, SCALAR_ENTRIES), ACT.Copy)
-        nc.vector.tensor_copy(*weave(0, SCALAR_ENTRIES, HALF))
-        nc.scalar.activation(*weave(1, 0, HALF), ACT.Copy)
-
-        weights = [wd_raw[:, planes(h), : SCALAR_COLUMNS * PACK] for h in range(2)]
-
-        def spread_weights(h):
-            for t in range(PAIR):
-                plane = PAIR * h + t
-                nc.scalar.activation(
-                    in_fours(weights[h][:, t]), rw_entries(half(h)), ACT.Copy, scale=cw_sb[:, plane : plane + 1]
-                )
-
-        x_scales = tile("x_scales", [P, N], U8)
         wd_bf = [tile("wd_bf%d" % u, [P, PAIR, P, PACK], BF16) for u in range(2)]
         wd_codes = tile("wd_codes", [P, V], U32)
         wd_scales = tile("wd_scales", [P, V], U8)
-
-        def quantize_x(h, takes_over=None):
-            codes = tile("x_codes%d" % h, [P, HALF], U32, takes_over)
-            nc.vector.quantize_mx(
-                codes[:].bitcast(E4M3), x_scales[:, half(h)], x_bf[h][:]
-            )
-            return codes
-
         wd_by_plane = wd_raw[:].rearrange("p j (m t) -> p m j t", t=PACK)
-        wd_dealt = [wd_bf[u][:].rearrange("p t m j -> p m j t") for u in range(2)]
-        nc.vector.tensor_copy(wd_dealt[0], wd_by_plane[:, :, :, planes(0)])
-        nc.scalar.activation(wd_dealt[1][:, :SCALAR_COLUMNS], wd_by_plane[:, :SCALAR_COLUMNS, :, planes(1)], ACT.Copy)
-        nc.vector.tensor_copy(wd_dealt[1][:, SCALAR_COLUMNS:], wd_by_plane[:, SCALAR_COLUMNS:, :, planes(1)])
-        for h in range(2):
-            spread_weights(h)
-        x_codes = [quantize_x(0)]
-        for t in range(PACK):
+        nc.vector.tensor_copy(wd_bf[0][:].rearrange("p t m j -> p m j t"), wd_by_plane[:, :, :, planes(0)])
+        nc.scalar.activation(wd_bf[1][:].rearrange("p t m j -> p m j t"), wd_by_plane[:, :, :, planes(1)], ACT.Copy)
+        for u in range(2):
             nc.vector.quantize_mx(
-                wd_codes[:, block(t)].bitcast(E4M3),
-                wd_scales[:, block(t)],
-                wd_bf[t // PAIR][:, t % PAIR].rearrange("p m j -> p (m j)"),
-            )
-        x_codes.append(quantize_x(1, takes_over="wd_bf0"))
-        weighted = [tile("wq%d" % h, [P, PACK, HALF], F32) for h in range(2)]
-
-        a_banks = {}
-        first_bank = bank("a_first")
-        for h in range(2):
-            for u in (h, 1 - h):
-                a_banks[h, u] = bank("a%d%d" % (h, u))
-                for t in range(PAIR * u, PAIR * (u + 1)):
-                    nc.tensor.matmul_mx(
-                        (first_bank if (h, t) == (0, 0) else a_banks[h, u])[:, half(t % PAIR)],
-                        lhsT=wd_codes[:, block(t)].bitcast(E4M3),
-                        lhsT_scale=wd_scales[:, block(t)],
-                        rhs=x_codes[h][:].bitcast(E4M3),
-                        rhs_scale=x_scales[:, half(h)],
-                        start=True,
-                        stop=True,
-                    )
-
-        q = {(h, u): tile("q%d%d" % (h, u), [P, PAIR, HALF], F32)[:] for h, u in ((0, 1), (1, 1))}
-        q[0, 0] = tile("q00", [P, PAIR, HALF], F32, takes_over="wd_bf1")[:]
-        q[1, 0] = y_sb[1][:, :, half(0)]
-        decay = [tile("e%d" % h, [P, 2, PACK, P], F32) for h in range(2)]
-        wv_scales = tile("wv_scales", [P, D], U8)
-        wv_codes = tile("wv_codes", [P, D], U32)
-
-        def gradient(h, c):
-            nc.vector.tensor_tensor(
-                as_words(g_words[h][:, chunk_words(c)]),
-                as_planes(weighted[h][:, :, block(c)]),
-                as_planes(decay[h][:, c]),
-                ALU.mult,
+                wd_codes[:, half(u)].bitcast(E4M3), wd_scales[:, half(u)], wd_bf[u][:].rearrange("p t m j -> p (t m j)")
             )
 
-        def quantize_g(h):
-            nc.vector.quantize_mx(g_codes[:, half(h + 1)].bitcast(E5M2), g_scales[:, half(h + 1)], g_words[h][:])
+        pieces = [block(0), block(1), half(1)]
+        x_bf = [tile("x_bf%d" % k, [P, (s.stop - s.start) * PACK], BF16) for k, s in enumerate(pieces)]
+        gathered = tile("gathered", [P, PACK, HALF], BF16)
+        for t in range(PACK):
+            for k in range(2):
+                nc.vector.tensor_copy(
+                    x_bf[k][:].rearrange("p (i t) -> p t i", t=PACK)[:, t], x_raw[t][:].indirect(listed(pieces[k]))
+                )
+            nc.scalar.activation(gathered[:, t], x_raw[t][:].indirect(listed(half(1))), ACT.Copy)
+        nc.scalar.activation(as_words(x_bf[2][:]), as_planes(gathered[:]), ACT.Copy)
 
-        def round_wv(columns, rounded):
-            nc.scalar.activation(as_words(rounded), as_planes(columns), ACT.Copy)
-            return rounded
+        x_scales = tile("x_scales", [P, N], U8)
+        x_codes = tile("x_codes", [P, N], U32)
 
-        def quantize_wv(first, last, words):
-            columns = slice(first * P, last * P)
-            nc.vector.quantize_mx(wv_codes[:, columns].bitcast(E4M3), wv_scales[:, columns], words)
-
-        def second_product(b, first, name, takes_over=None):
-            moving = slice(first, first + N)
-            acc = bank(name, takes_over)
+        def first_product(k, acc, t):
             nc.tensor.matmul_mx(
-                acc[:],
-                lhsT=wv_codes[:, block(b)].bitcast(E4M3),
-                lhsT_scale=wv_scales[:, block(b)],
-                rhs=g_codes[:, moving].bitcast(E5M2),
-                rhs_scale=g_scales[:, moving],
+                acc,
+                lhsT=wd_codes[:, block(t)].bitcast(E4M3),
+                lhsT_scale=wd_scales[:, block(t)],
+                rhs=x_codes[:, pieces[k]].bitcast(E4M3),
+                rhs_scale=x_scales[:, pieces[k]],
                 start=True,
                 stop=True,
             )
-            return acc
 
-        def stage(sums, staged):
-            nc.scalar.activation(staged, sums, ACT.Copy)
+        def quantize_x(k):
+            nc.vector.quantize_mx(x_codes[:, pieces[k]].bitcast(E4M3), x_scales[:, pieces[k]], x_bf[k][:])
+
+        def planes_tile(name, k):
+            return tile("%s%d" % (name, k), [P, PACK, pieces[k].stop - pieces[k].start], F32)
+
+        q = [planes_tile("q", k) for k in range(3)]
+        squared = [planes_tile("sq", k) for k in range(3)]
+        decay = [planes_tile("e", k) for k in range(3)]
+        weighted = [planes_tile("wq", k) for k in range(3)]
+        g_words = [tile("g%d" % h, [P, HALF * PACK], BF16) for h in range(2)]
+        g_codes = tile("g_codes", [P, N], U32)
+        g_scales = tile("g_scales", [P, N], U8)
+        wv_bf = [tile("wv_bf%d" % h, [P, HALF * PACK], BF16) for h in range(2)]
+        wv_scales = tile("wv_scales", [P, D], U8)
+        wv_codes = tile("wv_codes", [P, D], U32)
+
+        def chunk_residual(k):
+            acc = bank("a%d" % k)
+            for t in range(PACK):
+                first_product(k, acc[:, block(t)], t)
+            nc.vector.tensor_tensor(
+                q[k][:], acc[:].rearrange("p (t n) -> p t n", t=PACK), y_sb[0][:, :, pieces[k]], ALU.subtract
+            )
+
+        def late_residual(u):
+            acc = bank("a%d" % (2 + u))
+            for t in range(PAIR):
+                first_product(2, acc[:, half(t)], PAIR * u + t)
+            nc.vector.tensor_tensor(
+                q[2][:, planes(u)], acc[:].rearrange("p (t n) -> p t n", t=PAIR), y_sb[1][:, planes(u)], ALU.subtract
+            )
+
+        def exponentiate(k, part):
+            nc.scalar.activation(squared[k][:, part], q[k][:, part], ACT.Square)
+            nc.scalar.activation(decay[k][:, part], squared[k][:, part], ACT.Exp, scale=-0.5)
+
+        def weigh(k):
+            for t in range(PACK):
+                nc.vector.scalar_tensor_tensor(
+                    in_fours(weighted[k][:, t]),
+                    in_fours(q[k][:, t]),
+                    cw_sb[:, t : t + 1],
+                    rw_entries(pieces[k]),
+                    ALU.mult,
+                    ALU.mult,
+                )
+
+        def gradient(k, words):
+            nc.vector.tensor_tensor(as_words(words), as_planes(weighted[k][:]), as_planes(decay[k][:]), ALU.mult)
+
+        def quantize_g(h):
+            nc.vector.quantize_mx(g_codes[:, half(h)].bitcast(E5M2), g_scales[:, half(h)], g_words[h][:])
+
+        def quantize_wv(h):
+            nc.vector.quantize_mx(wv_codes[:, half(h)].bitcast(E4M3), wv_scales[:, half(h)], wv_bf[h][:])
+
+        def second_product(acc, b, entries):
+            nc.tensor.matmul_mx(
+                acc,
+                lhsT=wv_codes[:, block(b)].bitcast(E4M3),
+                lhsT_scale=wv_scales[:, block(b)],
+                rhs=g_codes[:, entries].bitcast(E5M2),
+                rhs_scale=g_scales[:, entries],
+                start=True,
+                stop=True,
+            )
+
+        def vector_scatter(b, staged, entries):
+            nc.vector.tensor_copy(windows[b][:].indirect(listed(entries)), staged)
+
+        def scalar_scatter(b, staged, entries):
+            nc.scalar.activation(windows[b][:].indirect(listed(entries)), staged, ACT.Copy)
+
+        def store(b):
+            nc.sync.dma_start(out[block(b), :], windows[b][:])
+
+        everything = slice(0, PACK)
+        for k in range(2):
+            quantize_x(k)
+        for k in range(2):
+            chunk_residual(k)
+            exponentiate(k, everything)
+        quantize_x(2)
+        weigh(0)
+        gradient(0, g_words[0][:, : P * PACK])
+        nc.scalar.activation(as_words(wv_bf[0][:]), as_planes(wv_raw[:, :, half(0)]), ACT.Copy)
+        for u in range(2):
+            late_residual(u)
+            exponentiate(2, planes(u))
+        weigh(1)
+        gradient(1, g_words[0][:, P * PACK :])
+        quantize_wv(0)
+        quantize_g(0)
+
+        def front_sums(h):
+            acc = bank("front%d" % h)
+            for b in range(2):
+                second_product(acc[:, half(b)], b, half(h))
+            staged = tile("dx_front%d" % h, [P, N], F32)
+            nc.scalar.activation(staged[:], acc[:], ACT.Copy)
             return staged
 
-        def scatter(b, staged, entries):
-            listed = offsets[:, entries.start // GROUP : entries.stop // GROUP]
-            nc.vector.tensor_copy(windows[b][:].indirect(listed), staged)
-
-        squared = {(0, u): tile("sq0%d" % u, [P, PAIR, HALF], F32) for u in range(2)}
-        late_squared = tile("sq10", [P, PACK, HALF], F32)
-        for h in range(2):
-            for u in (h, 1 - h):
-                if (h, u) == (0, 0):
-                    for t, sums in enumerate((first_bank, a_banks[h, u])):
-                        nc.vector.tensor_tensor(q[h, u][:, t], sums[:, half(t)], y_sb[u][:, t, half(h)], ALU.subtract)
-                    continue
-                nc.vector.tensor_tensor(
-                    q[h, u],
-                    a_banks[h, u][:].rearrange("p (t n) -> p t n", t=PAIR),
-                    y_sb[u][:, :, half(h)],
-                    ALU.subtract,
-                )
-            nc.gpsimd.tensor_tensor(weighted[h][:, planes(h)], q[h, h], weights[h], ALU.mult)
-        for h in range(2):
-            if h == 0:
-                for t in range(PAIR):
-                    nc.scalar.activation(squared[0, 0][:, t], q[0, 0][:, t], ACT.Square)
-                for t in range(PAIR):
-                    nc.scalar.activation(
-                        decay[0][:, :, t], squared[0, 0][:, t].rearrange("p (c i) -> p c i", c=2), ACT.Exp, scale=-0.5
-                    )
-                nc.scalar.activation(squared[0, 1][:], q[0, 1], ACT.Square)
-                nc.scalar.activation(
-                    decay[0][:, :, planes(1)],
-                    squared[0, 1][:].rearrange("p t (c i) -> p c t i", c=2),
-                    ACT.Exp,
-                    scale=-0.5,
-                )
-                wv_first = tile("wv_bf0", [P, P * PACK], BF16)
-                round_wv(wv_raw[:, :, :SCALAR_WV], wv_first[:, : SCALAR_WV * PACK])
-                continue
-            for u in (1, 0):
-                nc.scalar.activation(late_squared[:, planes(u)], q[h, u], ACT.Square)
-            for c in range(2):
-                nc.scalar.activation(decay[h][:, c], late_squared[:, :, block(c)], ACT.Exp, scale=-0.5)
-        for h in range(2):
-            for t in range(PAIR * (1 - h), PAIR * (2 - h)):
-                nc.vector.scalar_tensor_tensor(
-                    in_fours(weighted[h][:, t]),
-                    in_fours(q[h, 1 - h][:, t % PAIR]),
-                    cw_sb[:, t : t + 1],
-                    rw_entries(half(h)),
-                    ALU.mult,
-                    ALU.mult,
-                )
-        nc.vector.tensor_copy(as_words(wv_first[:, SCALAR_WV * PACK :]), as_planes(wv_raw[:, :, SCALAR_WV:P]))
-        g_words = [tile("g0", [P, HALF * PACK], BF16)]
-        for c in range(2):
-            gradient(0, c)
-        quantize_wv(0, 1, wv_first[:])
-        quantize_g(0)
-        g_words.append(tile("g1", [P, HALF * PACK], BF16, takes_over="wv_bf0"))
-        early_sums = second_product(0, 0, "early")[:, half(1)]
-        wv_second = round_wv(wv_raw[:, :, block(1)], tile("wv_bf1", [P, P * PACK], BF16, "sq10")[:])
-        for c in range(2):
-            gradient(1, c)
-        quantize_wv(1, 2, wv_second)
-        second_sums = second_product(1, 0, "early_second")[:, half(1)]
+        front = [front_sums(0)]
+        scalar_scatter(0, front[0][:, half(0)], half(0))
+        weigh(2)
+        gradient(2, g_words[1][:])
+        nc.vector.tensor_copy(as_words(wv_bf[1][:]), as_planes(wv_raw[:, :, half(1)]))
         quantize_g(1)
-        early = decay[1][:].rearrange("p c t i -> p (c t i)")[:, N + GROUP - HALF : N + GROUP]
-        for columns in (slice(0, HALF - GROUP), slice(HALF - GROUP, HALF)):
-            stage(early_sums[:, columns], early[:, columns])
-        scatter(0, early, half(0))
-        scatter(1, stage(second_sums, tile("dx_early1", [P, HALF], F32)[:]), half(0))
-        wv_rest = round_wv(wv_raw[:, :, half(1)], tile("wv_bf2", [P, HALF * PACK], BF16, "sq10")[:])
-        for b, entries in ((0, half(1)), (1, half(1)), (2, slice(0, N)), (3, slice(0, N))):
-            if b == 2:
-                quantize_wv(2, 4, wv_rest)
-            if b > 1:
-                windows.append(tile("window%d" % b, [P, T], F32, ("sq10", "dx_late1")[b - 2]))
-                nc.gpsimd.memset(windows[b][:], 0.0)
-            sums = second_product(b, HALF, "late%d" % b, "a%d%d" % (b // 2, b % 2))[:, entries]
-            scatter(b, stage(sums, tile("dx_late%d" % b, [P, entries.stop - entries.start], F32)[:]), entries)
-            nc.sync.dma_start(out[block(b), :], windows[b][:])
+        quantize_wv(1)
+        front.append(front_sums(1))
+        scalar_scatter(0, front[1][:, half(0)], half(1))
+        store(0)
+        for h in range(2):
+            vector_scatter(1, front[h][:, half(1)], half(h))
+        store(1)
+        back = {}
+        for b in (3, 2):
+            acc = bank("back%d" % b, "a%d" % (b - 2))
+            second_product(acc[:], b, slice(0, N))
+            back[b] = tile("dx_back%d" % b, [P, N], F32)
+            nc.scalar.activation(back[b][:], acc[:], ACT.Copy)
+        for h in range(2):
+            scalar_scatter(2, back[2][:, half(h)], half(h))
+        store(2)
+        vector_scatter(3, back[3][:], slice(0, N))
+        store(3)

@@ -63,18 +63,19 @@ def tile_attend_gml_wel_kernel(tc, xT, wd, wv, y, cw, rw, offs, out):
         x_planes = xT.rearrange("(p t) n -> p t n", t=PACK)
         x_raw = [tile("x_raw%d" % t, [P, T], F32) for t in range(PACK)]
         wd_raw = tile("wd_raw", [P, PACK, V], F32)
-        wv_raw = tile("wv_raw", [P, PACK, D], F32)
+        wv_raw = [tile("wv_raw%d" % h, [P, PACK, HALF], F32) for h in range(2)]
+        wv_planes = wv.rearrange("(p t) d -> p t d", t=PACK)
         y_planes = y.rearrange("(p t) n -> p t n", t=PACK)
         y_sb = [tile("y_sb%d" % h, [P, PACK, HALF], F32) for h in range(2)]
         nc.sync.dma_start(wd_raw[:], wd.rearrange("(p j) v -> p j v", j=PACK))
         nc.sync.dma_start(offsets[:], offs)
+        nc.scalar.dma_start(rw_sb[:], rw[0:1, :].rearrange("o (m j) -> m (o j)", j=PACK))
+        nc.scalar.dma_start(cw_sb[:], cw.rearrange("(p t) o -> p (t o)", t=PACK))
         for t in range(PACK):
             nc.sync.dma_start(x_raw[t][:], x_planes[:, t, :])
-        nc.sync.dma_start(rw_sb[:], rw[0:1, :].rearrange("o (m j) -> m (o j)", j=PACK))
-        nc.sync.dma_start(cw_sb[:], cw.rearrange("(p t) o -> p (t o)", t=PACK))
-        nc.sync.dma_start(y_sb[0][:], y_planes[:, :, half(0)])
-        nc.sync.dma_start(y_sb[1][:], y_planes[:, :, half(1)])
-        nc.sync.dma_start(wv_raw[:], wv.rearrange("(p t) d -> p t d", t=PACK))
+        for h in range(2):
+            nc.sync.dma_start(y_sb[h][:], y_planes[:, :, half(h)])
+            nc.sync.dma_start(wv_raw[h][:], wv_planes[:, :, half(h)])
 
         identity = tile("identity", [P, P], F32)
         make_identity(nc, identity[:])
@@ -87,7 +88,7 @@ def tile_attend_gml_wel_kernel(tc, xT, wd, wv, y, cw, rw, offs, out):
 
         windows = [tile("window%d" % b, [P, T], F32) for b in range(PACK)]
         for window in windows:
-            nc.gpsimd.memset(window[:], 0.0)
+            nc.vector.memset(window[:], 0.0)
 
         wd_bf = [tile("wd_bf%d" % u, [P, PAIR, P, PACK], BF16) for u in range(2)]
         wd_codes = tile("wd_codes", [P, V], U32)
@@ -100,8 +101,14 @@ def tile_attend_gml_wel_kernel(tc, xT, wd, wv, y, cw, rw, offs, out):
                 wd_codes[:, half(u)].bitcast(E4M3), wd_scales[:, half(u)], wd_bf[u][:].rearrange("p t m j -> p (t m j)")
             )
 
+        early_weights = tile("early_weights", [P, PACK, HALF], F32)
+        early_rw = tile("early_rw", [P, HALF], F32)
+        nc.scalar.activation(in_fours(early_rw[:]), rw_entries(half(0)), ACT.Copy)
+        for t in range(PACK):
+            nc.gpsimd.tensor_scalar(early_weights[:, t], early_rw[:], cw_sb[:, t : t + 1], 0.0, ALU.mult, ALU.add)
+
         pieces = [block(0), block(1), half(1)]
-        x_bf = [tile("x_bf%d" % k, [P, (s.stop - s.start) * PACK], BF16) for k, s in enumerate(pieces)]
+        x_bf = [tile("x_bf%d" % k, [P, P * PACK], BF16) for k in range(2)]
         gathered = tile("gathered", [P, PACK, HALF], BF16)
         for t in range(PACK):
             for k in range(2):
@@ -109,7 +116,6 @@ def tile_attend_gml_wel_kernel(tc, xT, wd, wv, y, cw, rw, offs, out):
                     x_bf[k][:].rearrange("p (i t) -> p t i", t=PACK)[:, t], x_raw[t][:].indirect(listed(pieces[k]))
                 )
             nc.scalar.activation(gathered[:, t], x_raw[t][:].indirect(listed(half(1))), ACT.Copy)
-        nc.scalar.activation(as_words(x_bf[2][:]), as_planes(gathered[:]), ACT.Copy)
 
         x_scales = tile("x_scales", [P, N], U8)
         x_codes = tile("x_codes", [P, N], U32)
@@ -128,26 +134,26 @@ def tile_attend_gml_wel_kernel(tc, xT, wd, wv, y, cw, rw, offs, out):
         def quantize_x(k):
             nc.vector.quantize_mx(x_codes[:, pieces[k]].bitcast(E4M3), x_scales[:, pieces[k]], x_bf[k][:])
 
-        def planes_tile(name, k):
-            return tile("%s%d" % (name, k), [P, PACK, pieces[k].stop - pieces[k].start], F32)
+        def planes_tiles(name):
+            return [tile("%s%d" % (name, h), [P, PACK, HALF], F32) for h in range(2)]
 
-        q = [planes_tile("q", k) for k in range(3)]
-        squared = [planes_tile("sq", k) for k in range(3)]
-        decay = [planes_tile("e", k) for k in range(3)]
-        weighted = [planes_tile("wq", k) for k in range(3)]
+        squared = planes_tiles("sq")
+        late_decay = tile("e1", [P, PACK * HALF + HALF - GROUP], F32)
+        decay = [tile("e0", [P, PACK, HALF], F32)[:], late_decay[:, : PACK * HALF].rearrange("p (t n) -> p t n", t=PACK)]
+        weighted = planes_tiles("wq")
         g_words = [tile("g%d" % h, [P, HALF * PACK], BF16) for h in range(2)]
         g_codes = tile("g_codes", [P, N], U32)
         g_scales = tile("g_scales", [P, N], U8)
-        wv_bf = [tile("wv_bf%d" % h, [P, HALF * PACK], BF16) for h in range(2)]
+        wv_bf = [tile("wv_bf0", [P, HALF * PACK], BF16)]
         wv_scales = tile("wv_scales", [P, D], U8)
-        wv_codes = tile("wv_codes", [P, D], U32)
+        wv_codes = tile("wv_codes", [P, D], U32, "early_weights")
 
         def chunk_residual(k):
             acc = bank("a%d" % k)
             for t in range(PACK):
                 first_product(k, acc[:, block(t)], t)
             nc.vector.tensor_tensor(
-                q[k][:], acc[:].rearrange("p (t n) -> p t n", t=PACK), y_sb[0][:, :, pieces[k]], ALU.subtract
+                q[0][:, :, pieces[k]], acc[:].rearrange("p (t n) -> p t n", t=PACK), y_sb[0][:, :, pieces[k]], ALU.subtract
             )
 
         def late_residual(u):
@@ -155,26 +161,15 @@ def tile_attend_gml_wel_kernel(tc, xT, wd, wv, y, cw, rw, offs, out):
             for t in range(PAIR):
                 first_product(2, acc[:, half(t)], PAIR * u + t)
             nc.vector.tensor_tensor(
-                q[2][:, planes(u)], acc[:].rearrange("p (t n) -> p t n", t=PAIR), y_sb[1][:, planes(u)], ALU.subtract
+                q[1][:, planes(u)], acc[:].rearrange("p (t n) -> p t n", t=PAIR), y_sb[1][:, planes(u)], ALU.subtract
             )
 
-        def exponentiate(k, part):
-            nc.scalar.activation(squared[k][:, part], q[k][:, part], ACT.Square)
-            nc.scalar.activation(decay[k][:, part], squared[k][:, part], ACT.Exp, scale=-0.5)
+        def exponentiate(h, part, entries):
+            nc.scalar.activation(squared[h][:, part, entries], q[h][:, part, entries], ACT.Square)
+            nc.scalar.activation(decay[h][:, part, entries], squared[h][:, part, entries], ACT.Exp, scale=-0.5)
 
-        def weigh(k):
-            for t in range(PACK):
-                nc.vector.scalar_tensor_tensor(
-                    in_fours(weighted[k][:, t]),
-                    in_fours(q[k][:, t]),
-                    cw_sb[:, t : t + 1],
-                    rw_entries(pieces[k]),
-                    ALU.mult,
-                    ALU.mult,
-                )
-
-        def gradient(k, words):
-            nc.vector.tensor_tensor(as_words(words), as_planes(weighted[k][:]), as_planes(decay[k][:]), ALU.mult)
+        def gradient(h):
+            nc.vector.tensor_tensor(as_words(g_words[h][:]), as_planes(weighted[h][:]), as_planes(decay[h]), ALU.mult)
 
         def quantize_g(h):
             nc.vector.quantize_mx(g_codes[:, half(h)].bitcast(E5M2), g_scales[:, half(h)], g_words[h][:])
@@ -202,53 +197,76 @@ def tile_attend_gml_wel_kernel(tc, xT, wd, wv, y, cw, rw, offs, out):
         def store(b):
             nc.sync.dma_start(out[block(b), :], windows[b][:])
 
-        everything = slice(0, PACK)
         for k in range(2):
             quantize_x(k)
+        x_bf.append(tile("x_bf2", [P, HALF * PACK], BF16, "x_bf0"))
+        nc.vector.tensor_copy(as_words(x_bf[2][:, : P * PACK]), as_planes(gathered[:, :, block(0)]))
+        nc.scalar.activation(as_words(x_bf[2][:, P * PACK :]), as_planes(gathered[:, :, block(1)]), ACT.Copy)
+        quantize_x(2)
+        q = [tile("q0", [P, PACK, HALF], F32, "x_bf0"), tile("q1", [P, PACK, HALF], F32)]
+        nc.scalar.activation(as_words(wv_bf[0][:]), as_planes(wv_raw[0][:]), ACT.Copy)
         for k in range(2):
             chunk_residual(k)
-            exponentiate(k, everything)
-        quantize_x(2)
-        weigh(0)
-        gradient(0, g_words[0][:, : P * PACK])
-        nc.scalar.activation(as_words(wv_bf[0][:]), as_planes(wv_raw[:, :, half(0)]), ACT.Copy)
+            nc.gpsimd.tensor_tensor(
+                weighted[0][:, :, pieces[k]], q[0][:, :, pieces[k]], early_weights[:, :, pieces[k]], ALU.mult
+            )
+            exponentiate(0, slice(0, PACK), pieces[k])
         for u in range(2):
             late_residual(u)
-            exponentiate(2, planes(u))
-        weigh(1)
-        gradient(1, g_words[0][:, P * PACK :])
+            exponentiate(1, planes(u), half(0))
+        for t in range(PACK):
+            nc.vector.scalar_tensor_tensor(
+                in_fours(weighted[1][:, t]),
+                in_fours(q[1][:, t]),
+                cw_sb[:, t : t + 1],
+                rw_entries(half(1)),
+                ALU.mult,
+                ALU.mult,
+            )
+        wv_bf.append(tile("wv_bf1", [P, HALF * PACK], BF16, "sq1"))
+        nc.scalar.activation(as_words(wv_bf[1][:]), as_planes(wv_raw[1][:]), ACT.Copy)
+        gradient(0)
         quantize_wv(0)
         quantize_g(0)
+
+        def stage(name, acc):
+            staged = tile(name, [P, N], F32)
+            nc.scalar.activation(staged[:], acc[:], ACT.Copy)
+            return staged
 
         def front_sums(h):
             acc = bank("front%d" % h)
             for b in range(2):
                 second_product(acc[:, half(b)], b, half(h))
-            staged = tile("dx_front%d" % h, [P, N], F32)
-            nc.scalar.activation(staged[:], acc[:], ACT.Copy)
-            return staged
+            return stage("dx_front%d" % h, acc)
 
-        front = [front_sums(0)]
-        scalar_scatter(0, front[0][:, half(0)], half(0))
-        weigh(2)
-        gradient(2, g_words[1][:])
-        nc.vector.tensor_copy(as_words(wv_bf[1][:]), as_planes(wv_raw[:, :, half(1)]))
-        quantize_g(1)
-        quantize_wv(1)
-        front.append(front_sums(1))
-        scalar_scatter(0, front[1][:, half(0)], half(1))
-        store(0)
-        for h in range(2):
-            vector_scatter(1, front[h][:, half(1)], half(h))
-        store(1)
-        back = {}
-        for b in (3, 2):
+        def back_sums(b):
             acc = bank("back%d" % b, "a%d" % (b - 2))
             second_product(acc[:], b, slice(0, N))
-            back[b] = tile("dx_back%d" % b, [P, N], F32)
-            nc.scalar.activation(back[b][:], acc[:], ACT.Copy)
-        for h in range(2):
-            scalar_scatter(2, back[2][:, half(h)], half(h))
-        store(2)
-        vector_scatter(3, back[3][:], slice(0, N))
+            return stage("dx_back%d" % b, acc)
+
+        early = bank("front0")
+        for b in range(2):
+            second_product(early[:, half(b)], b, half(0))
+        early0 = tile("dx_early0", [P, HALF], F32)
+        nc.scalar.activation(early0[:], early[:, half(0)], ACT.Copy)
+        scalar_scatter(0, early0[:], half(0))
+        early1 = late_decay[:, PACK * HALF - GROUP :]
+        nc.scalar.activation(early1[:, GROUP:], early[:, HALF + GROUP :], ACT.Copy)
+        gradient(1)
+        quantize_wv(1)
+        nc.vector.tensor_copy(early1[:, :GROUP], early[:, HALF : HALF + GROUP])
+        quantize_g(1)
+        late = front_sums(1)
+        vector_scatter(1, early1, half(0))
+        vector_scatter(1, late[:, half(1)], half(1))
+        store(1)
+        back3 = back_sums(3)
+        scalar_scatter(0, late[:, half(0)], half(1))
+        store(0)
+        vector_scatter(3, back3[:], slice(0, N))
         store(3)
+        back2 = back_sums(2)
+        for h in range(2):
+            scalar_scatter(2, back2[:, half(h)], half(h))
+        store(2)

@@ -62,20 +62,23 @@ def tile_attend_gml_wel_kernel(tc, xT, wd, wv, y, cw, rw, offs, out):
         rw_sb = tile("rw_sb", [P, PACK], F32)
         x_planes = xT.rearrange("(p t) n -> p t n", t=PACK)
         x_raw = [tile("x_raw%d" % t, [P, T], F32) for t in range(PACK)]
-        wd_raw = tile("wd_raw", [P, PACK, V], F32)
+        wd_raw = [tile("wd_raw%d" % h, [P, PACK, HALF], F32) for h in range(2)]
+        wd_planes = wd.rearrange("(p j) v -> p j v", j=PACK)
         wv_raw = [tile("wv_raw%d" % h, [P, PACK, HALF], F32) for h in range(2)]
         wv_planes = wv.rearrange("(p t) d -> p t d", t=PACK)
         y_planes = y.rearrange("(p t) n -> p t n", t=PACK)
         y_sb = [tile("y_sb%d" % h, [P, PACK, HALF], F32) for h in range(2)]
-        nc.sync.dma_start(wd_raw[:], wd.rearrange("(p j) v -> p j v", j=PACK))
+        nc.sync.dma_start(wd_raw[0][:], wd_planes[:, :, half(0)])
         nc.sync.dma_start(offsets[:], offs)
-        nc.scalar.dma_start(rw_sb[:], rw[0:1, :].rearrange("o (m j) -> m (o j)", j=PACK))
-        nc.scalar.dma_start(cw_sb[:], cw.rearrange("(p t) o -> p (t o)", t=PACK))
+        nc.sync.dma_start(rw_sb[:], rw[0:1, :].rearrange("o (m j) -> m (o j)", j=PACK))
+        nc.sync.dma_start(cw_sb[:], cw.rearrange("(p t) o -> p (t o)", t=PACK))
         for t in range(PACK):
             nc.sync.dma_start(x_raw[t][:], x_planes[:, t, :])
+        nc.sync.dma_start(wd_raw[1][:], wd_planes[:, :, half(1)])
+        nc.sync.dma_start(wv_raw[0][:], wv_planes[:, :, half(0)])
         for h in range(2):
             nc.sync.dma_start(y_sb[h][:], y_planes[:, :, half(h)])
-            nc.sync.dma_start(wv_raw[h][:], wv_planes[:, :, half(h)])
+        nc.sync.dma_start(wv_raw[1][:], wv_planes[:, :, half(1)])
 
         identity = tile("identity", [P, P], F32)
         make_identity(nc, identity[:])
@@ -87,19 +90,8 @@ def tile_attend_gml_wel_kernel(tc, xT, wd, wv, y, cw, rw, offs, out):
             return rw_bank[:].rearrange("p (j m) -> p m j", j=PACK)[:, entries.start // PACK : entries.stop // PACK, :]
 
         windows = [tile("window%d" % b, [P, T], F32) for b in range(PACK)]
-        for window in windows:
-            nc.vector.memset(window[:], 0.0)
-
-        wd_bf = [tile("wd_bf%d" % u, [P, PAIR, P, PACK], BF16) for u in range(2)]
-        wd_codes = tile("wd_codes", [P, V], U32)
-        wd_scales = tile("wd_scales", [P, V], U8)
-        wd_by_plane = wd_raw[:].rearrange("p j (m t) -> p m j t", t=PACK)
-        nc.vector.tensor_copy(wd_bf[0][:].rearrange("p t m j -> p m j t"), wd_by_plane[:, :, :, planes(0)])
-        nc.scalar.activation(wd_bf[1][:].rearrange("p t m j -> p m j t"), wd_by_plane[:, :, :, planes(1)], ACT.Copy)
-        for u in range(2):
-            nc.vector.quantize_mx(
-                wd_codes[:, half(u)].bitcast(E4M3), wd_scales[:, half(u)], wd_bf[u][:].rearrange("p t m j -> p (t m j)")
-            )
+        for b, window in enumerate(windows):
+            (nc.vector if b < 2 else nc.gpsimd).memset(window[:], 0.0)
 
         early_weights = tile("early_weights", [P, PACK, HALF], F32)
         early_rw = tile("early_rw", [P, HALF], F32)
@@ -107,37 +99,45 @@ def tile_attend_gml_wel_kernel(tc, xT, wd, wv, y, cw, rw, offs, out):
         for t in range(PACK):
             nc.gpsimd.tensor_scalar(early_weights[:, t], early_rw[:], cw_sb[:, t : t + 1], 0.0, ALU.mult, ALU.add)
 
-        pieces = [block(0), block(1), half(1)]
-        x_bf = [tile("x_bf%d" % k, [P, P * PACK], BF16) for k in range(2)]
+        x_bf = [tile("x_bf%d" % h, [P, HALF * PACK], BF16) for h in range(2)]
         gathered = tile("gathered", [P, PACK, HALF], BF16)
         for t in range(PACK):
-            for k in range(2):
-                nc.vector.tensor_copy(
-                    x_bf[k][:].rearrange("p (i t) -> p t i", t=PACK)[:, t], x_raw[t][:].indirect(listed(pieces[k]))
-                )
+            nc.vector.tensor_copy(
+                x_bf[0][:].rearrange("p (i t) -> p t i", t=PACK)[:, t], x_raw[t][:].indirect(listed(half(0)))
+            )
             nc.scalar.activation(gathered[:, t], x_raw[t][:].indirect(listed(half(1))), ACT.Copy)
+        nc.scalar.activation(as_words(x_bf[1][:]), as_planes(gathered[:]), ACT.Copy)
 
         x_scales = tile("x_scales", [P, N], U8)
         x_codes = tile("x_codes", [P, N], U32)
 
-        def first_product(k, acc, t):
-            nc.tensor.matmul_mx(
-                acc,
-                lhsT=wd_codes[:, block(t)].bitcast(E4M3),
-                lhsT_scale=wd_scales[:, block(t)],
-                rhs=x_codes[:, pieces[k]].bitcast(E4M3),
-                rhs_scale=x_scales[:, pieces[k]],
-                start=True,
-                stop=True,
+        def quantize_x(h):
+            nc.vector.quantize_mx(x_codes[:, half(h)].bitcast(E4M3), x_scales[:, half(h)], x_bf[h][:])
+
+        wd_bf = [tile("wd_bf%d" % u, [P, PAIR, P, PACK], BF16) for u in range(2)]
+        wd_codes = tile("wd_codes", [P, V], U32)
+        wd_scales = tile("wd_scales", [P, V], U8)
+
+        def deal(h, u):
+            columns = slice(h * HALF // PACK, (h + 1) * HALF // PACK)
+            return (
+                wd_bf[u][:].rearrange("p t m j -> p m j t")[:, columns],
+                wd_raw[h][:].rearrange("p j (m t) -> p m j t", t=PACK)[:, :, :, planes(u)],
             )
 
-        def quantize_x(k):
-            nc.vector.quantize_mx(x_codes[:, pieces[k]].bitcast(E4M3), x_scales[:, pieces[k]], x_bf[k][:])
+        nc.vector.tensor_copy(*deal(0, 0))
+        nc.scalar.activation(*deal(0, 1), ACT.Copy)
+        quantize_x(0)
+        for u in range(2):
+            nc.vector.tensor_copy(*deal(1, u))
+        for u in range(2):
+            nc.vector.quantize_mx(
+                wd_codes[:, half(u)].bitcast(E4M3), wd_scales[:, half(u)], wd_bf[u][:].rearrange("p t m j -> p (t m j)")
+            )
 
         def planes_tiles(name):
             return [tile("%s%d" % (name, h), [P, PACK, HALF], F32) for h in range(2)]
 
-        squared = planes_tiles("sq")
         late_decay = tile("e1", [P, PACK * HALF + HALF - GROUP], F32)
         decay = [tile("e0", [P, PACK, HALF], F32)[:], late_decay[:, : PACK * HALF].rearrange("p (t n) -> p t n", t=PACK)]
         weighted = planes_tiles("wq")
@@ -148,25 +148,26 @@ def tile_attend_gml_wel_kernel(tc, xT, wd, wv, y, cw, rw, offs, out):
         wv_scales = tile("wv_scales", [P, D], U8)
         wv_codes = tile("wv_codes", [P, D], U32, "early_weights")
 
-        def chunk_residual(k):
-            acc = bank("a%d" % k)
-            for t in range(PACK):
-                first_product(k, acc[:, block(t)], t)
-            nc.vector.tensor_tensor(
-                q[0][:, :, pieces[k]], acc[:].rearrange("p (t n) -> p t n", t=PACK), y_sb[0][:, :, pieces[k]], ALU.subtract
-            )
-
-        def late_residual(u):
-            acc = bank("a%d" % (2 + u))
+        def residual(h, u):
+            acc = bank("a%d" % (2 * h + u))
             for t in range(PAIR):
-                first_product(2, acc[:, half(t)], PAIR * u + t)
+                nc.tensor.matmul_mx(
+                    acc[:, half(t)],
+                    lhsT=wd_codes[:, block(PAIR * u + t)].bitcast(E4M3),
+                    lhsT_scale=wd_scales[:, block(PAIR * u + t)],
+                    rhs=x_codes[:, half(h)].bitcast(E4M3),
+                    rhs_scale=x_scales[:, half(h)],
+                    start=True,
+                    stop=True,
+                )
             nc.vector.tensor_tensor(
-                q[1][:, planes(u)], acc[:].rearrange("p (t n) -> p t n", t=PAIR), y_sb[1][:, planes(u)], ALU.subtract
+                q[h][:, planes(u)], acc[:].rearrange("p (t n) -> p t n", t=PAIR), y_sb[h][:, planes(u)], ALU.subtract
             )
 
-        def exponentiate(h, part, entries):
-            nc.scalar.activation(squared[h][:, part, entries], q[h][:, part, entries], ACT.Square)
-            nc.scalar.activation(decay[h][:, part, entries], squared[h][:, part, entries], ACT.Exp, scale=-0.5)
+        def exponentiate(h, u):
+            squared = tile("sq%d%d" % (h, u), [P, PAIR, HALF], F32, "sq%d" % u)
+            nc.scalar.activation(squared[:], q[h][:, planes(u)], ACT.Square)
+            nc.scalar.activation(decay[h][:, planes(u)], squared[:], ACT.Exp, scale=-0.5)
 
         def gradient(h):
             nc.vector.tensor_tensor(as_words(g_words[h][:]), as_planes(weighted[h][:]), as_planes(decay[h]), ALU.mult)
@@ -197,23 +198,17 @@ def tile_attend_gml_wel_kernel(tc, xT, wd, wv, y, cw, rw, offs, out):
         def store(b):
             nc.sync.dma_start(out[block(b), :], windows[b][:])
 
-        for k in range(2):
-            quantize_x(k)
-        x_bf.append(tile("x_bf2", [P, HALF * PACK], BF16, "x_bf0"))
-        nc.vector.tensor_copy(as_words(x_bf[2][:, : P * PACK]), as_planes(gathered[:, :, block(0)]))
-        nc.scalar.activation(as_words(x_bf[2][:, P * PACK :]), as_planes(gathered[:, :, block(1)]), ACT.Copy)
-        quantize_x(2)
-        q = [tile("q0", [P, PACK, HALF], F32, "x_bf0"), tile("q1", [P, PACK, HALF], F32)]
+        q = planes_tiles("q")
+        quantize_x(1)
         nc.scalar.activation(as_words(wv_bf[0][:]), as_planes(wv_raw[0][:]), ACT.Copy)
-        for k in range(2):
-            chunk_residual(k)
-            nc.gpsimd.tensor_tensor(
-                weighted[0][:, :, pieces[k]], q[0][:, :, pieces[k]], early_weights[:, :, pieces[k]], ALU.mult
-            )
-            exponentiate(0, slice(0, PACK), pieces[k])
-        for u in range(2):
-            late_residual(u)
-            exponentiate(1, planes(u), half(0))
+        for h in range(2):
+            for u in range(2):
+                residual(h, u)
+                if h == 0:
+                    nc.gpsimd.tensor_tensor(
+                        weighted[0][:, planes(u)], q[0][:, planes(u)], early_weights[:, planes(u)], ALU.mult
+                    )
+                exponentiate(h, u)
         for t in range(PACK):
             nc.vector.scalar_tensor_tensor(
                 in_fours(weighted[1][:, t]),
@@ -243,25 +238,29 @@ def tile_attend_gml_wel_kernel(tc, xT, wd, wv, y, cw, rw, offs, out):
         def back_sums(b):
             acc = bank("back%d" % b, "a%d" % (b - 2))
             second_product(acc[:], b, slice(0, N))
-            return stage("dx_back%d" % b, acc)
+            if b == 2:
+                return stage("dx_back%d" % b, acc)
+            staged = tile("dx_back%d" % b, [P, N], F32)
+            nc.vector.tensor_copy(staged[:], acc[:])
+            return staged
 
         early = bank("front0")
         for b in range(2):
             second_product(early[:, half(b)], b, half(0))
         early0 = tile("dx_early0", [P, HALF], F32)
-        nc.scalar.activation(early0[:], early[:, half(0)], ACT.Copy)
-        scalar_scatter(0, early0[:], half(0))
         early1 = late_decay[:, PACK * HALF - GROUP :]
+        nc.scalar.activation(early0[:], early[:, half(0)], ACT.Copy)
         nc.scalar.activation(early1[:, GROUP:], early[:, HALF + GROUP :], ACT.Copy)
+        scalar_scatter(0, early0[:], half(0))
         gradient(1)
         quantize_wv(1)
         nc.vector.tensor_copy(early1[:, :GROUP], early[:, HALF : HALF + GROUP])
         quantize_g(1)
         late = front_sums(1)
         vector_scatter(1, early1, half(0))
+        back3 = back_sums(3)
         vector_scatter(1, late[:, half(1)], half(1))
         store(1)
-        back3 = back_sums(3)
         scalar_scatter(0, late[:, half(0)], half(1))
         store(0)
         vector_scatter(3, back3[:], slice(0, N))

@@ -22,6 +22,7 @@ PAIR = 2
 HALF = 256
 GROUP = 16
 RUN = 4
+SCALAR_COLUMNS = 40
 
 
 def tile_attend_gml_wel_kernel(tc, xT, wd, wv, y, cw, rw, offs, out):
@@ -62,29 +63,30 @@ def tile_attend_gml_wel_kernel(tc, xT, wd, wv, y, cw, rw, offs, out):
         rw_sb = tile("rw_sb", [P, PACK], F32)
         x_planes = xT.rearrange("(p t) n -> p t n", t=PACK)
         x_raw = [tile("x_raw%d" % t, [P, T], F32) for t in range(PACK)]
-        wd_raw = [tile("wd_raw%d" % h, [P, PACK, HALF], F32) for h in range(2)]
-        wd_planes = wd.rearrange("(p j) v -> p j v", j=PACK)
+        wd_raw = tile("wd_raw", [P, PACK, V], F32)
         wv_raw = [tile("wv_raw%d" % h, [P, PACK, HALF], F32) for h in range(2)]
         wv_planes = wv.rearrange("(p t) d -> p t d", t=PACK)
+        y_sb = [tile("y_sb%d" % u, [P, PAIR, N], F32) for u in range(2)]
         y_planes = y.rearrange("(p t) n -> p t n", t=PACK)
-        y_sb = [tile("y_sb%d" % h, [P, PACK, HALF], F32) for h in range(2)]
-        nc.sync.dma_start(wd_raw[0][:], wd_planes[:, :, half(0)])
-        nc.sync.dma_start(offsets[:], offs)
         nc.sync.dma_start(rw_sb[:], rw[0:1, :].rearrange("o (m j) -> m (o j)", j=PACK))
+        nc.sync.dma_start(x_raw[0][:], x_planes[:, 0, :])
+        nc.sync.dma_start(offsets[:], offs)
         nc.sync.dma_start(cw_sb[:], cw.rearrange("(p t) o -> p (t o)", t=PACK))
-        for t in range(PACK):
+        for t in range(1, PACK):
             nc.sync.dma_start(x_raw[t][:], x_planes[:, t, :])
-        nc.sync.dma_start(wd_raw[1][:], wd_planes[:, :, half(1)])
+        nc.sync.dma_start(wd_raw[:], wd.rearrange("(p j) v -> p j v", j=PACK))
         nc.sync.dma_start(wv_raw[0][:], wv_planes[:, :, half(0)])
-        for h in range(2):
-            nc.sync.dma_start(y_sb[h][:], y_planes[:, :, half(h)])
+        for u in range(2):
+            nc.sync.dma_start(y_sb[u][:], y_planes[:, planes(u), :])
         nc.sync.dma_start(wv_raw[1][:], wv_planes[:, :, half(1)])
 
         identity = tile("identity", [P, P], F32)
         make_identity(nc, identity[:])
         rw_bank = bank("rw_bank")
+        rw_wide = tile("rw_wide", [P, PACK, P], F32)
+        nc.scalar.activation(rw_wide[:], rw_sb[:].unsqueeze(2).to_broadcast([P, PACK, P]), ACT.Copy)
         for j in range(PACK):
-            nc.tensor.transpose(rw_bank[:, block(j)], rw_sb[:, j : j + 1].to_broadcast([P, P]), identity[:])
+            nc.tensor.transpose(rw_bank[:, block(j)], rw_wide[:, j], identity[:])
 
         def rw_entries(entries):
             return rw_bank[:].rearrange("p (j m) -> p m j", j=PACK)[:, entries.start // PACK : entries.stop // PACK, :]
@@ -106,7 +108,7 @@ def tile_attend_gml_wel_kernel(tc, xT, wd, wv, y, cw, rw, offs, out):
                 x_bf[0][:].rearrange("p (i t) -> p t i", t=PACK)[:, t], x_raw[t][:].indirect(listed(half(0)))
             )
             nc.scalar.activation(gathered[:, t], x_raw[t][:].indirect(listed(half(1))), ACT.Copy)
-        nc.scalar.activation(as_words(x_bf[1][:]), as_planes(gathered[:]), ACT.Copy)
+        nc.vector.tensor_copy(as_words(x_bf[1][:]), as_planes(gathered[:]))
 
         x_scales = tile("x_scales", [P, N], U8)
         x_codes = tile("x_codes", [P, N], U32)
@@ -118,33 +120,33 @@ def tile_attend_gml_wel_kernel(tc, xT, wd, wv, y, cw, rw, offs, out):
         wd_codes = tile("wd_codes", [P, V], U32)
         wd_scales = tile("wd_scales", [P, V], U8)
 
-        def deal(h, u):
-            columns = slice(h * HALF // PACK, (h + 1) * HALF // PACK)
+        def deal(u, columns):
             return (
                 wd_bf[u][:].rearrange("p t m j -> p m j t")[:, columns],
-                wd_raw[h][:].rearrange("p j (m t) -> p m j t", t=PACK)[:, :, :, planes(u)],
+                wd_raw[:].rearrange("p j (m t) -> p m j t", t=PACK)[:, columns, :, planes(u)],
             )
 
-        nc.vector.tensor_copy(*deal(0, 0))
-        nc.scalar.activation(*deal(0, 1), ACT.Copy)
-        quantize_x(0)
-        for u in range(2):
-            nc.vector.tensor_copy(*deal(1, u))
-        for u in range(2):
+        def quantize_wd(u):
             nc.vector.quantize_mx(
                 wd_codes[:, half(u)].bitcast(E4M3), wd_scales[:, half(u)], wd_bf[u][:].rearrange("p t m j -> p (t m j)")
             )
 
+        quantize_x(0)
+        nc.scalar.activation(*deal(0, slice(0, SCALAR_COLUMNS)), ACT.Copy)
+        nc.vector.tensor_copy(*deal(0, slice(SCALAR_COLUMNS, P)))
+        nc.scalar.activation(*deal(1, slice(0, P)), ACT.Copy)
+        quantize_wd(0)
+        quantize_x(1)
+        quantize_wd(1)
+
         def planes_tiles(name):
             return [tile("%s%d" % (name, h), [P, PACK, HALF], F32) for h in range(2)]
 
-        late_decay = tile("e1", [P, PACK * HALF + HALF - GROUP], F32)
-        decay = [tile("e0", [P, PACK, HALF], F32)[:], late_decay[:, : PACK * HALF].rearrange("p (t n) -> p t n", t=PACK)]
-        weighted = planes_tiles("wq")
+        weighted = [tile("wq0", [P, PACK, HALF], F32)[:]]
         g_words = [tile("g%d" % h, [P, HALF * PACK], BF16) for h in range(2)]
         g_codes = tile("g_codes", [P, N], U32)
         g_scales = tile("g_scales", [P, N], U8)
-        wv_bf = [tile("wv_bf0", [P, HALF * PACK], BF16)]
+        wv_bf = []
         wv_scales = tile("wv_scales", [P, D], U8)
         wv_codes = tile("wv_codes", [P, D], U32, "early_weights")
 
@@ -161,16 +163,18 @@ def tile_attend_gml_wel_kernel(tc, xT, wd, wv, y, cw, rw, offs, out):
                     stop=True,
                 )
             nc.vector.tensor_tensor(
-                q[h][:, planes(u)], acc[:].rearrange("p (t n) -> p t n", t=PAIR), y_sb[h][:, planes(u)], ALU.subtract
+                q[h][:, planes(u)], acc[:].rearrange("p (t n) -> p t n", t=PAIR), y_sb[u][:, :, half(h)], ALU.subtract
             )
 
-        def exponentiate(h, u):
-            squared = tile("sq%d%d" % (h, u), [P, PAIR, HALF], F32, "sq%d" % u)
-            nc.scalar.activation(squared[:], q[h][:, planes(u)], ACT.Square)
-            nc.scalar.activation(decay[h][:, planes(u)], squared[:], ACT.Exp, scale=-0.5)
+        def exponentiate(h):
+            squared = [tile("sq%d%d" % (h, u), [P, PAIR, HALF], F32) for u in range(2)]
+            for u in range(2):
+                nc.scalar.activation(squared[u][:], q[h][:, planes(u)], ACT.Square)
+            for u in range(2):
+                nc.scalar.activation(decay[h][:, planes(u)], squared[u][:], ACT.Exp, scale=-0.5)
 
         def gradient(h):
-            nc.vector.tensor_tensor(as_words(g_words[h][:]), as_planes(weighted[h][:]), as_planes(decay[h]), ALU.mult)
+            nc.vector.tensor_tensor(as_words(g_words[h][:]), as_planes(weighted[h]), as_planes(decay[h]), ALU.mult)
 
         def quantize_g(h):
             nc.vector.quantize_mx(g_codes[:, half(h)].bitcast(E5M2), g_scales[:, half(h)], g_words[h][:])
@@ -199,17 +203,25 @@ def tile_attend_gml_wel_kernel(tc, xT, wd, wv, y, cw, rw, offs, out):
             nc.sync.dma_start(out[block(b), :], windows[b][:])
 
         q = planes_tiles("q")
-        quantize_x(1)
+        wv_bf.append(tile("wv_bf0", [P, HALF * PACK], BF16))
         nc.scalar.activation(as_words(wv_bf[0][:]), as_planes(wv_raw[0][:]), ACT.Copy)
-        for h in range(2):
-            for u in range(2):
+        for u in range(2):
+            for h in range(2):
                 residual(h, u)
-                if h == 0:
-                    nc.gpsimd.tensor_tensor(
-                        weighted[0][:, planes(u)], q[0][:, planes(u)], early_weights[:, planes(u)], ALU.mult
-                    )
-                exponentiate(h, u)
-        for t in range(PACK):
+        for u in range(2):
+            nc.gpsimd.tensor_tensor(weighted[0][:, planes(u)], q[0][:, planes(u)], early_weights[:, planes(u)], ALU.mult)
+        size = PACK * HALF
+        behind_residuals = tile("behind_residuals", [P, 3 * size + HALF - GROUP], F32, "y_sb1")
+        parts = [behind_residuals[:, k * size : (k + 1) * size].rearrange("p (t n) -> p t n", t=PACK) for k in range(3)]
+        late_decay = behind_residuals[:, 2 * size :]
+        decay = [parts[0], parts[2]]
+        weighted.append(parts[1])
+        for h in range(2):
+            exponentiate(h)
+        wv_bf.append(tile("wv_bf1", [P, HALF * PACK], BF16, "sq10"))
+        nc.scalar.activation(as_words(wv_bf[1][:]), as_planes(wv_raw[1][:]), ACT.Copy)
+
+        def weigh_late(t):
             nc.vector.scalar_tensor_tensor(
                 in_fours(weighted[1][:, t]),
                 in_fours(q[1][:, t]),
@@ -218,54 +230,56 @@ def tile_attend_gml_wel_kernel(tc, xT, wd, wv, y, cw, rw, offs, out):
                 ALU.mult,
                 ALU.mult,
             )
-        wv_bf.append(tile("wv_bf1", [P, HALF * PACK], BF16, "sq1"))
-        nc.scalar.activation(as_words(wv_bf[1][:]), as_planes(wv_raw[1][:]), ACT.Copy)
+
+        for t in range(PACK):
+            weigh_late(t)
         gradient(0)
         quantize_wv(0)
         quantize_g(0)
 
-        def stage(name, acc):
-            staged = tile(name, [P, N], F32)
-            nc.scalar.activation(staged[:], acc[:], ACT.Copy)
+        def stage_halves(name, acc):
+            staged = [tile("%s%d" % (name, h), [P, HALF], F32) for h in range(2)]
+            for h in range(2):
+                nc.scalar.activation(staged[h][:], acc[:, half(h)], ACT.Copy)
             return staged
 
-        def front_sums(h):
-            acc = bank("front%d" % h)
-            for b in range(2):
-                second_product(acc[:, half(b)], b, half(h))
-            return stage("dx_front%d" % h, acc)
-
-        def back_sums(b):
+        def back_pass(b):
             acc = bank("back%d" % b, "a%d" % (b - 2))
             second_product(acc[:], b, slice(0, N))
-            if b == 2:
-                return stage("dx_back%d" % b, acc)
-            staged = tile("dx_back%d" % b, [P, N], F32)
-            nc.vector.tensor_copy(staged[:], acc[:])
-            return staged
+            return acc
 
         early = bank("front0")
         for b in range(2):
             second_product(early[:, half(b)], b, half(0))
         early0 = tile("dx_early0", [P, HALF], F32)
-        early1 = late_decay[:, PACK * HALF - GROUP :]
         nc.scalar.activation(early0[:], early[:, half(0)], ACT.Copy)
+        early1 = late_decay[:, PACK * HALF - GROUP :]
         nc.scalar.activation(early1[:, GROUP:], early[:, HALF + GROUP :], ACT.Copy)
         scalar_scatter(0, early0[:], half(0))
         gradient(1)
         quantize_wv(1)
         nc.vector.tensor_copy(early1[:, :GROUP], early[:, HALF : HALF + GROUP])
         quantize_g(1)
-        late = front_sums(1)
+        acc = bank("front1")
+        for b in range(2):
+            second_product(acc[:, half(b)], b, half(1))
+        late = {b: tile("dx_late%d" % b, [P, HALF], F32) for b in range(2)}
+        for b in (1, 0):
+            nc.scalar.activation(late[b][:], acc[:, half(b)], ACT.Copy)
+        back3 = tile("dx_back3", [P, N], F32)
+        halves = [bank("back3%d" % h, "a%d" % (1 + h)) for h in range(2)]
+        for h in range(2):
+            second_product(halves[h][:, half(0)], 3, half(h))
+        nc.scalar.activation(back3[:, half(0)], halves[0][:, half(0)], ACT.Copy)
         vector_scatter(1, early1, half(0))
-        back3 = back_sums(3)
-        vector_scatter(1, late[:, half(1)], half(1))
+        nc.vector.tensor_copy(back3[:, half(1)], halves[1][:, half(0)])
+        vector_scatter(1, late[1][:], half(1))
         store(1)
-        scalar_scatter(0, late[:, half(0)], half(1))
+        scalar_scatter(0, late[0][:], half(1))
         store(0)
         vector_scatter(3, back3[:], slice(0, N))
         store(3)
-        back2 = back_sums(2)
+        back2 = stage_halves("dx_back", back_pass(2))
         for h in range(2):
-            scalar_scatter(2, back2[:, half(h)], half(h))
+            scalar_scatter(2, back2[h][:], half(h))
         store(2)

@@ -66,7 +66,9 @@ def tile_attend_gml_wel_kernel(tc, xT, wd, wv, y, cw, rw, offs, out):
         wd_raw = tile("wd_raw", [P, PACK, V], F32)
         wv_raw = [tile("wv_raw%d" % h, [P, PACK, HALF], F32) for h in range(2)]
         wv_planes = wv.rearrange("(p t) d -> p t d", t=PACK)
-        y_sb = [tile("y_sb%d" % u, [P, PAIR, N], F32) for u in range(2)]
+        size = PACK * HALF
+        shared = tile("shared", [P, 2 * size + HALF - GROUP], F32)
+        y_sb = [tile("y_sb0", [P, PAIR, N], F32)[:], shared[:, HALF : HALF + size].rearrange("p (t n) -> p t n", t=PAIR)]
         y_planes = y.rearrange("(p t) n -> p t n", t=PACK)
         nc.sync.dma_start(rw_sb[:], rw[0:1, :].rearrange("o (m j) -> m (o j)", j=PACK))
         nc.sync.dma_start(x_raw[0][:], x_planes[:, 0, :])
@@ -77,7 +79,7 @@ def tile_attend_gml_wel_kernel(tc, xT, wd, wv, y, cw, rw, offs, out):
         nc.sync.dma_start(wd_raw[:], wd.rearrange("(p j) v -> p j v", j=PACK))
         nc.sync.dma_start(wv_raw[0][:], wv_planes[:, :, half(0)])
         for u in range(2):
-            nc.sync.dma_start(y_sb[u][:], y_planes[:, planes(u), :])
+            nc.sync.dma_start(y_sb[u], y_planes[:, planes(u), :])
         nc.sync.dma_start(wv_raw[1][:], wv_planes[:, :, half(1)])
 
         identity = tile("identity", [P, P], F32)
@@ -166,12 +168,15 @@ def tile_attend_gml_wel_kernel(tc, xT, wd, wv, y, cw, rw, offs, out):
                 q[h][:, planes(u)], acc[:].rearrange("p (t n) -> p t n", t=PAIR), y_sb[u][:, :, half(h)], ALU.subtract
             )
 
-        def exponentiate(h):
+        def exponentiate(h, parts):
             squared = [tile("sq%d%d" % (h, u), [P, PAIR, HALF], F32) for u in range(2)]
-            for u in range(2):
-                nc.scalar.activation(squared[u][:], q[h][:, planes(u)], ACT.Square)
-            for u in range(2):
-                nc.scalar.activation(decay[h][:, planes(u)], squared[u][:], ACT.Exp, scale=-0.5)
+            for part in parts:
+                for t in part:
+                    nc.scalar.activation(squared[t.start // PAIR][:, t.start % PAIR :][:, : t.stop - t.start], q[h][:, t], ACT.Square)
+                for t in part:
+                    nc.scalar.activation(
+                        decay[h][:, t], squared[t.start // PAIR][:, t.start % PAIR :][:, : t.stop - t.start], ACT.Exp, scale=-0.5
+                    )
 
         def gradient(h):
             nc.vector.tensor_tensor(as_words(g_words[h][:]), as_planes(weighted[h]), as_planes(decay[h]), ALU.mult)
@@ -210,14 +215,12 @@ def tile_attend_gml_wel_kernel(tc, xT, wd, wv, y, cw, rw, offs, out):
                 residual(h, u)
         for u in range(2):
             nc.gpsimd.tensor_tensor(weighted[0][:, planes(u)], q[0][:, planes(u)], early_weights[:, planes(u)], ALU.mult)
-        size = PACK * HALF
-        behind_residuals = tile("behind_residuals", [P, 3 * size + HALF - GROUP], F32, "y_sb1")
-        parts = [behind_residuals[:, k * size : (k + 1) * size].rearrange("p (t n) -> p t n", t=PACK) for k in range(3)]
-        late_decay = behind_residuals[:, 2 * size :]
-        decay = [parts[0], parts[2]]
-        weighted.append(parts[1])
-        for h in range(2):
-            exponentiate(h)
+        parts = [shared[:, k * size : (k + 1) * size].rearrange("p (t n) -> p t n", t=PACK) for k in range(2)]
+        late_decay = shared[:, size:]
+        decay = [tile("e0", [P, PACK, HALF], F32)[:], parts[1]]
+        weighted.append(parts[0])
+        exponentiate(0, [[planes(0)], [slice(2, 3), slice(3, 4)]])
+        exponentiate(1, [[planes(0), planes(1)]])
         wv_bf.append(tile("wv_bf1", [P, HALF * PACK], BF16, "sq10"))
         nc.scalar.activation(as_words(wv_bf[1][:]), as_planes(wv_raw[1][:]), ACT.Copy)
 

@@ -46,11 +46,14 @@ def tile_attend_gml_wel_kernel(tc, xT, wd, wv, y, cw, rw, offs, out):
         def planes(u):
             return slice(PAIR * u, PAIR * (u + 1))
 
+        def by_plane(columns, count):
+            return columns.rearrange("p (t n) -> p t n", t=count)
+
         def as_words(packed):
             return packed.rearrange("p (c i t) -> p c t i", i=RUN, t=PACK)
 
-        def as_planes(by_plane):
-            return by_plane.rearrange("p t (c i) -> p c t i", i=RUN)
+        def as_planes(values):
+            return values.rearrange("p t (c i) -> p c t i", i=RUN)
 
         def in_fours(columns):
             return columns.rearrange("p (m j) -> p m j", j=PACK)
@@ -66,9 +69,9 @@ def tile_attend_gml_wel_kernel(tc, xT, wd, wv, y, cw, rw, offs, out):
         wd_raw = tile("wd_raw", [P, PACK, V], F32)
         wv_raw = [tile("wv_raw%d" % h, [P, PACK, HALF], F32) for h in range(2)]
         wv_planes = wv.rearrange("(p t) d -> p t d", t=PACK)
-        size = PACK * HALF
-        shared = tile("shared", [P, 2 * size + HALF - GROUP], F32)
-        y_sb = [tile("y_sb0", [P, PAIR, N], F32)[:], shared[:, HALF : HALF + size].rearrange("p (t n) -> p t n", t=PAIR)]
+        late_size = PACK * HALF
+        late_values = tile("late_values", [P, 2 * late_size], F32)
+        y_sb = [tile("y_sb0", [P, PAIR, N], F32)[:], by_plane(late_values[:, HALF : HALF + late_size], PAIR)]
         y_planes = y.rearrange("(p t) n -> p t n", t=PACK)
         nc.sync.dma_start(rw_sb[:], rw[0:1, :].rearrange("o (m j) -> m (o j)", j=PACK))
         nc.sync.dma_start(x_raw[0][:], x_planes[:, 0, :])
@@ -95,7 +98,7 @@ def tile_attend_gml_wel_kernel(tc, xT, wd, wv, y, cw, rw, offs, out):
 
         windows = [tile("window%d" % b, [P, T], F32) for b in range(PACK)]
         for b, window in enumerate(windows):
-            (nc.vector if b < 2 else nc.gpsimd).memset(window[:], 0.0)
+            (nc.vector if b < PACK // 2 else nc.gpsimd).memset(window[:], 0.0)
 
         early_weights = tile("early_weights", [P, PACK, HALF], F32)
         early_rw = tile("early_rw", [P, HALF], F32)
@@ -141,10 +144,7 @@ def tile_attend_gml_wel_kernel(tc, xT, wd, wv, y, cw, rw, offs, out):
         quantize_x(1)
         quantize_wd(1)
 
-        def planes_tiles(name):
-            return [tile("%s%d" % (name, h), [P, PACK, HALF], F32) for h in range(2)]
-
-        weighted = [tile("wq0", [P, PACK, HALF], F32)[:]]
+        weighted = [tile("wq0", [P, PACK, HALF], F32)[:], by_plane(late_values[:, :late_size], PACK)]
         g_words = [tile("g%d" % h, [P, HALF * PACK], BF16) for h in range(2)]
         g_codes = tile("g_codes", [P, N], U32)
         g_scales = tile("g_scales", [P, N], U8)
@@ -164,19 +164,13 @@ def tile_attend_gml_wel_kernel(tc, xT, wd, wv, y, cw, rw, offs, out):
                     start=True,
                     stop=True,
                 )
-            nc.vector.tensor_tensor(
-                q[h][:, planes(u)], acc[:].rearrange("p (t n) -> p t n", t=PAIR), y_sb[u][:, :, half(h)], ALU.subtract
-            )
+            nc.vector.tensor_tensor(q[h][:, planes(u)], by_plane(acc[:], PAIR), y_sb[u][:, :, half(h)], ALU.subtract)
 
-        def exponentiate(h, parts):
-            squared = [tile("sq%d%d" % (h, u), [P, PAIR, HALF], F32) for u in range(2)]
-            for part in parts:
-                for t in part:
-                    nc.scalar.activation(squared[t.start // PAIR][:, t.start % PAIR :][:, : t.stop - t.start], q[h][:, t], ACT.Square)
-                for t in part:
-                    nc.scalar.activation(
-                        decay[h][:, t], squared[t.start // PAIR][:, t.start % PAIR :][:, : t.stop - t.start], ACT.Exp, scale=-0.5
-                    )
+        def exponentiate(h, steps):
+            for part, squares in steps:
+                nc.scalar.activation(squares, q[h][:, part], ACT.Square)
+            for part, squares in steps:
+                nc.scalar.activation(decay[h][:, part], squares, ACT.Exp, scale=-0.5)
 
         def gradient(h):
             nc.vector.tensor_tensor(as_words(g_words[h][:]), as_planes(weighted[h]), as_planes(decay[h]), ALU.mult)
@@ -207,7 +201,10 @@ def tile_attend_gml_wel_kernel(tc, xT, wd, wv, y, cw, rw, offs, out):
         def store(b):
             nc.sync.dma_start(out[block(b), :], windows[b][:])
 
-        q = planes_tiles("q")
+        def stage(staged, sums):
+            nc.scalar.activation(staged, sums, ACT.Copy)
+
+        q = [tile("q%d" % h, [P, PACK, HALF], F32) for h in range(2)]
         wv_bf.append(tile("wv_bf0", [P, HALF * PACK], BF16))
         nc.scalar.activation(as_words(wv_bf[0][:]), as_planes(wv_raw[0][:]), ACT.Copy)
         for u in range(2):
@@ -215,16 +212,16 @@ def tile_attend_gml_wel_kernel(tc, xT, wd, wv, y, cw, rw, offs, out):
                 residual(h, u)
         for u in range(2):
             nc.gpsimd.tensor_tensor(weighted[0][:, planes(u)], q[0][:, planes(u)], early_weights[:, planes(u)], ALU.mult)
-        parts = [shared[:, k * size : (k + 1) * size].rearrange("p (t n) -> p t n", t=PACK) for k in range(2)]
-        late_decay = shared[:, size:]
-        decay = [tile("e0", [P, PACK, HALF], F32)[:], parts[1]]
-        weighted.append(parts[0])
-        exponentiate(0, [[planes(0)], [slice(2, 3), slice(3, 4)]])
-        exponentiate(1, [[planes(0), planes(1)]])
+        decay = [tile("e0", [P, PACK, HALF], F32)[:], by_plane(late_values[:, late_size:], PACK)]
+        squared = [tile("sq0%d" % u, [P, PAIR, HALF], F32) for u in range(2)]
+        exponentiate(0, [(planes(0), squared[0][:])])
+        exponentiate(0, [(slice(PAIR + t, PAIR + t + 1), squared[1][:, t : t + 1]) for t in range(PAIR)])
+        squared = [tile("sq1%d" % u, [P, PAIR, HALF], F32) for u in range(2)]
+        exponentiate(1, [(planes(u), squared[u][:]) for u in range(2)])
         wv_bf.append(tile("wv_bf1", [P, HALF * PACK], BF16, "sq10"))
         nc.scalar.activation(as_words(wv_bf[1][:]), as_planes(wv_raw[1][:]), ACT.Copy)
 
-        def weigh_late(t):
+        for t in range(PACK):
             nc.vector.scalar_tensor_tensor(
                 in_fours(weighted[1][:, t]),
                 in_fours(q[1][:, t]),
@@ -233,56 +230,47 @@ def tile_attend_gml_wel_kernel(tc, xT, wd, wv, y, cw, rw, offs, out):
                 ALU.mult,
                 ALU.mult,
             )
-
-        for t in range(PACK):
-            weigh_late(t)
         gradient(0)
         quantize_wv(0)
         quantize_g(0)
 
-        def stage_halves(name, acc):
-            staged = [tile("%s%d" % (name, h), [P, HALF], F32) for h in range(2)]
-            for h in range(2):
-                nc.scalar.activation(staged[h][:], acc[:, half(h)], ACT.Copy)
-            return staged
-
-        def back_pass(b):
-            acc = bank("back%d" % b, "a%d" % (b - 2))
-            second_product(acc[:], b, slice(0, N))
-            return acc
-
-        early = bank("front0")
+        early_sums = [bank("early%d" % b) for b in range(2)]
         for b in range(2):
-            second_product(early[:, half(b)], b, half(0))
-        early0 = tile("dx_early0", [P, HALF], F32)
-        nc.scalar.activation(early0[:], early[:, half(0)], ACT.Copy)
-        early1 = late_decay[:, PACK * HALF - GROUP :]
-        nc.scalar.activation(early1[:, GROUP:], early[:, HALF + GROUP :], ACT.Copy)
-        scalar_scatter(0, early0[:], half(0))
+            second_product(early_sums[b][:, half(0)], b, half(0))
+        early = [tile("dx_early%d" % b, [P, HALF], F32) for b in range(2)]
+        for b in range(2):
+            stage(early[b][:], early_sums[b][:, half(0)])
+        scalar_scatter(0, early[0][:], half(0))
         gradient(1)
         quantize_wv(1)
-        nc.vector.tensor_copy(early1[:, :GROUP], early[:, HALF : HALF + GROUP])
         quantize_g(1)
-        acc = bank("front1")
+
+        late_sums = bank("late_sums")
         for b in range(2):
-            second_product(acc[:, half(b)], b, half(1))
-        late = {b: tile("dx_late%d" % b, [P, HALF], F32) for b in range(2)}
+            second_product(late_sums[:, half(b)], b, half(1))
+        late = [tile("dx_late%d" % b, [P, HALF], F32) for b in range(2)]
         for b in (1, 0):
-            nc.scalar.activation(late[b][:], acc[:, half(b)], ACT.Copy)
-        back3 = tile("dx_back3", [P, N], F32)
-        halves = [bank("back3%d" % h, "a%d" % (1 + h)) for h in range(2)]
+            stage(late[b][:], late_sums[:, half(b)])
+
+        last = tile("dx_window3", [P, N], F32)
+        last_sums = [bank("window3_sums%d" % h, "a%d" % (1 + h)) for h in range(2)]
         for h in range(2):
-            second_product(halves[h][:, half(0)], 3, half(h))
-        nc.scalar.activation(back3[:, half(0)], halves[0][:, half(0)], ACT.Copy)
-        vector_scatter(1, early1, half(0))
-        nc.vector.tensor_copy(back3[:, half(1)], halves[1][:, half(0)])
+            second_product(last_sums[h][:, half(0)], 3, half(h))
+        stage(last[:, half(0)], last_sums[0][:, half(0)])
+        vector_scatter(1, early[1][:], half(0))
+        nc.vector.tensor_copy(last[:, half(1)], last_sums[1][:, half(0)])
         vector_scatter(1, late[1][:], half(1))
         store(1)
         scalar_scatter(0, late[0][:], half(1))
         store(0)
-        vector_scatter(3, back3[:], slice(0, N))
+        vector_scatter(3, last[:], slice(0, N))
         store(3)
-        back2 = stage_halves("dx_back", back_pass(2))
+
+        third_sums = bank("window2_sums", "a0")
+        second_product(third_sums[:], 2, slice(0, N))
+        third = [tile("dx_window2_%d" % h, [P, HALF], F32) for h in range(2)]
         for h in range(2):
-            scalar_scatter(2, back2[h][:], half(h))
+            stage(third[h][:], third_sums[:, half(h)])
+        for h in range(2):
+            scalar_scatter(2, third[h][:], half(h))
         store(2)

from contextlib import ExitStack

import concourse.mybir as mybir
from concourse.masks import make_identity

N, T, D, V = 512, 1024, 512, 512
FLOPS = 2 * D * V * N + 2 * V * D * N

F32 = mybir.dt.float32
BF16 = mybir.dt.bfloat16
U32 = mybir.dt.uint32
U16 = mybir.dt.uint16
U8 = mybir.dt.uint8
E4M3 = mybir.dt.float8_e4m3fn_x4
E5M2 = mybir.dt.float8_e5m2_x4
ACT = mybir.ActivationFunctionType
ALU = mybir.AluOpType

P = 128
PACK = 4
PAIR = 2
HALF = 256
GROUP = 16
RUN = 4
SCALAR_COLUMNS = 40


def tile_attend_gml_wel_kernel(tc, xT, wd, wv, y, cw, rw, offs, out):
    nc = tc.nc
    with ExitStack() as ctx:
        sb = ctx.enter_context(tc.tile_pool(name="sb", bufs=1))
        ps = ctx.enter_context(tc.psum_pool(name="ps", bufs=1))

        def tile(name, shape, dtype, takes_over=None):
            return sb.tile(shape, dtype, name=name, tag=takes_over or name, align_bytes=64)

        def bank(name, takes_over=None):
            return ps.tile([P, N], F32, name=name, tag=takes_over or name)

        def half(h):
            return slice(h * HALF, (h + 1) * HALF)

        def block(b):
            return slice(b * P, (b + 1) * P)

        def planes(u):
            return slice(PAIR * u, PAIR * (u + 1))

        def by_plane(columns, count):
            return columns.rearrange("p (t n) -> p t n", t=count)

        def as_words(packed):
            return packed.rearrange("p (c i t) -> p c t i", i=RUN, t=PACK)

        def as_planes(values):
            return values.rearrange("p t (c i) -> p c t i", i=RUN)

        def in_fours(columns):
            return columns.rearrange("p (m j) -> p m j", j=PACK)

        def listed(entries):
            return offsets[:, entries.start // GROUP : entries.stop // GROUP]

        offsets = sb.tile([P, N // GROUP], U16, name="offsets")
        cw_sb = tile("cw_sb", [P, PACK], F32)
        rw_sb = tile("rw_sb", [P, PACK], F32)
        x_planes = xT.rearrange("(p t) n -> p t n", t=PACK)
        x_raw = [tile("x_raw%d" % t, [P, T], F32) for t in range(PACK)]
        wd_raw = tile("wd_raw", [P, PACK, V], F32)
        wv_raw = [tile("wv_raw%d" % h, [P, PACK, HALF], F32) for h in range(2)]
        wv_planes = wv.rearrange("(p t) d -> p t d", t=PACK)
        late_size = PACK * HALF
        late_values = tile("late_values", [P, 2 * late_size], F32)
        y_sb = [tile("y_sb0", [P, PAIR, N], F32)[:], by_plane(late_values[:, HALF : HALF + late_size], PAIR)]
        y_planes = y.rearrange("(p t) n -> p t n", t=PACK)
        nc.sync.dma_start(rw_sb[:], rw[0:1, :].rearrange("o (m j) -> m (o j)", j=PACK))
        nc.sync.dma_start(x_raw[0][:], x_planes[:, 0, :])
        nc.sync.dma_start(offsets[:], offs)
        nc.sync.dma_start(cw_sb[:], cw.rearrange("(p t) o -> p (t o)", t=PACK))
        for t in range(1, PACK):
            nc.sync.dma_start(x_raw[t][:], x_planes[:, t, :])
        nc.sync.dma_start(wd_raw[:], wd.rearrange("(p j) v -> p j v", j=PACK))
        nc.sync.dma_start(wv_raw[0][:], wv_planes[:, :, half(0)])
        for u in range(2):
            nc.sync.dma_start(y_sb[u], y_planes[:, planes(u), :])
        nc.sync.dma_start(wv_raw[1][:], wv_planes[:, :, half(1)])

        identity = tile("identity", [P, P], F32)
        make_identity(nc, identity[:])
        rw_bank = bank("rw_bank")
        rw_wide = tile("rw_wide", [P, PACK, P], F32)
        nc.scalar.activation(rw_wide[:], rw_sb[:].unsqueeze(2).to_broadcast([P, PACK, P]), ACT.Copy)
        for j in range(PACK):
            nc.tensor.transpose(rw_bank[:, block(j)], rw_wide[:, j], identity[:])

        def rw_entries(entries):
            return rw_bank[:].rearrange("p (j m) -> p m j", j=PACK)[:, entries.start // PACK : entries.stop // PACK, :]

        windows = [tile("window%d" % b, [P, T], F32) for b in range(PACK)]
        for b, window in enumerate(windows):
            (nc.vector if b < PACK // 2 else nc.gpsimd).memset(window[:], 0.0)

        early_weights = tile("early_weights", [P, PACK, HALF], F32)
        early_rw = tile("early_rw", [P, HALF], F32)
        nc.scalar.activation(in_fours(early_rw[:]), rw_entries(half(0)), ACT.Copy)
        for t in range(PACK):
            nc.gpsimd.tensor_scalar(early_weights[:, t], early_rw[:], cw_sb[:, t : t + 1], 0.0, ALU.mult, ALU.add)

        x_bf = [tile("x_bf%d" % h, [P, HALF * PACK], BF16) for h in range(2)]
        gathered = tile("gathered", [P, PACK, HALF], BF16)
        for t in range(PACK):
            nc.vector.tensor_copy(
                x_bf[0][:].rearrange("p (i t) -> p t i", t=PACK)[:, t], x_raw[t][:].indirect(listed(half(0)))
            )
            nc.scalar.activation(gathered[:, t], x_raw[t][:].indirect(listed(half(1))), ACT.Copy)
        nc.vector.tensor_copy(as_words(x_bf[1][:]), as_planes(gathered[:]))

        x_scales = tile("x_scales", [P, N], U8)
        x_codes = tile("x_codes", [P, N], U32)

        def quantize_x(h):
            nc.vector.quantize_mx(x_codes[:, half(h)].bitcast(E4M3), x_scales[:, half(h)], x_bf[h][:])

        wd_bf = [tile("wd_bf%d" % u, [P, PAIR, P, PACK], BF16) for u in range(2)]
        wd_codes = tile("wd_codes", [P, V], U32)
        wd_scales = tile("wd_scales", [P, V], U8)

        def deal(u, columns):
            return (
                wd_bf[u][:].rearrange("p t m j -> p m j t")[:, columns],
                wd_raw[:].rearrange("p j (m t) -> p m j t", t=PACK)[:, columns, :, planes(u)],
            )

        def quantize_wd(u):
            nc.vector.quantize_mx(
                wd_codes[:, half(u)].bitcast(E4M3), wd_scales[:, half(u)], wd_bf[u][:].rearrange("p t m j -> p (t m j)")
            )

        quantize_x(0)
        nc.scalar.activation(*deal(0, slice(0, SCALAR_COLUMNS)), ACT.Copy)
        nc.vector.tensor_copy(*deal(0, slice(SCALAR_COLUMNS, P)))
        nc.scalar.activation(*deal(1, slice(0, P)), ACT.Copy)
        quantize_wd(0)
        quantize_x(1)
        quantize_wd(1)

        weighted = [tile("wq0", [P, PACK, HALF], F32)[:], by_plane(late_values[:, :late_size], PACK)]
        g_words = [tile("g%d" % h, [P, HALF * PACK], BF16) for h in range(2)]
        g_codes = tile("g_codes", [P, N], U32)
        g_scales = tile("g_scales", [P, N], U8)
        wv_bf = []
        wv_scales = tile("wv_scales", [P, D], U8)
        wv_codes = tile("wv_codes", [P, D], U32, "early_weights")

        def residual(h, u):
            acc = bank("a%d" % (2 * h + u))
            for t in range(PAIR):
                nc.tensor.matmul_mx(
                    acc[:, half(t)],
                    lhsT=wd_codes[:, block(PAIR * u + t)].bitcast(E4M3),
                    lhsT_scale=wd_scales[:, block(PAIR * u + t)],
                    rhs=x_codes[:, half(h)].bitcast(E4M3),
                    rhs_scale=x_scales[:, half(h)],
                    start=True,
                    stop=True,
                )
            nc.vector.tensor_tensor(q[h][:, planes(u)], by_plane(acc[:], PAIR), y_sb[u][:, :, half(h)], ALU.subtract)

        def exponentiate(h, steps):
            for part, squares in steps:
                nc.scalar.activation(squares, q[h][:, part], ACT.Square)
            for part, squares in steps:
                nc.scalar.activation(decay[h][:, part], squares, ACT.Exp, scale=-0.5)

        def gradient(h):
            nc.vector.tensor_tensor(as_words(g_words[h][:]), as_planes(weighted[h]), as_planes(decay[h]), ALU.mult)

        def quantize_g(h):
            nc.vector.quantize_mx(g_codes[:, half(h)].bitcast(E5M2), g_scales[:, half(h)], g_words[h][:])

        def quantize_wv(h):
            nc.vector.quantize_mx(wv_codes[:, half(h)].bitcast(E4M3), wv_scales[:, half(h)], wv_bf[h][:])

        def second_product(acc, b, entries):
            nc.tensor.matmul_mx(
                acc,
                lhsT=wv_codes[:, block(b)].bitcast(E4M3),
                lhsT_scale=wv_scales[:, block(b)],
                rhs=g_codes[:, entries].bitcast(E5M2),
                rhs_scale=g_scales[:, entries],
                start=True,
                stop=True,
            )

        def vector_scatter(b, staged, entries):
            nc.vector.tensor_copy(windows[b][:].indirect(listed(entries)), staged)

        def scalar_scatter(b, staged, entries):
            nc.scalar.activation(windows[b][:].indirect(listed(entries)), staged, ACT.Copy)

        def store(b):
            nc.sync.dma_start(out[block(b), :], windows[b][:])

        def stage(staged, sums):
            nc.scalar.activation(staged, sums, ACT.Copy)

        q = [tile("q%d" % h, [P, PACK, HALF], F32) for h in range(2)]
        wv_bf.append(tile("wv_bf0", [P, HALF * PACK], BF16))
        nc.scalar.activation(as_words(wv_bf[0][:]), as_planes(wv_raw[0][:]), ACT.Copy)
        for u in range(2):
            for h in range(2):
                residual(h, u)
        for u in range(2):
            nc.gpsimd.tensor_tensor(weighted[0][:, planes(u)], q[0][:, planes(u)], early_weights[:, planes(u)], ALU.mult)
        decay = [tile("e0", [P, PACK, HALF], F32)[:], by_plane(late_values[:, late_size:], PACK)]
        squared = [tile("sq0%d" % u, [P, PAIR, HALF], F32) for u in range(2)]
        exponentiate(0, [(planes(0), squared[0][:])])
        exponentiate(0, [(slice(PAIR + t, PAIR + t + 1), squared[1][:, t : t + 1]) for t in range(PAIR)])
        squared = [tile("sq1%d" % u, [P, PAIR, HALF], F32) for u in range(2)]
        exponentiate(1, [(planes(u), squared[u][:]) for u in range(2)])
        wv_bf.append(tile("wv_bf1", [P, HALF * PACK], BF16, "sq10"))
        nc.scalar.activation(as_words(wv_bf[1][:]), as_planes(wv_raw[1][:]), ACT.Copy)

        for t in range(PACK):
            nc.vector.scalar_tensor_tensor(
                in_fours(weighted[1][:, t]),
                in_fours(q[1][:, t]),
                cw_sb[:, t : t + 1],
                rw_entries(half(1)),
                ALU.mult,
                ALU.mult,
            )
        gradient(0)
        quantize_wv(0)
        quantize_g(0)

        early_sums = [bank("early%d" % b) for b in range(2)]
        for b in range(2):
            second_product(early_sums[b][:, half(0)], b, half(0))
        early = [tile("dx_early%d" % b, [P, HALF], F32) for b in range(2)]
        for b in range(2):
            stage(early[b][:], early_sums[b][:, half(0)])
        scalar_scatter(0, early[0][:], half(0))
        gradient(1)
        quantize_wv(1)
        quantize_g(1)

        late_sums = bank("late_sums")
        for b in range(2):
            second_product(late_sums[:, half(b)], b, half(1))
        late = [tile("dx_late%d" % b, [P, HALF], F32) for b in range(2)]
        for b in (1, 0):
            stage(late[b][:], late_sums[:, half(b)])

        last = tile("dx_window3", [P, N], F32)
        last_sums = [bank("window3_sums%d" % h, "a%d" % (1 + h)) for h in range(2)]
        for h in range(2):
            second_product(last_sums[h][:, half(0)], 3, half(h))
        stage(last[:, half(0)], last_sums[0][:, half(0)])
        vector_scatter(1, early[1][:], half(0))
        nc.vector.tensor_copy(last[:, half(1)], last_sums[1][:, half(0)])
        vector_scatter(1, late[1][:], half(1))
        store(1)
        scalar_scatter(0, late[0][:], half(1))
        store(0)
        vector_scatter(3, last[:], slice(0, N))
        store(3)

        third_sums = bank("window2_sums", "a0")
        second_product(third_sums[:], 2, slice(0, N))
        third = [tile("dx_window2_%d" % h, [P, HALF], F32) for h in range(2)]
        for h in range(2):
            stage(third[h][:], third_sums[:, half(h)])
        for h in range(2):
            scalar_scatter(2, third[h][:], half(h))
        store(2)
